import numpy as np, ml_dtypes
CORES = [25,29,65,69,153,157,193,197]
N = 8
import mx_ref
BF = ml_dtypes.bfloat16
def tile(rs):
    return np.stack(rs, axis=2).reshape(128, -1).astype(BF)
def pick(q, e):
    c = np.concatenate([q[0].reshape(128, -1, 4), np.zeros((128, 1, 4), np.uint8)], axis=1); s = np.concatenate([q[1], np.ones((16, 1), np.uint8)], axis=1)
    return (np.ascontiguousarray(c[:, e].reshape(128, -1)), np.ascontiguousarray(s[:, e]))
def join(*qs):
    return (np.concatenate([q[0] for q in qs], axis=1), np.concatenate([q[1] for q in qs], axis=1))
def put(q, e, v):
    c, s = q[0].reshape(128, -1, 4).copy(), q[1].copy(); c[:, e] = v[0].reshape(128, -1, 4); s[:, e] = v[1]
    return (c.reshape(128, -1), s)
def pk(c, s):
    return (np.ascontiguousarray(c), mx_ref.live(s))
def emit(q):
    return q[0], q[1]
def packed(v, rng):
    q = [mx_ref.quantize(np.ascontiguousarray(v[r])) for r in range(N)]
    return np.stack([a for a, b in q]), np.stack([mx_ref.plane(b, rng) for a, b in q])
def values_of_codes():
    e, c = np.zeros((128, 128, 4), np.float32), np.zeros((128, 2, 4), np.uint8)
    e[np.arange(128), np.arange(128), 0] = 1
    c[:127, :, 0] = np.arange(256).reshape(2, 128).T[:127]
    return mx_ref.matmul(mx_ref.quantize(e.reshape(128, 512).astype(BF)), (c.reshape(128, 8), np.full((16, 2), 127, np.uint8))).T.reshape(-1).astype(np.float64)
CODE_VALUE, SCALE_VALUE = values_of_codes(), 2.0 ** (np.arange(256) - 127.0)
def decode(q):
    return (CODE_VALUE[q[0]].reshape(16, 8, -1, 4) * SCALE_VALUE[q[1]][:, None, :, None] + 0.0).reshape(128, -1).astype(np.float32)
def f(rng, *shape):
    return mx_ref.flush((rng.standard_normal(shape, dtype=np.float32) * np.exp2(rng.integers(-2, 3, shape[:-1] + (1,)))).astype(BF))
def wide(rng, *shape, cols=0):
    v = rng.standard_normal(shape, dtype=np.float32) * np.exp2(rng.integers(-12, 13, shape)).astype(np.float32)
    if cols: v *= np.repeat(np.exp2(rng.integers(-cols, cols + 1, shape[:-2] + (1, shape[-1] // 4))) * (rng.random(shape[:-2] + (1, shape[-1] // 4)) > 0.0625), 4, axis=-1).astype(np.float32)
    return mx_ref.flush(v.astype(BF))
C, H, E = 288, 96, 384
STEP = [1, 2, 4]
def parts(t, h, n):
    return np.ascontiguousarray(t.reshape(8, 16, -1, 4)[h, :, n].transpose(0, 2, 1, 3)).reshape(128, -1)
def big(v):
    v = v.astype(np.float32)
    v[np.abs(v) < np.float32(2.0 ** -16)] = 0
    return v.astype(BF)
def numbers_of(rng):
    return {"x": big(f(rng, N, 128, 4 * C)), "u": np.array(f(rng, N, 128, 512)), "v": np.array(f(rng, N, 128, 512))}
def edges(rng):
    return {"nb": rng.integers(0, E, (N, 4, C)).astype(np.int32), "e": rng.integers(0, 8, (N, 4, C)).astype(np.int32)}
def layers(rng):
    return big(f(rng, N, 128, 2048)).reshape(N, 8, 16, 4, 8, 16, 4)
def weights(rng, w):
    c, p = packed(np.ascontiguousarray(w).reshape(N, 128, 2048), rng)
    return {"wc": c, "ws": p}
def bare(u):
    u = u.reshape(N, 128, 128, 4)
    u[:, :, ::16] = 0
    u[:, :, 1::16] = 0
    u[:, :, 2] = 0
    return u
def setup_inputs(rng):
    return {**numbers_of(rng), **edges(rng), **weights(rng, layers(rng))}
def setup_inputs_ties(rng):
    d = numbers_of(rng)
    x = d["x"].reshape(N, 8, 16, C, 4)
    x[:, :, :3] = 0
    x[:, :, :3, :, 0] = rng.integers(1, 4, (N, 8, 3, C)).astype(np.float32).astype(BF)
    u = bare(d["u"])
    o = rng.permutation(N)
    for r in range(N):
        k = 0.0 if r == o[0] else -1.0 if r == o[1] else 1.0
        u[r, 2, 2, 0] = k
        for h in range(0, 128, 16):
            u[r, h, h, 0] = k
            u[r, h + 1, h + 1, 0] = k
    w = layers(rng)
    w[:, :, :, :, :, :3] = 0
    return {"x": x.reshape(N, 128, 4 * C), "u": u.reshape(N, 128, 512), "v": d["v"], **edges(rng), **weights(rng, w)}
def setup_inputs_near(rng):
    d = numbers_of(rng)
    x = d["x"].astype(np.float32).reshape(N, 8, 16, C, 4)
    u = bare(d["u"])
    o = rng.permutation(N) % 4
    x[:, :, 0] = 0
    x[:, :, 8:] = 0
    s = rng.integers(0, 16, (N, 8, 3, C))
    x[:, :, 8:11] = ((s[..., None] >> np.arange(4)) & 1) * np.exp2(np.arange(4) - 23.0)
    x[:, :, 11, :, 0] = 2.0 ** -10
    for r in range(N):
        x[r, :, 0, :, 0] = -1.0 if o[r] == 1 else 1.0
        if o[r] == 3:
            x[r, :, 8:] = 0
            x[r, :, 8:11, :, 0] = rng.choice([0.0, 1.0, 1.125], (8, 3, C)) * 2.0 ** -29
            x[r, :, 12, :, 0] = 2.0 ** -29
            for g in np.append(0, 1 + rng.permutation(7)[:3]): x[r, int(g), 8:11, int(rng.integers(C)), 0] = 2.0 ** 29
        k = 1.0 if o[r] == 0 else 2.0 ** -30
        for h, i, j in [(h, 8 + i, h + i) for h in range(0, 128, 16) for i in (0, 1)] + [(0, 10, 2)]:
            u[r, h + i, j] = k if o[r] < 3 or j == 2 else k * 1.25 if h < 64 else k * 1.125
            if o[r] < 2:
                u[r, h, j, 0] = k
                u[r, h + 11, j, 0] = k
        if o[r] == 2:
            a, b = [16 * int(h) for h in rng.permutation(8)[:2]]
            u[r, a, a, 0] = 1.0
            u[r, b, b, 0] = -1.0
            u[r, b, b + 1, 0] = -1.0
            m, n = [int(h) for h in rng.permutation(C)[:2]]
            x[r, :, 0, m, 1] = 1.0
            x[r, :, 0, n, 1] = -1.0
            u[r, 0, 2, 1] = 1.0
        if o[r] == 3: u[r, 12, 2, 0] = -k
    w = layers(rng)
    for i in [0] + [8 + k for k in range(8)]:
        w[:, :, i] = 0
        w[:, :, :, :, :, i] = 0
    return {"x": x.reshape(N, 128, 4 * C).astype(BF), "u": u.reshape(N, 128, 512), "v": d["v"], **edges(rng), **weights(rng, w)}
def setup_inputs_huge(rng):
    d = numbers_of(rng)
    o = rng.permutation(N)
    c = rng.integers(0, 2, (N, C)) * 2.0 - 1.0
    a = 2.0 ** 29 * (1.0 - 0.1 * rng.random((N, 8, 16, 17, 4)))
    for g in range(8):
        a[:, g, :, g] *= 2.0
        a[:, g, :, 8 + g] *= 2.0
    for r in range(N):
        if o[r] < 2: c[r] = -1.0
        if o[r] == 0:
            c[r, rng.permutation(C)[:H // 2]] = 1.0
            a[r] = 2.0 ** 30
            for g in range(8):
                a[r, 0, :7 - g, g] *= 0.5
                a[r, 0, :7 - g, 8 + g] *= 0.5
        if o[r] >= N // 2: a[r, :, :, 8:16] *= (rng.permutation(8) % 2 * 2.0 - 1.0)[:, None]
    x = (0.6 + 0.09 * rng.random((N, 8, 16, C, 4))) * c[:, None, None, :, None]
    x[o == 0] = 0.875 * np.sign(x[o == 0])
    u = bare(d["u"])
    u[:, :, [16 * h for h in range(8)] + [16 * h + 1 for h in range(8)] + [2]] = a.reshape(N, 128, 17, 4).astype(np.float32).astype(BF)
    w = np.zeros((N, 128, 4, 128, 4), np.float32)
    i = np.arange(128)
    for b in range(4): w[:, i, b, i, b] = 1
    return {"x": (2.0 ** 30 * x).astype(np.float32).reshape(N, 128, 4 * C).astype(BF), "u": u.reshape(N, 128, 512), "v": d["v"], **edges(rng), **weights(rng, w.astype(BF))}
def setup_inputs_few(rng):
    d = numbers_of(rng)
    x = (129 + 2 * rng.integers(0, 64, (N, 8, 16, C, 4))) * np.exp2(rng.integers(-14, -7, (N, 8, 16, C, 4)) - 7.0) * (rng.integers(0, 2, (N, 8, 16, C, 4)) * 2.0 - 1.0)
    x[:, :, ::8, :, 0] = 1.96875
    u = d["u"].reshape(N, 8, 16, 128, 4)
    u[:, :, ::8] = 0
    t = edges(rng)
    o = rng.permutation(N)
    t["nb"][o[0]] = E - 1
    t["nb"][o[1]] = np.arange(C)
    t["e"][o[1]] = 7
    t["nb"][o[2]] = C + rng.integers(0, H, (4, C))
    t["nb"][o[3]] = 0
    t["e"][o[3]] = 0
    w = layers(rng)
    w[:, :, :, :, :, 8:] = 0
    return {"x": (16.0 * x).astype(np.float32).reshape(N, 128, 4 * C).astype(BF), "u": u.reshape(N, 128, 512), "v": d["v"], **t, **weights(rng, w)}
def setup_inputs_spread(rng):
    d = setup_inputs(rng)
    d["x"] = big(wide(rng, N, 128, 4 * C, cols=6))
    return d
def check_inputs(d):
    b = []
    for k in ("x", "u", "v"):
        a = np.abs(d[k].astype(np.float32))
        if not (np.isfinite(a).all() and ((a == 0) | (a >= 2.0 ** -30) & (a <= 2.0 ** 30)).all()): b.append("a value of " + k)
    if not ((d["nb"] >= 0) & (d["nb"] < E)).all(): b.append("an entry of nb")
    if not ((d["e"] >= 0) & (d["e"] < 8)).all(): b.append("an entry of e")
    none, least, most = [emit(mx_ref.quantize(np.full((128, 16), k, np.float32).astype(BF)))[1][0, 0] for k in (0.0, 2.0 ** -30, 2.0 ** 30)]
    for r in range(N):
        if ((d["wc"][r] == 0x7F) | (d["wc"][r] == 0xFF)).any(): b.append("wc: a code that is no number")
        s = mx_ref.live(d["ws"][r])
        if ((s != none) & ((s < least) | (s > most))).any(): b.append("ws: a scale out of range")
    return b
def reference(x, u, v, nb, e, wc, ws):
    qu = [mx_ref.quantize(u[r]) for r in range(N)]
    lay = [pk(wc[r], ws[r]) for r in range(N)]
    now = [x[r] for r in range(N)]
    shift = e.astype(np.int64)
    g, i = np.arange(8), np.arange(C)
    for d in STEP:
        q = [mx_ref.quantize(now[r]) for r in range(N)]
        own = [mx_ref.matmul(qu[r], q[r]) + np.float32(0.0) for r in range(N)]
        border = [pick(q[r], np.argsort(-own[r][2], kind="stable")[:H]) for r in range(N)]
        made = []
        for r in range(N):
            came = border[(r + d) % N]
            p = np.concatenate([own[r], mx_ref.matmul(qu[r], came) + np.float32(0.0)], axis=1)
            val = decode(join(q[r], came))
            k = np.argmax(p[1::16], axis=0)
            shift[r] = (shift[r] + k[nb[r]] - k[:C]) % 8
            src = (g[:, None, None] + shift[r]) % 8
            c = np.argmax(p[::16][src, nb[r]], axis=1)
            a = parts(val, (g[:, None] + k[:C]) % 8, i)
            b = parts(val, np.take_along_axis(src, c[:, None], axis=1)[:, 0], nb[r][c, i])
            z = mx_ref.quantize(((a + b) * np.float32(0.5)).astype(BF))
            made.append(tile([np.maximum(mx_ref.matmul(pick(lay[r], np.arange(128 * t, 128 * t + 128)), z), np.float32(0.0)) * np.float32(0.03125) + a[:, t::4] for t in range(4)]))
        now = made
    y, oe = np.zeros((N, 128, C), np.float32), np.zeros((N, 4, C), np.float32)
    oc, osc = np.zeros((N, 128, 4 * C), np.uint8), np.zeros((N, 16, C), np.uint8)
    for r in range(N):
        q = mx_ref.quantize(now[r])
        y[r] = mx_ref.matmul(mx_ref.quantize(v[r]), q)
        oe[r] = shift[r]
        oc[r], osc[r] = emit(q)
    return {"y": y, "oe": oe, "oc": oc, "osc": osc}

@@ -1,0 +1,721 @@
+from concourse.bass import DstId, RemoteDMATransfer
+from concourse.mybir import dt, AluOpType, ActivationFunctionType
+
+C, H, E = 288, 96, 384
+STEP = [1, 2, 4]
+BIG = 1.0e29
+TURN, OWN, FAR = 4 * C, 32 * C, 4 * H
+MADE = 4
+TRIES = 9000
+CYC, PEC, FIX, HOP, DMA_T, WIRE_X, WIRE_L = 1.0, 0.6, 60.0, 120.0, 2200.0, 7000.0, 4500.0
+F32, BF, I32, U16, X4, U8 = "float32", "bfloat16", "int32", "uint16", "float8_e4m3fn_x4", "uint8"
+
+SCRATCH = {"ps": ("psum", [128, 4096], F32)}
+for _n, _c, _d in [
+    ("xin", 1152, BF), ("uin", 512, BF), ("vin", 512, BF), ("xt", 1152, BF), ("zt", 1152, BF),
+    ("wq", 512, X4), ("wsc", 512, U8), ("uq", 128, X4), ("us", 128, U8), ("vq", 128, X4), ("vs", 128, U8),
+    ("upq", 560, X4), ("ups", 560, U8), ("eq", 960, X4), ("es", 960, U8), ("cq", 768, X4), ("cs", 768, U8),
+    ("fq", 288, X4), ("fs", 288, U8), ("gq", 128, X4), ("gs", 128, U8), ("jq", 128, X4), ("js", 128, U8),
+    ("hq", 150, X4), ("hs", 150, U8), ("zq", 288, X4), ("zs", 288, U8),
+    ("ones", 520, BF), ("ebig", 1024, BF), ("sel", 1552, BF), ("tri", 288, BF), ("zb", 520, BF),
+    ("rw", 288, BF), ("rf", 64, BF), ("rc", 144, BF), ("iot", 288, F32), ("ci", 96, I32), ("cf", 128, F32), ("pb", 16, F32),
+    ("lu", 36, U16), ("l12", 18, U16), ("l3", 10, U16), ("lown", 10, U16), ("lnb", 10, U16),
+    ("m0", 256, I32), ("m1", 128, F32), ("vv", 160, F32), ("vg", 288, F32), ("vt", 288, F32), ("vi", 160, I32),
+    ("si", 48, I32), ("sf", 192, F32), ("sa", 144, I32), ("nbm", 144, F32), ("mul", 144, F32),
+    ("pc", 4, F32), ("th", 288, F32), ("ft", 1152, BF), ("w1", 288, F32), ("o1", 18, U16), ("lst", 288, F32), ("w2", 128, F32),
+    ("pm", 384, F32), ("ff", 512, BF), ("fg", 512, BF), ("fl", 384, BF), ("flx", 288, BF), ("fa", 600, BF), ("kb", 144, F32),
+    ("basea", 144, F32), ("oa", 18, U16), ("ob", 10, U16), ("aa", 144, I32), ("offs", 144, F32), ("offa", 148, F32), ("dl", 144, F32),
+    ("mk", 8 * E, F32), ("vw", OWN + 38 * H, BF), ("mm", 152, F32), ("px", 144, F32), ("zz", 144, F32), ("oz", 18, U16),
+    ("ah", 1152, BF), ("af", 1152, BF), ("rr", 1152, F32), ("yo", 288, F32), ("oe1", 128, F32), ("oe2", 128, F32),
+] + [(k % t, c, d) for t in range(4) for k, c, d in (("xq%d", C, X4), ("xs%d", C, U8))] + [
+    (k % t, c, d) for t in range(3) for k, c, d in (
+        ("fxq%d", C, X4), ("fxs%d", C, U8), ("ll%d", 8, U16), ("sl%d", 8, U16), ("bq%d", 128, X4), ("bs%d", 128, U8),
+        ("rq%d", C // 2, X4), ("rs%d", C, U8), ("rl%d", 8, U16))]:
+    SCRATCH[_n] = ("sbuf", [128, _c], _d)
+SHARE = {"pi": ("ci", 0), "pbi": ("ci", 8), "mi": ("ci", 32), "mj": ("ci", 64), "ma": ("cf", 0), "mb": ("cf", 32), "c16": ("cf", 64),
+         "idx": ("cf", 96), "sb": ("si", 0), "ab": ("si", 16), "nbi": ("si", 32), "oag": ("sf", 0), "oaf": ("sf", 32), "obf": ("sf", 64),
+         "ocf": ("sf", 96), "baseb": ("sf", 128), "nb8b": ("sf", 160)}
+
+
+def A(name, c0, c1, step=1, p0=0, p1=128):
+    name, at = SHARE.get(name, (name, 0))
+    return ("ap", name, p0, p1, at + c0, at + c1, step)
+
+
+def bank(k, c0, c1, step=1, p0=0, p1=128):
+    return A("ps", 512 * k + c0, 512 * k + c1, step, p0, p1)
+
+
+def cast(a, d):
+    return ("cast", a, d)
+
+
+def ind(a, off):
+    return ("ind", a, off)
+
+
+def hbm(name, idx):
+    return ("hbm", name, idx)
+
+
+def _real(T, a):
+    if not isinstance(a, tuple):
+        return a
+    if a[0] == "ap":
+        if a[6] == 1:
+            return T[a[1]][a[2]:a[3], a[4]:a[5]]
+        return T[a[1]][a[2]:a[3], a[4]:a[5]:a[6]]
+    if a[0] == "cast":
+        return _real(T, a[1]).bitcast(dt.uint8 if a[2] == 8 else dt.uint32)
+    if a[0] == "ind":
+        return _real(T, a[1]).indirect(_real(T, a[2]))
+    return T[a[1]][a[2]]
+
+
+def _parts(a):
+    if not isinstance(a, tuple) or a[0] == "hbm":
+        return [], []
+    if a[0] == "ap":
+        return [a], []
+    if a[0] == "cast":
+        return _parts(a[1])
+    return _parts(a[1])[0], [a[2]]
+
+
+def _count(a):
+    if a[0] == "ind":
+        return 16 * (a[2][5] - a[2][4])
+    if a[0] == "cast":
+        return _count(a[1])
+    return len(range(a[4], a[5], a[6]))
+
+
+def _two(a):
+    return a[0] == "ap" and SCRATCH[a[1]][2] == BF
+
+
+def _mask(a):
+    if a[6] == 1:
+        return ((1 << (a[5] - a[4])) - 1) << a[4]
+    m = 0
+    for c in range(a[4], a[5], a[6]):
+        m |= 1 << c
+    return m
+
+
+def _program():
+    ops = []
+    AL, AF = AluOpType, ActivationFunctionType
+    POOL = A("pool", 0, 1)
+
+    def add(how, outs, ins, acc=False, tag=None):
+        rd, wr = [], []
+        for o in outs:
+            d, f = _parts(o)
+            wr += d
+            rd += f
+        for i in ins:
+            d, f = _parts(i)
+            rd += d + f
+        ops.append({"how": how, "rd": rd, "wr": wr, "acc": acc, "tag": tag})
+
+    def vcost(n, r):
+        return FIX + max(64.0, n * r) * CYC
+
+    def rate(out, in_):
+        if in_[0] == "ind":
+            return 1.56
+        if out[0] == "ind":
+            return 3.8
+        return 0.5 if _two(out) and _two(in_) else 1.0
+
+    def copy(out, in_, eng="V", scale=None):
+        n, how = _count(out if out[0] != "ind" else in_), {}
+        if "V" in eng:
+            if scale is None:
+                how["V"] = (vcost(n, rate(out, in_)), lambda q, R: q.tensor_copy(R(out), R(in_)))
+            else:
+                how["V"] = (vcost(n, rate(out, in_)), lambda q, R: q.tensor_scalar(R(out), R(in_), scale, None, AL.mult))
+        if "S" in eng:
+            r = 1.56 if in_[0] == "ind" else 1.0
+            if scale is None:
+                how["S"] = (vcost(n, r), lambda q, R: q.activation(R(out), R(in_), AF.Copy))
+            else:
+                how["S"] = (vcost(n, r), lambda q, R: q.activation(R(out), R(in_), AF.Copy, scale=scale))
+        add(how, [out], [in_])
+
+    def lin(out, in_, m, plus):
+        c = vcost(_count(out), 1.0)
+        add({"V": (c, lambda q, R: q.tensor_scalar(R(out), R(in_), m, R(plus), AL.mult, AL.add)),
+             "S": (c, lambda q, R: q.activation(R(out), R(in_), AF.Identity, bias=R(plus), scale=m))}, [out], [in_, plus])
+
+    def ts(out, in0, s1, s2, op0, op1=None):
+        if op1 is None:
+            f = lambda q, R: q.tensor_scalar(R(out), R(in0), R(s1), None, op0)
+        else:
+            f = lambda q, R: q.tensor_scalar(R(out), R(in0), R(s1), R(s2), op0, op1)
+        add({"V": (vcost(_count(out), rate(out, in0)), f)}, [out], [in0, s1, s2])
+
+    def tt(out, in0, in1, op):
+        r = 1.0 if "ps" in (in0[1], in1[1]) else 2.0
+        add({"V": (vcost(_count(out), r), lambda q, R: q.tensor_tensor(R(out), R(in0), R(in1), op))}, [out], [in0, in1])
+
+    def scan(out, d0, d1, op0, op1):
+        add({"V": (vcost(_count(out), 1.0), lambda q, R: q.tensor_tensor_scan(R(out), R(d0), R(d1), 0.0, op0, op1))}, [out], [d0, d1])
+
+    def fill(out, v):
+        add({"V": (vcost(_count(out), 0.5 if _two(out) else 1.0), lambda q, R: q.memset(R(out), v))}, [out], [])
+
+    def zero(out):
+        src = A("ones", 0, _count(out), 1, out[2], out[3])
+        add({"V": (vcost(_count(out), 1.0), lambda q, R: q.memset(R(out), 0.0)),
+             "S": (vcost(_count(out), 1.0), lambda q, R: q.activation(R(out), R(src), AF.Copy, scale=0.0))}, [out], [src])
+
+    def turn(out, in_):
+        add({"V": (vcost(_count(out), 1.0), lambda q, R: q.transpose(R(out), R(in_)))}, [out], [in_])
+
+    def act(out, in_, func, bias=None, scale=1.0):
+        if bias is None:
+            f = lambda q, R: q.activation(R(out), R(in_), func, scale=scale)
+        else:
+            f = lambda q, R: q.activation(R(out), R(in_), func, bias=R(bias))
+        add({"S": (vcost(_count(out), 1.0), f)}, [out], [in_, bias])
+
+    def quant(pair, c0, n, in_):
+        o, s = A(pair[0], c0, c0 + n), A(pair[1], c0, c0 + n)
+        add({"V": (FIX + n, lambda q, R: q.quantize_mx(R(o), R(s), R(in_)))}, [o, s], [in_])
+
+    def mm(k, st, s0, mv, m0, n, start=True, stop=True):
+        o = bank(k, 0, n)
+        a, b, c, d = A(st[0], s0, s0 + 128), A(st[1], s0, s0 + 128), A(mv[0], m0, m0 + n), A(mv[1], m0, m0 + n)
+        add({"P": (20 + (n + 16) * PEC, lambda q, R: q.matmul_mx(R(o), R(a), R(b), R(c), R(d), start, stop))}, [o], [a, b, c, d], acc=not start)
+
+    def pick(dst, d0, src, ncols, off):
+        n = _count(ind(None, off))
+        copy(cast(A(dst[0], d0, d0 + n), 32), ind(cast(A(src[0], 0, ncols), 32), off), "V")
+        copy(A(dst[1], d0, d0 + n), ind(A(src[1], 0, ncols), off), "VS")
+
+    def dma(out, in_, eng="Y", t=DMA_T, behind=None):
+        add({eng: (t, lambda q, R: q.dma_start(R(out), R(in_)))}, [out], [in_, behind], tag="dma")
+
+    def blank(name, c0, c1, p1=128):
+        dma(A(name, c0, c1, 1, 0, p1), A("zb", 0, c1 - c0, 1, 0, p1))
+
+    def iota(out, pat, base, cm, flag):
+        if flag:
+            f = lambda q, R: q.iota(R(out), pat, base, cm, allow_small_or_imprecise_dtypes=True)
+        else:
+            f = lambda q, R: q.iota(R(out), pat, base, cm)
+        add({"G": (150 + 2 * _count(out) * CYC, f)}, [out, POOL], [])
+
+    def where(out, in_, pat, op, fillv, base, cm):
+        add({"G": (190 + 2 * _count(out) * CYC, lambda q, R: q.affine_select(R(out), R(in_), pat, op, fillv, base, cm))}, [out, POOL], [in_])
+
+    def send(t, kind, cost, ins):
+        add({"G": (cost, None)}, [A("wire", 2 * t + kind, 2 * t + kind + 1)], ins, tag=("send", t, kind))
+
+    def land(t, kind, cost, outs):
+        add({"N": (cost, None)}, outs, [A("wire", 2 * t + min(kind, 1), 2 * t + min(kind, 1) + 1)], tag=("land", t, kind))
+
+    UQ, VQ, WQ, UP, EQ, CQ = ("uq", "us"), ("vq", "vs"), ("wq", "wsc"), ("upq", "ups"), ("eq", "es"), ("cq", "cs")
+    FQ, GQ, JQ, HQ, ZQ = ("fq", "fs"), ("gq", "gs"), ("jq", "js"), ("hq", "hs"), ("zq", "zs")
+    XQ = [("xq%d" % t, "xs%d" % t) for t in range(4)]
+    every = slice(None)
+
+    def pb(k):
+        return A("pb", k, k + 1)
+
+    dma(A("xin", 0, 1152), hbm("x", every), "Y", 3000)
+    dma(A("uin", 0, 512), hbm("u", every), "S", 2600)
+    for c in range(4):
+        dma(A("m0", 32 * c, 32 * c + 32, 1, 0, 9), hbm("nb", (c, every)))
+        dma(A("m0", 128 + 32 * c, 160 + 32 * c, 1, 0, 9), hbm("e", (c, every)))
+    dma(cast(A("wq", 0, 512), 8), hbm("wc", every))
+    dma(A("wsc", 0, 512), hbm("ws", every))
+    dma(A("vin", 0, 512), hbm("v", every))
+    iota(A("pi", 0, 2), [[1, 2]], 0, 1, False)
+    iota(A("mi", 0, 32), [[1, 32]], 128, -1, False)
+    fill(A("zb", 0, 520), 0.0)
+    fill(A("ones", 0, 520), 1.0)
+    p0, p1 = A("pi", 0, 1), A("pi", 1, 2)
+    ts(A("pbi", 1, 2), p0, 7, None, AL.bitwise_and)
+    ts(A("pbi", 6, 7), p1, 7, None, AL.bitwise_and)
+    ts(A("pbi", 0, 1), p0, 15, None, AL.bitwise_and)
+    ts(A("pbi", 2, 3), p0, 3, None, AL.bitwise_and)
+    ts(A("pbi", 3, 4), p0, 3, 1, AL.logical_shift_right, AL.bitwise_and)
+    ts(A("pbi", 4, 5), p0, 2, 1, AL.logical_shift_right, AL.bitwise_and)
+    ts(A("pbi", 5, 6), p0, 4, None, AL.logical_shift_right)
+    copy(A("pb", 0, 7), A("pbi", 0, 7))
+    fill(A("c16", 0, 16), 16.0)
+    fill(pb(15), float(TURN))
+    fill(A("lu", 0, 18), 2)
+    ts(A("lu", 8, 16), A("c16", 0, 8), pb(1), 1.0, AL.mult, AL.add)
+    ts(A("lu", 18, 27), A("c16", 0, 9), pb(1), None, AL.mult)
+    ts(A("lu", 27, 36), A("c16", 0, 9), pb(6), None, AL.mult)
+    quant(UQ, 0, 128, A("uin", 0, 512))
+    quant(XQ[0], 0, C, A("xin", 0, 1152))
+    pick(UP, 0, UQ, 128, A("lu", 0, 17))
+    pick(UP, 272, UQ, 128, A("lu", 18, 36))
+    fill(A("tri", 256, 288), BIG)
+    where(A("tri", 0, 256), A("zb", 0, 256), [[0, 2], [1, 128]], AL.is_ge, BIG, 0, -1)
+    where(A("tri", 256, 288, 1, 96, 128), A("zb", 0, 32, 1, 96, 128), [[1, 32]], AL.is_ge, BIG, 0, -1)
+    quant(CQ, 0, 128, A("ones", 0, 512))
+    for c0 in (0, 384, 768):
+        blank("ft", c0, c0 + 384, 96)
+    ts(A("mj", 0, 32), A("mi", 0, 32), 15, None, AL.bitwise_and)
+    ts(A("ma", 0, 32), A("mj", 0, 32), 0.0, 8192.0, AL.is_equal, AL.mult)
+    ts(A("mb", 0, 32), A("mj", 0, 32), 1.0, -4096.0, AL.is_equal, AL.mult)
+    tt(A("rw", 0, 32), A("ma", 0, 32), A("mb", 0, 32), AL.add)
+    copy(A("rw", 32, 64), A("rw", 0, 32), "VS")
+    copy(A("rw", 256, 288), A("rw", 0, 32), "VS")
+    copy(A("rw", 64, 128), A("rw", 0, 64), "VS")
+    copy(A("rw", 128, 256), A("rw", 0, 128), "VS")
+    ts(pb(13), pb(0), 15.0, 4096.0, AL.not_equal, AL.mult)
+    ts(pb(14), pb(13), -1.0, None, AL.add)
+    iota(A("iot", 0, 288), [[1, 288]], 0, 0, True)
+    where(A("ebig", 0, 512), A("ones", 0, 512), [[-1, 512]], AL.is_equal, 0.0, 3, 4)
+    copy(A("ebig", 512, 1024), A("ebig", 0, 512), "VS")
+    for b in range(4):
+        quant(EQ, 240 * b, 240, A("ebig", 3 - b, 963 - b))
+    for c0, c1 in ((0, 512), (512, 1032), (1032, 1552)):
+        blank("sel", c0, c1)
+    s_sum, s_a, s_c = A("sel", 0, 512, 4), A("sel", 516, 1028, 8), A("sel", 1036, 1548, 8)
+    where(s_sum, A("ones", 0, 128), [[-16, 8], [0, 16]], AL.is_ge, 0.0, 0, 1)
+    where(s_sum, s_sum, [[16, 8], [0, 16]], AL.is_ge, 0.0, 15, -1)
+    where(s_a, A("ones", 0, 64), [[0, 8], [-16, 8]], AL.is_ge, 0.0, 0, 1)
+    where(s_a, s_a, [[0, 8], [16, 8]], AL.is_ge, 0.0, 15, -1)
+    where(s_c, A("ones", 0, 64), [[-1, 8], [-16, 8]], AL.is_equal, 0.0, 0, 1)
+    for k, c0 in enumerate((0, 516, 512, 1036, 1032)):
+        quant(CQ, 128 * (k + 1), 128, A("sel", c0, c0 + 512))
+    fill(A("rf", 0, 64), 0.0)
+    blank("rc", 0, 144)
+    fill(A("rf", 0, 64, 16), -BIG)
+    fill(A("rc", 0, 144, 4), -BIG)
+    for a in (A("mm", 0, 8), A("offa", 0, 1), A("vv", 0, 160), A("oe1", 0, 128, 1, 0, 32)):
+        zero(a)
+    for name, c0, c1 in (("ff", 0, 256), ("fg", 0, 256), ("fa", 0, 304), ("fa", 304, 600)):
+        blank(name, c0, c1)
+    for u0, u1 in ((1, 3), (5, 6), (32, 33), (35, 37)):
+        blank("vw", OWN + H * u0, OWN + H * u1)
+    lin(pb(8), pb(3), 16.0, pb(4))
+    lin(pb(9), pb(5), 2.0, pb(8))
+    lin(pb(10), pb(2), 32.0, pb(9))
+    ts(pb(11), pb(3), 32.0, 32.0, AL.mult, AL.add)
+    lin(pb(12), pb(2), 64.0, pb(11))
+    ts(A("lown", 0, 9), A("iot", 0, 288, 32), pb(9), None, AL.add)
+    ts(A("l12", 0, 2), A("iot", 0, 4, 2), pb(10), None, AL.add)
+    ts(A("l12", 2, 18, 2), A("iot", 0, 128, 16), pb(0), None, AL.add)
+    ts(A("l12", 3, 18, 2), A("iot", 0, 128, 16), pb(0), None, AL.add)
+    ts(A("l3", 0, 9), A("iot", 0, 9), pb(12), None, AL.add)
+    lin(A("idx", 0, 18), A("iot", 0, 288, 16), 1.0, pb(0))
+    ts(A("m1", 0, 128, 1, 0, 9), A("m0", 0, 128, 1, 0, 9), 8.0, None, AL.mult)
+    tt(A("vv", 0, 128, 1, 0, 9), A("m1", 0, 128, 1, 0, 9), A("m0", 128, 256, 1, 0, 9), AL.add)
+    for k in (32, 64, 96):
+        dma(A("vv", 0, 128, 1, k, k + 9), A("vv", 0, 128, 1, 0, 9))
+    copy(A("vg", 0, 288), ind(A("vv", 0, 160), A("l12", 0, 18)), "VS")
+    turn(A("vt", 0, 288), A("vg", 0, 288))
+    copy(A("vi", 0, 9), A("vt", 0, 9))
+    copy(A("vi", 16, 160), ind(A("vt", 0, 288), A("l3", 0, 9)))
+    ts(A("sb", 0, 9), A("vi", 0, 9), 7, None, AL.bitwise_and)
+    ts(A("sa", 0, 144), A("vi", 16, 160), 7, None, AL.bitwise_and)
+    tt(A("nb8b", 0, 9), A("vi", 0, 9), A("sb", 0, 9), AL.subtract)
+    ts(A("aa", 0, 144), A("vi", 16, 160), 3, None, AL.logical_shift_right)
+    ts(A("dl", 0, 144), A("aa", 0, 144), float(C), None, AL.is_ge)
+    copy(A("offs", 0, 144), A("dl", 0, 144), "VS", float(OWN - C))
+    tt(A("nbm", 0, 144), A("offs", 0, 144), A("aa", 0, 144), AL.add)
+    lin(A("mul", 0, 144), A("dl", 0, 144), float(FAR - TURN), pb(15))
+    ts(A("nbi", 0, 9), A("vi", 0, 9), 3, None, AL.logical_shift_right)
+    copy(A("lnb", 0, 9), A("nbi", 0, 9))
+    quant(VQ, 0, 128, A("vin", 0, 512))
+
+    turns = [0]
+
+    def stream(st, s0, mv, n, c1, out, scale):
+        k = 5 + turns[0] % 3
+        turns[0] += 1
+        mm(k, st, s0, mv, 0, n)
+        copy(out, bank(k, 0, c1), "VS", scale)
+
+    def frames(to, ks, ff, gq, at):
+        for w in range(3):
+            a = at + 64 * w
+            scan(A("pm", a, a + 64), A("rf", 0, 64), bank(ks[w], 0, 64), AL.add, AL.max)
+            tt(A(ff, w, 224, 4), A("pm", a, a + 56), A("pm", a + 8, a + 64), AL.is_lt)
+        copy(A(ff, 256, 512), A(ff, 0, 256), "VS")
+        quant(gq, 0, 128, A(ff, 0, 512))
+        for w in range(3):
+            mm(ks[w], gq, 0, EQ, 240 * w, 128)
+        copy(A(to, 0, 128), bank(ks[0], 0, 128), "VS")
+        copy(A(to, 128, 256), bank(ks[1], 0, 128), "VS")
+        copy(A(to, 256, 288), bank(ks[2], 96, 128), "VS")
+
+    def counted(window, lst):
+        copy(A("fa", 0, 576, 4), ind(window, lst), "VS")
+        quant(HQ, 0, 150, A("fa", 0, 600))
+        mm(1, CQ, 128, HQ, 0, 144)
+        mm(2, CQ, 256, HQ, 0, 144, True, False)
+        mm(2, CQ, 384, HQ, 4, 144, False, True)
+        scan(A("kb", 0, 144), A("rw", 0, 144), bank(1, 0, 144), AL.add, AL.min)
+
+    def mark_at(r):
+        return 272 + r if r % 2 == 0 else 416 + r - 1
+
+    for t in range(3):
+        X, L, FX = XQ[t], ("bq%d" % t, "bs%d" % t), ("fxq%d" % t, "fxs%d" % t)
+        send(t, 0, 800.0, [A(X[0], 0, C), A(X[1], 0, C)])
+        mm(0, UP, 0, X, 0, C)
+        for w, c0 in enumerate((0, 128, 160)):
+            mm(1 + w, X, c0, UP, 128, 130)
+            copy(A("pc", w, w + 1), bank(1 + w, 128, 129), "S")
+        for w, (c0, c1) in enumerate(((0, 128), (128, 256), (256, 288))):
+            act(A("th", c0, c1), A("tri", c0, c1), AF.Identity, A("pc", w, w + 1))
+        ts(A("ft", 0, 512, 4), bank(0, 0, 128), A("pc", 0, 1), None, AL.is_lt)
+        ts(A("ft", 512, 1152, 4), bank(0, 128, 288), A("pc", 0, 1), None, AL.is_le)
+        ts(A("ft", 1, 1024, 4), bank(0, 0, 256), A("pc", 1, 2), None, AL.is_lt)
+        ts(A("ft", 1025, 1152, 4), bank(0, 256, 288), A("pc", 1, 2), None, AL.is_le)
+        ts(A("ft", 2, 1152, 4, 96, 128), bank(0, 0, 288, 1, 96, 128), A("pc", 2, 3, 1, 96, 128), None, AL.is_lt)
+        tt(A("ft", 3, 1152, 4), bank(0, 0, 288), A("th", 0, 288), AL.is_equal)
+        quant(FQ, 0, C, A("ft", 0, 1152))
+        mm(0, CQ, 0, FQ, 0, C)
+        scan(A("w1", 0, 288), A("rw", 0, 288), bank(0, 0, 288), AL.add, AL.min)
+        ts(A("o1", 0, 18), A("w1", 15, 288, 16), pb(14), None, AL.add)
+        copy(ind(A("lst", 0, 288), A("o1", 0, 18)), A("iot", 0, 288))
+        scan(A("w2", 0, 128), A("rw", 0, 128), A("lst", 0, 128), AL.add, AL.min)
+        ts(A("sl%d" % t, 0, 8), A("w2", 15, 128, 16), pb(13), None, AL.add)
+        send(t, 1, 400.0, [A("sl%d" % t, 0, 8)])
+        issued = A("wire", 8 + t, 9 + t)
+        land(t, 2, 100.0, [issued])
+        frames("fl", (1, 2, 3), "ff", GQ, 0)
+        counted(A("fl", 0, C), A("lown", 0, 9))
+        tt(A("baseb", 0, 9), A("sb", 0, 9), A("kb", 15, 144, 16), AL.subtract)
+        tt(A("basea", 0, 144), A("sa", 0, 144), bank(2, 0, 144), AL.subtract)
+        copy(A("oag", 0, 18), bank(2, 0, 144, 8), "VS", float(TURN))
+        tt(A("oaf", 0, 18), A("oag", 0, 18), A("idx", 0, 18), AL.add)
+        copy(A("oa", 0, 18), A("oaf", 0, 18))
+        step = min(MADE, 2)
+        for r in range(MADE):
+            for b in range(4):
+                stream(EQ, 240 * b + 16 * r, X, C, C, A("vw", TURN * r + C * b, TURN * r + C * b + C), 0.5)
+            if r % step == step - 1:
+                r0 = r + 1 - step
+                for to in range(r0 + MADE, 8, MADE):
+                    c0, cut, w = TURN * r0, 16 * (to - r0), TURN * step
+                    dma(A("vw", TURN * to, TURN * to + w, 1, 0, 128 - cut), A("vw", c0, c0 + w, 1, cut, 128), "Y", DMA_T + 1500 * step, issued)
+                    dma(A("vw", TURN * to, TURN * to + w, 1, 128 - cut, 128), A("vw", c0, c0 + w, 1, 0, cut), "Y", DMA_T + 1500 * step, issued)
+        for r in range(8):
+            stream(UP, mark_at(r), X, C, C, A("mk", r, 8 * C, 8), None)
+        for b in range(4):
+            copy(A("ah", C * b, C * b + C), ind(A("vw", C * b, OWN - C * (3 - b)), A("oa", 0, 18)), "VS")
+            copy(A("af", C * b, C * b + C), A("ah", C * b, C * b + C), "VS", 2.0)
+        land(t, 0, WIRE_X, [A(FX[0], 0, C), A(FX[1], 0, C)])
+        for w, c0 in enumerate((0, 128, 160)):
+            mm((0, 4, 3)[w], FX, c0, UP, 128, 128)
+        frames("flx", (0, 4, 3), "fg", JQ, 192)
+        land(t, 1, WIRE_L, [A("ll%d" % t, 0, 8)])
+        copy(A("fl", C, E), ind(A("flx", 0, C), A("ll%d" % t, 0, 6)), "VS")
+        pick(L, 0, FX, C, A("ll%d" % t, 0, 8))
+        for r in range(8):
+            stream(UP, mark_at(r), L, 128, H, A("mk", 8 * C + r, 8 * E, 8), None)
+        counted(A("fl", 0, E), A("lnb", 0, 9))
+        tt(A("ab", 0, 9), A("kb", 15, 144, 16), A("baseb", 0, 9), AL.add)
+        ts(A("sb", 0, 9), A("ab", 0, 9), 7, None, AL.bitwise_and)
+        tt(A("obf", 0, 9), A("sb", 0, 9), A("nb8b", 0, 9), AL.add)
+        copy(A("ob", 0, 9), A("obf", 0, 9))
+        tt(A("aa", 0, 144), bank(2, 0, 144), A("basea", 0, 144), AL.add)
+        ts(A("sa", 0, 144), A("aa", 0, 144), 7, None, AL.bitwise_and)
+        tt(A("offs", 0, 144), A("sa", 0, 144), A("mul", 0, 144), AL.mult)
+        tt(A("offa", 1, 145), A("offs", 0, 144), A("nbm", 0, 144), AL.add)
+        tt(A("dl", 0, 144), A("offa", 0, 144), A("offa", 1, 145), AL.subtract)
+        for b in range(4):
+            for r in range(8):
+                at = OWN + FAR * r + C * b
+                stream(EQ, 240 * b + 16 * r, L, 128, H, A("vw", at, at + H), 0.5)
+        copy(A("mm", 8, 152), ind(A("mk", 0, 8 * E), A("ob", 0, 9)), "VS")
+        scan(A("px", 0, 144), A("mm", 7, 151), A("rc", 0, 144), AL.max, AL.add)
+        tt(A("fa", 0, 576, 4), A("mm", 8, 152), A("px", 0, 144), AL.is_le)
+        quant(HQ, 0, 150, A("fa", 0, 600))
+        mm(1, CQ, 512, HQ, 0, 144, True, False)
+        mm(1, CQ, 640, HQ, 4, 144, False, True)
+        scan(A("zz", 0, 144), A("dl", 0, 144), bank(1, 0, 144), AL.add, AL.mult)
+        tt(A("ocf", 0, 18), A("zz", 3, 144, 8), A("offa", 4, 145, 8), AL.add)
+        copy(A("oz", 0, 18), A("ocf", 0, 18))
+        runs = ((0, 160), (160, 288))
+        for h, (c0, c1) in enumerate(runs):
+            for b in range(4):
+                tt(A("zt", 4 * c0 + b, 4 * c1, 4), ind(A("vw", C * b, C * b + OWN + 29 * H), A("oz", c0 // 16, c1 // 16)),
+                   A("ah", C * b + c0, C * b + c1), AL.add)
+            quant(ZQ, c0, c1 - c0, A("zt", 4 * c0, 4 * c1))
+            for b in range(4):
+                mm(4 * h + b, WQ, 128 * b, ZQ, c0, c1 - c0)
+                act(A("rr", C * b + c0, C * b + c1), bank(4 * h + b, 0, c1 - c0), AF.Relu, None, 0.03125)
+        for h, (c0, c1) in enumerate(runs):
+            for b in range(4):
+                tt(A("xt", 4 * c0 + b, 4 * c1, 4), A("rr", C * b + c0, C * b + c1), A("af", C * b + c0, C * b + c1), AL.add)
+            quant(XQ[t + 1], c0, c1 - c0, A("xt", 4 * c0, 4 * c1))
+    for c in range(4):
+        copy(A("oe1", 32 * c, 32 * c + 18, 1, 0, 32), A("sa", c, 144, 8, 0, 32))
+    turn(A("oe2", 0, 128, 1, 0, 32), A("oe1", 0, 128, 1, 0, 32))
+    for c in range(4):
+        dma(hbm("oe", (c, every)), A("oe2", 32 * c, 32 * c + 16, 1, 0, 18))
+    for h, (c0, c1) in enumerate(((0, 160), (160, 288))):
+        mm(h, VQ, 0, XQ[3], c0, c1 - c0)
+        copy(A("yo", c0, c1), bank(h, 0, c1 - c0), "VS")
+    dma(hbm("oc", every), cast(A("xq3", 0, C), 8))
+    for k in range(4):
+        dma(hbm("osc", (slice(4 * k, 4 * k + 4), every)), A("xs3", 0, C, 1, 32 * k, 32 * k + 4), "Y" if k % 2 else "S")
+    dma(hbm("y", every), A("yo", 0, C), "S")
+    return ops
+
+
+def _depends(ops):
+    seen = {}
+    for i, op in enumerate(ops):
+        deps = {}
+        for a, w in [(a, False) for a in op["rd"]] + [(a, True) for a in op["wr"]]:
+            if a[1] == "ps":
+                key, m, lo, hi = ("ps", a[4] // 512), 1, 0, 128
+            else:
+                key, m, lo, hi = a[1], _mask(a), a[2], a[3]
+            old = seen.setdefault(key, [])
+            for j, m2, lo2, hi2, w2 in old:
+                if j != i and m & m2 and lo < hi2 and lo2 < hi:
+                    if w or w2:
+                        deps[j] = deps.get(j, False) or not (op["acc"] and a[1] == "ps")
+                    elif a[1] == "ps":
+                        deps.setdefault(j, False)
+            if w:
+                old[:] = [o for o in old if o[0] == i or not (o[1] & ~m == 0 and lo <= o[2] and o[3] <= hi)]
+            old.append((i, m, lo, hi, w))
+        op["deps"] = deps
+
+
+def _kind(op):
+    w = op["wr"][0] if op["wr"] else A("out", 0, 1)
+    name = w[1].rstrip("0123")
+    if name == "ps":
+        return "p" + op["rd"][2][1].rstrip("0123") + str(min(w[4] // 512, 5))
+    if name in ("vw", "mk"):
+        return name + str(w[4] >= (OWN if name == "vw" else 8 * C))
+    if name in ("zt", "xt", "rr"):
+        return name + str(w[4] % C > 0 if name == "rr" else w[4] >= 640)
+    return name + str(w[4]) + (op["rd"][0][1] + str(op["rd"][0][5]) if name == "fa" else "")
+
+
+def _place(ops, before, turn, spare):
+    n = len(ops)
+    busy = {e: [] for e in "VSPGYN"}
+    done, eng = [0.0] * n, [None] * n
+    for i in turn:
+        op, best = ops[i], None
+        for e, (cost, f) in op["how"].items():
+            t = 0.0
+            for j, hard in before[i]:
+                d = done[j] + (HOP if hard or eng[j] != e else 0.0)
+                if d > t:
+                    t = d
+            hold = 100.0 if op["tag"] == "dma" else 1.0 if e == "N" else cost
+            row = busy[e]
+            lo, hi = 0, len(row)
+            while lo < hi:
+                mid = (lo + hi) // 2
+                if row[mid][1] <= t:
+                    lo = mid + 1
+                else:
+                    hi = mid
+            while lo < len(row) and row[lo][0] < t + hold:
+                t = max(t, row[lo][1])
+                lo += 1
+            worth = t + cost + (spare.get(op["kind"], 400.0) if e == "V" else 0.0)
+            if best is None or worth < best[0]:
+                best = (worth, t, e, lo, hold, cost)
+        done[i], eng[i] = best[1] + best[5], best[2]
+        busy[best[2]].insert(best[3], (best[1], best[1] + best[4], i))
+    return max(done), done, eng, {e: [x[2] for x in busy[e]] for e in busy}
+
+
+def _schedule():
+    ops = _program()
+    _depends(ops)
+    n, count = len(ops), {}
+    for op in ops:
+        op["kind"] = _kind(op)
+        if op["kind"] in ("hq0", "kb0"):
+            count[op["kind"]] = count.get(op["kind"], 0) + 1
+            op["kind"] += str(count[op["kind"]] % (3 if op["kind"] == "hq0" else 2))
+    before = [list(op["deps"].items()) for op in ops]
+    after = [[] for _ in range(n)]
+    for i in range(n):
+        for j, hard in before[i]:
+            after[j].append(i)
+    left = [0.0] * n
+    for i in range(n - 1, -1, -1):
+        left[i] = min(c for c, f in ops[i]["how"].values()) + HOP + max([left[k] for k in after[i]] + [0.0])
+    kinds = sorted(set(op["kind"] for op in ops))
+    free = sorted(set(op["kind"] for op in ops if len(op["how"]) > 1))
+    ahead = {"vwFalse": 2500, "ztFalse": 2000, "zq0": 4000, "rrFalse": 3000, "xtFalse": 500, "mm8": 2000, "jq0": 2500}
+    spare = {"vwTrue": 9000, "vwFalse": 3000, "mkTrue": 1500, "mm8": 9000, "af0": 9000, "af288": 9000, "af576": 9000, "af864": 9000}
+    seed, now, best = [12345], None, None
+
+    def draw(row):
+        seed[0] = (seed[0] * 1103515245 + 12345) % 2147483648
+        return row[(seed[0] >> 8) % len(row)]
+
+    for trial in range(TRIES):
+        a2, s2 = dict(ahead), dict(spare)
+        for k in range(draw((1, 1, 2, 3)) if trial else 0):
+            if draw(range(5)) == 0:
+                s2[draw(free)] = draw((0, 100, 200, 400, 800, 1500, 3000, 9000))
+            else:
+                name = draw(kinds)
+                a2[name] = draw((0, a2.get(name, 0) + draw((-1, 1)) * draw((200, 500, 1000, 2000, 4000))))
+        key = [0.0] * n
+        for i in range(n - 1, -1, -1):
+            key[i] = max([left[i] + a2.get(ops[i]["kind"], 0)] + [key[k] + 1.0 for k in after[i]])
+        got = _place(ops, before, sorted(range(n), key=lambda k: -key[k]), s2)
+        if now is None or got[0] <= now + draw(range(150)) * (1.0 - trial / TRIES):
+            now, ahead, spare = got[0], a2, s2
+            if best is None or now < best[0]:
+                best = got
+    span, done, eng, order = best
+    for i, op in enumerate(ops):
+        op["eng"], op["at"] = eng[i], done[i] - op["how"][eng[i]][0]
+    for op in ops:
+        op["all"] = set(j for j, hard in op["deps"].items() if hard or ops[j]["eng"] != op["eng"])
+        inner = set(j for k in op["all"] if ops[k]["eng"] != "N" for j in ops[k]["all"])
+        op["waits"] = [j for j in sorted(op["all"]) if j not in inner]
+    wanted = set(j for op in ops for j in op["waits"])
+    names = []
+    for e in "VSPGY":
+        k = 0
+        for i in order[e]:
+            op = ops[i]
+            if op["tag"] == "dma":
+                op["sig"] = ("d%d" % i, 16)
+                names.append("d%d" % i)
+            elif op["tag"] is None and i in wanted:
+                k += 1
+                op["sig"] = ("on" + e, k)
+            else:
+                op["sig"] = None
+    return ops, order, names, span
+
+
+OPS, ORDER, _DMA_SEMS, SPAN = _schedule()
+SEMAPHORES = ["onV", "onS", "onP", "onG", "left", "issued"] + [k % t for t in range(3) for k in ("arrx%d", "arrl%d", "rela%d", "relb%d")] + _DMA_SEMS
+
+
+def _bits(engines):
+    m = 0
+    for k in engines:
+        m |= 1 << k
+    return m
+
+
+def _helpers(T, topo, src, dst):
+    if topo.may_write(src, dst):
+        return []
+    near = [c for c in topo.cores_of(src) if topo.die(c) == topo.die(src) and T.rank_of(c) is None and topo.may_write(c, dst)]
+    return near[:2]
+
+
+def _arrivals(T, topo, src, dst, kind):
+    via = _helpers(T, topo, src, dst)
+    if not via:
+        return len(topo.engines(src, dst)) * (1 if kind else 2)
+    if kind:
+        return len(topo.engines(via[1], dst))
+    return 2 * len(topo.engines(via[0], dst)) + len(topo.engines(via[1], dst))
+
+
+def _codes(T, name, c0, c1):
+    return T[name][:, c0:c1].bitcast(dt.uint8)
+
+
+def _hand_on(g, core, T, topo):
+    n, sent = len(T.cores), 0
+    for t, d in enumerate(STEP):
+        for r in range(n):
+            src, dst = T.cores[r], T.cores[(r - d) % n]
+            via = _helpers(T, topo, src, dst)
+            if core not in via:
+                continue
+            k, width = via.index(core), len(topo.engines(src, core))
+            rid, pid = topo.addr(dst, core)
+            g.wait_ge(T.sem["rela%d" % t], width // 2)
+            g.remote_dma(_codes(T, "fxq%d" % t, k * C // 2, (k + 1) * C // 2), _codes(T, "rq%d" % t, 0, C // 2),
+                         T.sem["arrx%d" % t], T.sem.left, pid, rid, topo.mask(core, dst))
+            g.wait_ge(T.sem["relb%d" % t], width)
+            if k == 0:
+                g.remote_dma(T["fxs%d" % t][:, 0:C], T["rs%d" % t][:, 0:C], T.sem["arrx%d" % t], T.sem.left, pid, rid, topo.mask(core, dst))
+            else:
+                g.remote_dma(T["ll%d" % t][:, 0:8], T["rl%d" % t][:, 0:8], T.sem["arrl%d" % t], T.sem.left, pid, rid, topo.mask(core, dst))
+            sent += 2 * len(topo.engines(core, dst))
+    if sent:
+        g.wait_ge(T.sem.left, sent)
+
+
+def _send(g, core, T, topo, dst, t, kind):
+    via = _helpers(T, topo, core, dst)
+    first = via[kind] if via else dst
+    rid, pid = topo.addr(first, core)
+    eng = topo.engines(core, first)
+    if kind:
+        out, sem = (T["rl%d" % t], T.sem["relb%d" % t]) if via else (T["ll%d" % t], T.sem["arrl%d" % t])
+        g.remote_dma(out[:, 0:8], T["sl%d" % t][:, 0:8], sem, T.sem.left, pid, rid, _bits(eng))
+        if MADE < 8:
+            g.sem_inc(T.sem.issued, 1)
+        return len(eng)
+    half, parts = len(eng) // 2, []
+    for k in range(2):
+        r2, p2 = topo.addr(via[k] if via else dst, core)
+        out = _codes(T, "rq%d" % t, 0, C // 2) if via else _codes(T, "fxq%d" % t, k * C // 2, (k + 1) * C // 2)
+        parts.append(RemoteDMATransfer(dst_ids=[DstId(rid=r2, pnc=p2)], dma_engine_mask=_bits(eng[k * half:(k + 1) * half]),
+                                       remote_sem=T.sem[("rela%d" if via else "arrx%d") % t],
+                                       src=_codes(T, "xq%d" % t, k * C // 2, (k + 1) * C // 2), dst=out))
+    g.remote_dma_fused(parts, local_sem=T.sem.left)
+    out, sem = (T["rs%d" % t], T.sem["relb%d" % t]) if via else (T["fxs%d" % t], T.sem["arrx%d" % t])
+    g.remote_dma(out[:, 0:C], T["xs%d" % t][:, 0:C], sem, T.sem.left, pid, rid, _bits(eng))
+    return 2 * len(eng)
+
+
+def rank_program(g, core, T, topo):
+    rank = T.rank_of(core)
+    if rank is None:
+        _hand_on(g, core, T, topo)
+        return
+    n = len(T.cores)
+    queues = {"V": g.vector, "S": g.scalar, "P": g.tensor, "G": g, "Y": g.sync}
+    R = lambda a: _real(T, a)
+    top, waited, sent = {}, {}, 0
+    for e in "YSVPG":
+        q, have = queues[e], {}
+        for i in ORDER[e]:
+            op, wants = OPS[i], {}
+            for j in op["waits"]:
+                tag = OPS[j]["tag"]
+                if OPS[j]["eng"] != "N":
+                    name, k = OPS[j]["sig"]
+                elif tag[2] == 2:
+                    name, k = "issued", tag[1] + 1
+                else:
+                    name = ("arrl%d" if tag[2] else "arrx%d") % tag[1]
+                    k = _arrivals(T, topo, T.cores[(rank + STEP[tag[1]]) % n], core, tag[2])
+                wants[name] = max(wants.get(name, 0), k)
+            for name, k in wants.items():
+                if have.get(name, 0) < k:
+                    q.wait_ge(T.sem[name], k)
+                    have[name] = k
+                    waited[name] = max(waited.get(name, 0), k)
+            if op["how"][e][1] is None:
+                t = op["tag"][1]
+                sent += _send(g, core, T, topo, T.cores[(rank - STEP[t]) % n], t, op["tag"][2])
+                continue
+            call = op["how"][e][1](q, R)
+            if op["sig"] is not None:
+                name, k = op["sig"]
+                call.then_inc(T.sem[name], 16 if op["tag"] == "dma" else 1)
+                top[name] = k
+    g.wait_ge(T.sem.left, sent)
+    for name, k in top.items():
+        if waited.get(name, 0) < k:
+            g.wait_ge(T.sem[name], k)

@@ -4,37 +4,44 @@ from concourse.mybir import dt, AluOpType, ActivationFunctionType
 C, H, E = 288, 96, 384
 STEP = [1, 2, 4]
 BIG = 1.0e29
+PRE = 128
 TURN, OWN, FAR = 4 * C, 32 * C, 4 * H
-MADE = 4
-TRIES = 9000
-CYC, PEC, FIX, HOP, DMA_T, WIRE_X, WIRE_L = 1.0, 0.6, 60.0, 120.0, 2200.0, 7000.0, 4500.0
+MT = 512
+MADE, MADEB, EARLY = 1, 2, 2
+EW = 128 + 16 * (max(MADE, MADEB) - 1)
+CAP, HOLD = 65536.0, 16384.0
+TRIES = 1
+CYC, PEC, FIX, HOP, DMA_T, WIRE_X, WIRE_L = 1.0, 0.6, 60.0, 120.0, 1700.0, 5000.0, 3500.0
+ROW, RATE = 25.0, 25.0
 F32, BF, I32, U16, X4, U8 = "float32", "bfloat16", "int32", "uint16", "float8_e4m3fn_x4", "uint8"
+SIZE = {F32: 4, BF: 2, I32: 4, U16: 2, X4: 4, U8: 1}
 
 SCRATCH = {"ps": ("psum", [128, 4096], F32)}
 for _n, _c, _d in [
     ("xin", 1152, BF), ("uin", 512, BF), ("vin", 512, BF), ("xt", 1152, BF), ("zt", 1152, BF),
     ("wq", 512, X4), ("wsc", 512, U8), ("uq", 128, X4), ("us", 128, U8), ("vq", 128, X4), ("vs", 128, U8),
-    ("upq", 560, X4), ("ups", 560, U8), ("eq", 960, X4), ("es", 960, U8), ("cq", 768, X4), ("cs", 768, U8),
+    ("upq", 688, X4), ("ups", 688, U8), ("eq", 4 * EW, X4), ("es", 4 * EW, U8), ("cq", 928, X4), ("cs", 928, U8),
     ("fq", 288, X4), ("fs", 288, U8), ("gq", 128, X4), ("gs", 128, U8), ("jq", 128, X4), ("js", 128, U8),
-    ("hq", 150, X4), ("hs", 150, U8), ("zq", 288, X4), ("zs", 288, U8),
-    ("ones", 520, BF), ("ebig", 1024, BF), ("sel", 1552, BF), ("tri", 288, BF), ("zb", 520, BF),
-    ("rw", 288, BF), ("rf", 64, BF), ("rc", 144, BF), ("iot", 288, F32), ("ci", 96, I32), ("cf", 128, F32), ("pb", 16, F32),
-    ("lu", 36, U16), ("l12", 18, U16), ("l3", 10, U16), ("lown", 10, U16), ("lnb", 10, U16),
-    ("m0", 256, I32), ("m1", 128, F32), ("vv", 160, F32), ("vg", 288, F32), ("vt", 288, F32), ("vi", 160, I32),
-    ("si", 48, I32), ("sf", 192, F32), ("sa", 144, I32), ("nbm", 144, F32), ("mul", 144, F32),
-    ("pc", 4, F32), ("th", 288, F32), ("ft", 1152, BF), ("w1", 288, F32), ("o1", 18, U16), ("lst", 288, F32), ("w2", 128, F32),
-    ("pm", 384, F32), ("ff", 512, BF), ("fg", 512, BF), ("fl", 384, BF), ("flx", 288, BF), ("fa", 600, BF), ("kb", 144, F32),
-    ("basea", 144, F32), ("oa", 18, U16), ("ob", 10, U16), ("aa", 144, I32), ("offs", 144, F32), ("offa", 148, F32), ("dl", 144, F32),
-    ("mk", 8 * E, F32), ("vw", OWN + 38 * H, BF), ("mm", 152, F32), ("px", 144, F32), ("zz", 144, F32), ("oz", 18, U16),
-    ("ah", 1152, BF), ("af", 1152, BF), ("rr", 1152, F32), ("yo", 288, F32), ("oe1", 128, F32), ("oe2", 128, F32),
-] + [(k % t, c, d) for t in range(4) for k, c, d in (("xq%d", C, X4), ("xs%d", C, U8))] + [
-    (k % t, c, d) for t in range(3) for k, c, d in (
-        ("fxq%d", C, X4), ("fxs%d", C, U8), ("ll%d", 8, U16), ("sl%d", 8, U16), ("bq%d", 128, X4), ("bs%d", 128, U8),
+    ("nq", 128, X4), ("ns", 128, U8), ("hq", 200, X4), ("hs", 200, U8), ("kq", 200, X4), ("ks", 200, U8),
+    ("zq", 288, X4), ("zs", 288, U8), ("xq", PRE + 4 * C, X4), ("xs", PRE + 4 * C, U8), ("bq", PRE + 3 * H, X4), ("bs", PRE + 3 * H, U8),
+    ("ones", 512, BF), ("ebig", 4 * EW + 8, BF), ("dig", 1024, BF), ("sel", 2176, BF), ("tri", 128, BF), ("zb", 576, BF), ("zf", 160, F32),
+    ("rw", 144, BF), ("rf", 192, BF), ("rc", 144, BF), ("qrow", 144, BF), ("grow", 128, BF), ("nrow", 96, BF), ("iot", 32, F32),
+    ("ci", 96, I32), ("cf", 320, F32), ("pb", 32, F32),
+    ("lu", 28, U16), ("l12", 20, U16), ("l3", 6, U16), ("lown", 10, U16), ("lnb", 10, U16),
+    ("m0", 256, I32), ("m1", 128, F32), ("vv", 160, F32), ("vg", 320, F32), ("vt", 320, F32), ("vi", 80, I32),
+    ("nbm", 72, F32), ("mul", 72, F32), ("sa", 72, I32), ("aa", 72, I32), ("offs", 72, F32), ("offa", 76, F32), ("dl", 72, F32),
+    ("pc", 4, F32), ("th", 288, F32), ("ft", 1152, BF), ("oh", 512, BF), ("w2", 96, F32),
+    ("pm", 384, F32), ("ff", 512, BF), ("fg", 512, BF), ("fl", 384, BF), ("flx", 288, BF), ("fa", 800, BF), ("kb", 144, F32),
+    ("oa", 18, U16), ("ob", 10, U16), ("mk", 8 * MT, F32), ("vw", OWN + 8 * FAR, BF), ("mm", 152, F32), ("px", 144, F32),
+    ("zz", 72, F32), ("oz", 18, U16), ("ah", 1152, BF), ("af", 1152, BF), ("rr", 1152, F32), ("yo", 288, F32),
+    ("saf", 72, F32), ("oe1", 128, F32), ("oe2", 128, F32),
+] + [(k % t, c, d) for t in range(3) for k, c, d in (
+        ("fxq%d", C, X4), ("fxs%d", C, U8), ("ll%d", 8, U16), ("sl%d", 8, U16),
         ("rq%d", C // 2, X4), ("rs%d", C, U8), ("rl%d", 8, U16))]:
     SCRATCH[_n] = ("sbuf", [128, _c], _d)
-SHARE = {"pi": ("ci", 0), "pbi": ("ci", 8), "mi": ("ci", 32), "mj": ("ci", 64), "ma": ("cf", 0), "mb": ("cf", 32), "c16": ("cf", 64),
-         "idx": ("cf", 96), "sb": ("si", 0), "ab": ("si", 16), "nbi": ("si", 32), "oag": ("sf", 0), "oaf": ("sf", 32), "obf": ("sf", 64),
-         "ocf": ("sf", 96), "baseb": ("sf", 128), "nb8b": ("sf", 160)}
+SHARE = {"pi": ("ci", 0), "vb": ("ci", 32), "ab": ("ci", 48), "nbi": ("ci", 64),
+         "ma": ("cf", 0), "mb": ("cf", 32), "idx": ("cf", 96), "lrow": ("cf", 128), "c18": ("cf", 160),
+         "ta": ("cf", 192), "tb": ("cf", 208), "oaf": ("cf", 224), "ocf": ("cf", 256), "tc": ("cf", 288), "td": ("cf", 304)}
 
 
 def A(name, c0, c1, step=1, p0=0, p1=128):
@@ -103,12 +110,20 @@ def _mask(a):
     return m
 
 
-def _program():
-    ops = []
-    AL, AF = AluOpType, ActivationFunctionType
-    POOL = A("pool", 0, 1)
+def _load(a):
+    a = _parts(a)[0][0]
+    rows, width = a[3] - a[2], _count(a) * SIZE[SCRATCH[a[1]][2]]
+    return max(rows, 16) / 16.0 * ROW + rows * width / (16.0 * RATE)
 
-    def add(how, outs, ins, acc=False, tag=None):
+
+def _program():
+    ops, label = [], ["start"]
+    AL, AF = AluOpType, ActivationFunctionType
+
+    def part(name):
+        label[0] = name
+
+    def add(how, outs, ins, tag=None, load=0.0, calls=1):
         rd, wr = [], []
         for o in outs:
             d, f = _parts(o)
@@ -117,7 +132,7 @@ def _program():
         for i in ins:
             d, f = _parts(i)
             rd += d + f
-        ops.append({"how": how, "rd": rd, "wr": wr, "acc": acc, "tag": tag})
+        ops.append({"how": how, "rd": rd, "wr": wr, "tag": tag, "kind": label[0], "load": load, "calls": calls})
 
     def vcost(n, r):
         return FIX + max(64.0, n * r) * CYC
@@ -125,29 +140,28 @@ def _program():
     def rate(out, in_):
         if in_[0] == "ind":
             return 1.56
-        if out[0] == "ind":
-            return 3.8
         return 0.5 if _two(out) and _two(in_) else 1.0
 
     def copy(out, in_, eng="V", scale=None):
-        n, how = _count(out if out[0] != "ind" else in_), {}
+        n, how = _count(out), {}
         if "V" in eng:
             if scale is None:
                 how["V"] = (vcost(n, rate(out, in_)), lambda q, R: q.tensor_copy(R(out), R(in_)))
             else:
-                how["V"] = (vcost(n, rate(out, in_)), lambda q, R: q.tensor_scalar(R(out), R(in_), scale, None, AL.mult))
+                how["V"] = (vcost(n, rate(out, in_)), lambda q, R: q.tensor_scalar(R(out), R(in_), R(scale), None, AL.mult))
         if "S" in eng:
             r = 1.56 if in_[0] == "ind" else 1.0
             if scale is None:
                 how["S"] = (vcost(n, r), lambda q, R: q.activation(R(out), R(in_), AF.Copy))
             else:
-                how["S"] = (vcost(n, r), lambda q, R: q.activation(R(out), R(in_), AF.Copy, scale=scale))
-        add(how, [out], [in_])
+                how["S"] = (vcost(n, r), lambda q, R: q.activation(R(out), R(in_), AF.Copy if isinstance(scale, float) else AF.Identity, scale=R(scale)))
+        add(how, [out], [in_, scale])
 
     def lin(out, in_, m, plus):
         c = vcost(_count(out), 1.0)
         add({"V": (c, lambda q, R: q.tensor_scalar(R(out), R(in_), m, R(plus), AL.mult, AL.add)),
-             "S": (c, lambda q, R: q.activation(R(out), R(in_), AF.Identity, bias=R(plus), scale=m))}, [out], [in_, plus])
+             "S": (c, lambda q, R: q.activation(R(out), R(in_), AF.Copy if isinstance(plus, float) else AF.Identity, bias=R(plus), scale=m))},
+            [out], [in_, plus])
 
     def ts(out, in0, s1, s2, op0, op1=None):
         if op1 is None:
@@ -168,7 +182,7 @@ def _program():
 
     def zero(out):
         src = A("ones", 0, _count(out), 1, out[2], out[3])
-        add({"V": (vcost(_count(out), 1.0), lambda q, R: q.memset(R(out), 0.0)),
+        add({"V": (vcost(_count(out), 0.5 if _two(out) else 1.0), lambda q, R: q.memset(R(out), 0.0)),
              "S": (vcost(_count(out), 1.0), lambda q, R: q.activation(R(out), R(src), AF.Copy, scale=0.0))}, [out], [src])
 
     def turn(out, in_):
@@ -178,7 +192,7 @@ def _program():
         if bias is None:
             f = lambda q, R: q.activation(R(out), R(in_), func, scale=scale)
         else:
-            f = lambda q, R: q.activation(R(out), R(in_), func, bias=R(bias))
+            f = lambda q, R: q.activation(R(out), R(in_), func, bias=R(bias), scale=scale)
         add({"S": (vcost(_count(out), 1.0), f)}, [out], [in_, bias])
 
     def quant(pair, c0, n, in_):
@@ -188,282 +202,368 @@ def _program():
     def mm(k, st, s0, mv, m0, n, start=True, stop=True):
         o = bank(k, 0, n)
         a, b, c, d = A(st[0], s0, s0 + 128), A(st[1], s0, s0 + 128), A(mv[0], m0, m0 + n), A(mv[1], m0, m0 + n)
-        add({"P": (20 + (n + 16) * PEC, lambda q, R: q.matmul_mx(R(o), R(a), R(b), R(c), R(d), start, stop))}, [o], [a, b, c, d], acc=not start)
+        add({"P": (20 + (n + 16) * PEC, lambda q, R: q.matmul_mx(R(o), R(a), R(b), R(c), R(d), start, stop))}, [o], [a, b, c, d])
 
     def pick(dst, d0, src, ncols, off):
         n = _count(ind(None, off))
         copy(cast(A(dst[0], d0, d0 + n), 32), ind(cast(A(src[0], 0, ncols), 32), off), "V")
         copy(A(dst[1], d0, d0 + n), ind(A(src[1], 0, ncols), off), "VS")
 
-    def dma(out, in_, eng="Y", t=DMA_T, behind=None):
-        add({eng: (t, lambda q, R: q.dma_start(R(out), R(in_)))}, [out], [in_, behind], tag="dma")
+    def dma(pairs, eng="Y", behind=None):
+        load = sum(_load(o if o[0] != "hbm" else i) for o, i in pairs)
+        add({e: (DMA_T, lambda q, R: [q.dma_start(R(o), R(i)) for o, i in pairs]) for e in eng},
+            [o for o, i in pairs], [i for o, i in pairs] + [behind], tag="dma", load=load, calls=len(pairs))
 
-    def blank(name, c0, c1, p1=128):
-        dma(A(name, c0, c1, 1, 0, p1), A("zb", 0, c1 - c0, 1, 0, p1))
+    def blank(runs):
+        dma([(A(name, c0, c1), A("zb", 0, c1 - c0)) for name, c0, c1 in runs])
 
-    def iota(out, pat, base, cm, flag):
+    def again(dst, d0, src, s0, n):
+        dma([(cast(A(dst[0], d0, d0 + n), 8), cast(A(src[0], s0, s0 + n), 8)), (A(dst[1], d0, d0 + n), A(src[1], s0, s0 + n))])
+
+    def iota(out, pat, base, cm, flag=True):
         if flag:
             f = lambda q, R: q.iota(R(out), pat, base, cm, allow_small_or_imprecise_dtypes=True)
         else:
             f = lambda q, R: q.iota(R(out), pat, base, cm)
-        add({"G": (150 + 2 * _count(out) * CYC, f)}, [out, POOL], [])
+        add({"G": (150 + 2 * _count(out) * CYC, f)}, [out], [])
 
     def where(out, in_, pat, op, fillv, base, cm):
-        add({"G": (190 + 2 * _count(out) * CYC, lambda q, R: q.affine_select(R(out), R(in_), pat, op, fillv, base, cm))}, [out, POOL], [in_])
+        add({"G": (190 + 2 * _count(out) * CYC, lambda q, R: q.affine_select(R(out), R(in_), pat, op, fillv, base, cm))}, [out], [in_])
 
-    def send(t, kind, cost, ins):
-        add({"G": (cost, None)}, [A("wire", 2 * t + kind, 2 * t + kind + 1)], ins, tag=("send", t, kind))
+    def send(t, kind, cost, ins, load):
+        add({"G": (cost, None)}, [A("wire", 2 * t + kind, 2 * t + kind + 1)], ins, tag=("send", t, kind), load=load)
 
     def land(t, kind, cost, outs):
         add({"N": (cost, None)}, outs, [A("wire", 2 * t + min(kind, 1), 2 * t + min(kind, 1) + 1)], tag=("land", t, kind))
 
     UQ, VQ, WQ, UP, EQ, CQ = ("uq", "us"), ("vq", "vs"), ("wq", "wsc"), ("upq", "ups"), ("eq", "es"), ("cq", "cs")
-    FQ, GQ, JQ, HQ, ZQ = ("fq", "fs"), ("gq", "gs"), ("jq", "js"), ("hq", "hs"), ("zq", "zs")
-    XQ = [("xq%d" % t, "xs%d" % t) for t in range(4)]
+    FQ, GQ, JQ, NQ, HQ, KQ, ZQ, XQ, BQ = [(k + "q", k + "s") for k in "fgjnhkzxb"]
+    U_ORD, U_FRM, U_MRK = 0, 144, 400
+    C_ONE, C_HI, C_LO, C_SUM, C_CNT, C_OWN, C_CHO = 0, 128, 256, 384, 512, 648, 792
     every = slice(None)
 
-    def pb(k):
-        return A("pb", k, k + 1)
+    def pb(k, p0=0):
+        return A("pb", k, k + 1, 1, p0, 128)
 
-    dma(A("xin", 0, 1152), hbm("x", every), "Y", 3000)
-    dma(A("uin", 0, 512), hbm("u", every), "S", 2600)
-    for c in range(4):
-        dma(A("m0", 32 * c, 32 * c + 32, 1, 0, 9), hbm("nb", (c, every)))
-        dma(A("m0", 128 + 32 * c, 160 + 32 * c, 1, 0, 9), hbm("e", (c, every)))
-    dma(cast(A("wq", 0, 512), 8), hbm("wc", every))
-    dma(A("wsc", 0, 512), hbm("ws", every))
-    dma(A("vin", 0, 512), hbm("v", every))
-    iota(A("pi", 0, 2), [[1, 2]], 0, 1, False)
-    iota(A("mi", 0, 32), [[1, 32]], 128, -1, False)
-    fill(A("zb", 0, 520), 0.0)
-    fill(A("ones", 0, 520), 1.0)
-    p0, p1 = A("pi", 0, 1), A("pi", 1, 2)
-    ts(A("pbi", 1, 2), p0, 7, None, AL.bitwise_and)
-    ts(A("pbi", 6, 7), p1, 7, None, AL.bitwise_and)
-    ts(A("pbi", 0, 1), p0, 15, None, AL.bitwise_and)
-    ts(A("pbi", 2, 3), p0, 3, None, AL.bitwise_and)
-    ts(A("pbi", 3, 4), p0, 3, 1, AL.logical_shift_right, AL.bitwise_and)
-    ts(A("pbi", 4, 5), p0, 2, 1, AL.logical_shift_right, AL.bitwise_and)
-    ts(A("pbi", 5, 6), p0, 4, None, AL.logical_shift_right)
-    copy(A("pb", 0, 7), A("pbi", 0, 7))
-    fill(A("c16", 0, 16), 16.0)
-    fill(pb(15), float(TURN))
-    fill(A("lu", 0, 18), 2)
-    ts(A("lu", 8, 16), A("c16", 0, 8), pb(1), 1.0, AL.mult, AL.add)
-    ts(A("lu", 18, 27), A("c16", 0, 9), pb(1), None, AL.mult)
-    ts(A("lu", 27, 36), A("c16", 0, 9), pb(6), None, AL.mult)
+    part("load")
+    dma([(A("xin", 0, 1152), hbm("x", every))], "Y")
+    dma([(A("uin", 0, 512), hbm("u", every))], "S")
+    part("loadn")
+    dma([(A("m0", 32 * c, 32 * c + 32, 1, 0, 9), hbm("nb", (c, every))) for c in range(4)]
+        + [(A("m0", 128 + 32 * c, 160 + 32 * c, 1, 0, 9), hbm("e", (c, every))) for c in range(4)])
+    part("loadw")
+    dma([(cast(A("wq", 0, 512), 8), hbm("wc", every)), (A("wsc", 0, 512), hbm("ws", every))])
+    part("loadv")
+    dma([(A("vin", 0, 512), hbm("v", every))])
+    part("pb")
+    for k in range(3):
+        iota(A("pi", k, k + 1), [[1, 1]], 0, 1 << k, False)
+    ts(A("pi", 3, 6), A("pi", 0, 3), 15, None, AL.bitwise_and)
+    copy(A("pb", 0, 6), A("pi", 0, 6))
+    P, Q16, Q8X2, Q4X4, G16, G, B3X8, B2X8, B3 = pb(0), pb(3), pb(4), pb(5), pb(6), pb(7), pb(23), pb(24), pb(25)
+    part("pb2")
+    lin(G16, Q16, -1.0, P)
+    lin(G, G16, 0.0625, 0.0)
+    lin(B3X8, Q8X2, -0.5, Q16)
+    lin(B2X8, Q4X4, -0.5, Q8X2)
+    part("fill")
+    fill(A("zb", 0, 576), 0.0)
+    fill(A("ones", 0, 512), 1.0)
+    fill(A("lu", 0, 10), 2)
+    part("blank0")
+    zero(A("ft", 2, 1152, 4, 0, 96))
+    zero(A("oh", 0, 512))
+    zero(A("dig", 3, 1024, 4))
+    zero(A("dig", 2, 1024, 4, 0, 96))
+    part("lu")
+    lin(pb(22), Q8X2, 8.0, 1.0)
+    ts(A("lu", 10, 18), A("ones", 0, 8), pb(22), None, AL.mult)
+    ts(A("lu", 18, 27), A("ones", 0, 9), Q8X2, 8.0, AL.mult, AL.mult)
+    part("qu")
     quant(UQ, 0, 128, A("uin", 0, 512))
-    quant(XQ[0], 0, C, A("xin", 0, 1152))
-    pick(UP, 0, UQ, 128, A("lu", 0, 17))
-    pick(UP, 272, UQ, 128, A("lu", 18, 36))
-    fill(A("tri", 256, 288), BIG)
-    where(A("tri", 0, 256), A("zb", 0, 256), [[0, 2], [1, 128]], AL.is_ge, BIG, 0, -1)
-    where(A("tri", 256, 288, 1, 96, 128), A("zb", 0, 32, 1, 96, 128), [[1, 32]], AL.is_ge, BIG, 0, -1)
-    quant(CQ, 0, 128, A("ones", 0, 512))
-    for c0 in (0, 384, 768):
-        blank("ft", c0, c0 + 384, 96)
-    ts(A("mj", 0, 32), A("mi", 0, 32), 15, None, AL.bitwise_and)
-    ts(A("ma", 0, 32), A("mj", 0, 32), 0.0, 8192.0, AL.is_equal, AL.mult)
-    ts(A("mb", 0, 32), A("mj", 0, 32), 1.0, -4096.0, AL.is_equal, AL.mult)
+    quant(XQ, PRE, C, A("xin", 0, 1152))
+    pick(UP, U_ORD, UQ, 128, A("lu", 0, 9))
+    part("qu2")
+    pick(UP, U_FRM, UQ, 128, A("lu", 10, 18))
+    again(UP, U_FRM + 128, UP, U_FRM, 128)
+    part("qu3")
+    pick(UP, U_MRK, UQ, 128, A("lu", 18, 27))
+    again(UP, U_MRK + 144, UP, U_MRK + 1, 136)
+    part("pre")
+    again(XQ, 0, XQ, PRE, PRE)
+    part("pre2")
+    again(BQ, 0, XQ, PRE, PRE)
+    part("tri")
+    where(A("tri", 0, 128), A("zb", 0, 128), [[1, 128]], AL.is_ge, BIG, 0, -1)
+    fill(A("th", 256, 288, 1, 0, 96), BIG)
+    quant(CQ, C_ONE, 128, A("ones", 0, 512))
+    part("etile")
+    where(A("ebig", 0, 512), A("ones", 0, 512), [[-1, 512]], AL.is_equal, 0.0, 3, 4)
+    copy(A("ebig", 512, 4 * EW + 8), A("ebig", 0, 4 * EW + 8 - 512), "VS")
+    for b in range(4):
+        quant(EQ, EW * b, EW, A("ebig", 3 - b, 4 * EW + 3 - b))
+    part("dig")
+    iota(A("nrow", 0, H), [[1, H]], 1, 0)
+    lin(pb(17), G16, 1.0, 128.0)
+    lin(pb(18), G16, 2.0, 64.0)
+    lin(pb(19), G16, -1.0, 96.0)
+    lin(pb(20), pb(19), 1.0, Q16)
+    for at, col, q0 in ((0, 6, 0), (1, 17, 0), (2, 18, 96), (512, 3, 0), (513, 3, 0), (514, 20, 96)):
+        copy(A("dig", at, at - at % 4 + 512, 4, q0, 128), A("ones", 0, 128, 1, q0, 128), "VS", pb(col, q0))
+    quant(CQ, C_HI, 256, A("dig", 0, 1024))
+    part("rw")
+    iota(A("qrow", 0, 144), [[0, 9], [1, 16]], 0, 0)
+    lin(pb(21), Q16, 1.0, 1.0)
+    ts(A("ma", 0, 32), A("qrow", 0, 32), Q16, CAP, AL.is_equal, AL.mult)
+    ts(A("mb", 0, 32), A("qrow", 0, 32), pb(21), -HOLD, AL.is_equal, AL.mult)
     tt(A("rw", 0, 32), A("ma", 0, 32), A("mb", 0, 32), AL.add)
     copy(A("rw", 32, 64), A("rw", 0, 32), "VS")
-    copy(A("rw", 256, 288), A("rw", 0, 32), "VS")
-    copy(A("rw", 64, 128), A("rw", 0, 64), "VS")
-    copy(A("rw", 128, 256), A("rw", 0, 128), "VS")
-    ts(pb(13), pb(0), 15.0, 4096.0, AL.not_equal, AL.mult)
-    ts(pb(14), pb(13), -1.0, None, AL.add)
-    iota(A("iot", 0, 288), [[1, 288]], 0, 0, True)
-    where(A("ebig", 0, 512), A("ones", 0, 512), [[-1, 512]], AL.is_equal, 0.0, 3, 4)
-    copy(A("ebig", 512, 1024), A("ebig", 0, 512), "VS")
-    for b in range(4):
-        quant(EQ, 240 * b, 240, A("ebig", 3 - b, 963 - b))
-    for c0, c1 in ((0, 512), (512, 1032), (1032, 1552)):
-        blank("sel", c0, c1)
-    s_sum, s_a, s_c = A("sel", 0, 512, 4), A("sel", 516, 1028, 8), A("sel", 1036, 1548, 8)
-    where(s_sum, A("ones", 0, 128), [[-16, 8], [0, 16]], AL.is_ge, 0.0, 0, 1)
-    where(s_sum, s_sum, [[16, 8], [0, 16]], AL.is_ge, 0.0, 15, -1)
-    where(s_a, A("ones", 0, 64), [[0, 8], [-16, 8]], AL.is_ge, 0.0, 0, 1)
-    where(s_a, s_a, [[0, 8], [16, 8]], AL.is_ge, 0.0, 15, -1)
-    where(s_c, A("ones", 0, 64), [[-1, 8], [-16, 8]], AL.is_equal, 0.0, 0, 1)
-    for k, c0 in enumerate((0, 516, 512, 1036, 1032)):
-        quant(CQ, 128 * (k + 1), 128, A("sel", c0, c0 + 512))
-    fill(A("rf", 0, 64), 0.0)
-    blank("rc", 0, 144)
-    fill(A("rf", 0, 64, 16), -BIG)
+    copy(A("rw", 64, 96), A("rw", 0, 32), "VS")
+    copy(A("rw", 96, 144), A("rw", 0, 48), "VS")
+    ts(pb(13), Q16, 15.0, HOLD, AL.not_equal, AL.mult)
+    part("rf")
+    blank([("rf", 0, 192), ("ff", 0, 256), ("fg", 0, 256), ("rc", 0, 144)])
+    fill(A("rf", 0, 192, 8), -BIG)
+    part("sel")
+    blank([("sel", 0, 512), ("sel", 512, 1056), ("sel", 1056, 1600), ("sel", 1600, 2176)])
+    iota(A("grow", 0, 128), [[1, 8], [0, 16]], 0, 0)
+    ts(A("sel", 0, 512, 4), A("grow", 0, 128), G, MT / 2.0, AL.is_equal, AL.mult)
+    copy(A("sel", 1, 512, 4), A("sel", 0, 512, 4), "VS", -1.0)
+    ts(A("sel", 512, 1056, 4), A("qrow", 8, 144), G, 0.5, AL.is_equal, AL.mult)
+    copy(A("sel", 513, 1056, 4), A("sel", 512, 1056, 4), "VS", -1.0)
+    copy(A("sel", 1057, 1600, 4), A("sel", 512, 1056, 4), "VS", float(TURN))
+    where(A("sel", 1600, 2176, 4), A("ones", 0, 144), [[-1, 9], [-16, 16]], AL.is_equal, 0.0, -7, 1)
+    quant(CQ, C_SUM, 264, A("sel", 0, 1056))
+    quant(CQ, C_OWN, 280, A("sel", 1056, 2176))
+    part("blank")
     fill(A("rc", 0, 144, 4), -BIG)
-    for a in (A("mm", 0, 8), A("offa", 0, 1), A("vv", 0, 160), A("oe1", 0, 128, 1, 0, 32)):
-        zero(a)
-    for name, c0, c1 in (("ff", 0, 256), ("fg", 0, 256), ("fa", 0, 304), ("fa", 304, 600)):
-        blank(name, c0, c1)
-    for u0, u1 in ((1, 3), (5, 6), (32, 33), (35, 37)):
-        blank("vw", OWN + H * u0, OWN + H * u1)
-    lin(pb(8), pb(3), 16.0, pb(4))
-    lin(pb(9), pb(5), 2.0, pb(8))
-    lin(pb(10), pb(2), 32.0, pb(9))
-    ts(pb(11), pb(3), 32.0, 32.0, AL.mult, AL.add)
-    lin(pb(12), pb(2), 64.0, pb(11))
-    ts(A("lown", 0, 9), A("iot", 0, 288, 32), pb(9), None, AL.add)
-    ts(A("l12", 0, 2), A("iot", 0, 4, 2), pb(10), None, AL.add)
-    ts(A("l12", 2, 18, 2), A("iot", 0, 128, 16), pb(0), None, AL.add)
-    ts(A("l12", 3, 18, 2), A("iot", 0, 128, 16), pb(0), None, AL.add)
-    ts(A("l3", 0, 9), A("iot", 0, 9), pb(12), None, AL.add)
-    lin(A("idx", 0, 18), A("iot", 0, 288, 16), 1.0, pb(0))
-    ts(A("m1", 0, 128, 1, 0, 9), A("m0", 0, 128, 1, 0, 9), 8.0, None, AL.mult)
-    tt(A("vv", 0, 128, 1, 0, 9), A("m1", 0, 128, 1, 0, 9), A("m0", 128, 256, 1, 0, 9), AL.add)
-    for k in (32, 64, 96):
-        dma(A("vv", 0, 128, 1, k, k + 9), A("vv", 0, 128, 1, 0, 9))
-    copy(A("vg", 0, 288), ind(A("vv", 0, 160), A("l12", 0, 18)), "VS")
-    turn(A("vt", 0, 288), A("vg", 0, 288))
-    copy(A("vi", 0, 9), A("vt", 0, 9))
-    copy(A("vi", 16, 160), ind(A("vt", 0, 288), A("l3", 0, 9)))
-    ts(A("sb", 0, 9), A("vi", 0, 9), 7, None, AL.bitwise_and)
-    ts(A("sa", 0, 144), A("vi", 16, 160), 7, None, AL.bitwise_and)
-    tt(A("nb8b", 0, 9), A("vi", 0, 9), A("sb", 0, 9), AL.subtract)
-    ts(A("aa", 0, 144), A("vi", 16, 160), 3, None, AL.logical_shift_right)
-    ts(A("dl", 0, 144), A("aa", 0, 144), float(C), None, AL.is_ge)
-    copy(A("offs", 0, 144), A("dl", 0, 144), "VS", float(OWN - C))
-    tt(A("nbm", 0, 144), A("offs", 0, 144), A("aa", 0, 144), AL.add)
-    lin(A("mul", 0, 144), A("dl", 0, 144), float(FAR - TURN), pb(15))
-    ts(A("nbi", 0, 9), A("vi", 0, 9), 3, None, AL.logical_shift_right)
+    zero(A("zf", 0, 160))
+    blank([("fa", 0, 400), ("fa", 400, 800)])
+    dma([(A("vv", 0, 160), A("zf", 0, 160))])
+    dma([(A("mm", 0, 8), A("zf", 0, 8)), (A("offa", 0, 4), A("zf", 0, 4)), (A("oe1", 0, 128, 1, 0, 32), A("zf", 0, 128, 1, 0, 32))])
+    part("gaps")
+    for r in range(7):
+        iota(A("mk", MT * r + E, MT * r + MT), [[0, MT - E]], 0, 0)
+    part("lists")
+    iota(A("iot", 0, 32), [[1, 32]], 0, 0)
+    iota(A("lrow", 0, 4), [[8, 2], [1, 2]], 0, 0)
+    iota(A("lrow", 4, 20), [[16, 2], [32, 4], [0, 2]], 0, 0)
+    iota(A("idx", 0, 18), [[FAR, 3], [16, 6]], 0, 0)
+    lin(A("idx", 0, 18), A("idx", 0, 18), 1.0, Q16)
+    lin(pb(8), B2X8, 2.0, G)
+    lin(pb(9), Q4X4, 8.0, pb(8))
+    lin(pb(10), B2X8, 16.0, 64.0)
+    lin(pb(11), Q4X4, 8.0, pb(10))
+    lin(pb(12), B3X8, 0.125, pb(11))
+    lin(pb(14), B3X8, -0.125, 1.0)
+    lin(B3, B3X8, 0.125, 0.0)
+    lin(pb(15), B3X8, 4.0, 0.0)
+    ts(A("l12", 0, 4), A("lrow", 0, 4), pb(9), None, AL.add)
+    ts(A("l12", 4, 20), A("lrow", 4, 20), Q16, None, AL.add)
+    ts(A("l3", 0, 5), A("iot", 0, 5), 2.0, pb(12), AL.mult, AL.add)
+    lin(A("ta", 0, 9), A("iot", 0, 9), 64.0, pb(15))
+    ts(A("tb", 0, 9), A("ta", 0, 9), float(C), 8.0 - C, AL.is_ge, AL.mult)
+    tt(A("tb", 0, 9), A("ta", 0, 9), A("tb", 0, 9), AL.add)
+    ts(A("lown", 0, 9), A("tb", 0, 9), pb(8), None, AL.add)
+    part("edges")
+    ts(A("m1", 0, 128, 1, 0, 9), A("m0", 128, 256, 1, 0, 9), float(MT), None, AL.mult)
+    tt(A("vv", 0, 128, 1, 0, 9), A("m1", 0, 128, 1, 0, 9), A("m0", 0, 128, 1, 0, 9), AL.add)
+    dma([(A("vv", 0, 128, 1, k, k + 9), A("vv", 0, 128, 1, 0, 9)) for k in (32, 64, 96)])
+    copy(A("vg", 0, 320), ind(A("vv", 0, 160), A("l12", 0, 20)), "VS")
+    turn(A("vt", 0, 320), A("vg", 0, 320))
+    part("edgeb")
+    copy(A("c18", 0, 9), A("vt", 0, 9), "VS")
+    copy(A("c18", 9, 18), A("vt", 32, 41), "VS")
+    copy(A("tc", 0, 9), A("c18", 0, 18, 2), "VS", pb(14))
+    copy(A("td", 0, 9), A("c18", 1, 18, 2), "VS", B3)
+    tt(A("vb", 0, 9), A("tc", 0, 9), A("td", 0, 9), AL.add)
+    ts(A("nbi", 0, 9), A("vb", 0, 9), MT - 1, None, AL.bitwise_and)
     copy(A("lnb", 0, 9), A("nbi", 0, 9))
+    part("edgea")
+    copy(A("vi", 0, 80), ind(A("vt", 0, 320), A("l3", 0, 5)))
+    ts(A("sa", 0, 72), A("vi", 0, 72), 9, None, AL.logical_shift_right)
+    ts(A("aa", 0, 72), A("vi", 0, 72), MT - 1, None, AL.bitwise_and)
+    ts(A("dl", 0, 72), A("aa", 0, 72), float(C), None, AL.is_ge)
+    lin(A("mul", 0, 72), A("dl", 0, 72), float(FAR - TURN), float(TURN))
+    ts(A("zz", 0, 72), A("aa", 0, 72), float(H), float(C), AL.is_ge, AL.mult)
+    ts(A("saf", 0, 72), A("aa", 0, 72), float(2 * H), float(C), AL.is_ge, AL.mult)
+    copy(A("offs", 0, 72), A("dl", 0, 72), "VS", float(OWN - 3 * C))
+    tt(A("nbm", 0, 72), A("zz", 0, 72), A("aa", 0, 72), AL.add)
+    tt(A("offs", 0, 72), A("offs", 0, 72), A("saf", 0, 72), AL.add)
+    tt(A("nbm", 0, 72), A("nbm", 0, 72), A("offs", 0, 72), AL.add)
+    part("qv")
     quant(VQ, 0, 128, A("vin", 0, 512))
 
     turns = [0]
 
-    def stream(st, s0, mv, n, c1, out, scale):
-        k = 5 + turns[0] % 3
+    def stream():
         turns[0] += 1
-        mm(k, st, s0, mv, 0, n)
-        copy(out, bank(k, 0, c1), "VS", scale)
+        return 5 + turns[0] % 3
 
-    def frames(to, ks, ff, gq, at):
+    def unpack(mv, end, r, at):
+        for m in range(2):
+            k = stream()
+            mm(k, EQ, EW * (2 * m + 1) + 16 * r, mv, end - 128 - H, 128 + H)
+            mm(k, EQ, EW * 2 * m + 16 * r, mv, end - 128, 128)
+            copy(A("vw", at + 2 * H * m, at + 2 * H * m + 2 * H), bank(k, 128 - H, 128 + H), "VS", 0.5)
+
+    def spread(at, width, made, issued, early):
+        for n, to in enumerate(range(made, 8, made)):
+            cut, w = 16 * to, width * made
+            dma([(A("vw", at + width * to, at + width * to + w, 1, 0, 128 - cut), A("vw", at, at + w, 1, cut, 128)),
+                 (A("vw", at + width * to, at + width * to + w, 1, 128 - cut, 128), A("vw", at, at + w, 1, 0, cut))],
+                "Y", None if n < early else issued)
+
+    def frames(to, k, src, x0, ff, gq, at):
+        for w, c0 in ((2, 160), (1, 128), (0, 0)):
+            mm(k, src, x0 + c0, UP, U_FRM, 128 + 64 * w)
+        scan(A("pm", at, at + 192), A("rf", 0, 192), bank(k, 64, 256), AL.add, AL.max)
         for w in range(3):
             a = at + 64 * w
-            scan(A("pm", a, a + 64), A("rf", 0, 64), bank(ks[w], 0, 64), AL.add, AL.max)
-            tt(A(ff, w, 224, 4), A("pm", a, a + 56), A("pm", a + 8, a + 64), AL.is_lt)
+            ts(A(ff, w, 256, 4), A("pm", a, a + 64), A("pm", a + 7, a + 8), None, AL.is_lt)
         copy(A(ff, 256, 512), A(ff, 0, 256), "VS")
         quant(gq, 0, 128, A(ff, 0, 512))
-        for w in range(3):
-            mm(ks[w], gq, 0, EQ, 240 * w, 128)
-        copy(A(to, 0, 128), bank(ks[0], 0, 128), "VS")
-        copy(A(to, 128, 256), bank(ks[1], 0, 128), "VS")
-        copy(A(to, 256, 288), bank(ks[2], 96, 128), "VS")
+        for w, n in ((2, C), (1, 256), (0, 128)):
+            mm(k, gq, 0, EQ, EW * w + 128 - n, n)
+        copy(A(to, 0, C), bank(k, 0, C), "VS")
 
-    def counted(window, lst):
-        copy(A("fa", 0, 576, 4), ind(window, lst), "VS")
-        quant(HQ, 0, 150, A("fa", 0, 600))
-        mm(1, CQ, 128, HQ, 0, 144)
-        mm(2, CQ, 256, HQ, 0, 144, True, False)
-        mm(2, CQ, 384, HQ, 4, 144, False, True)
-        scan(A("kb", 0, 144), A("rw", 0, 144), bank(1, 0, 144), AL.add, AL.min)
+    def halves(k, tile, mv):
+        mm(k, CQ, tile + 8, mv, 0, 128, True, False)
+        mm(k, CQ, tile, mv, 72, 128, False, True)
 
     def mark_at(r):
-        return 272 + r if r % 2 == 0 else 416 + r - 1
+        return U_MRK + r if r % 2 == 0 else U_MRK + 144 + r - 1
 
+    blocks = (0, 128, 160)
     for t in range(3):
-        X, L, FX = XQ[t], ("bq%d" % t, "bs%d" % t), ("fxq%d" % t, "fxs%d" % t)
-        send(t, 0, 800.0, [A(X[0], 0, C), A(X[1], 0, C)])
-        mm(0, UP, 0, X, 0, C)
-        for w, c0 in enumerate((0, 128, 160)):
-            mm(1 + w, X, c0, UP, 128, 130)
-            copy(A("pc", w, w + 1), bank(1 + w, 128, 129), "S")
-        for w, (c0, c1) in enumerate(((0, 128), (128, 256), (256, 288))):
-            act(A("th", c0, c1), A("tri", c0, c1), AF.Identity, A("pc", w, w + 1))
+        x0, b1, FX = PRE + C * t, PRE + H * (t + 1), ("fxq%d" % t, "fxs%d" % t)
+        part("sendx")
+        send(t, 0, 800.0, [A("xq", x0, x0 + C), A("xs", x0, x0 + C)], 1200.0)
+        part("sort")
+        for w, c0 in enumerate(blocks):
+            mm(1 + w, XQ, x0 + c0, UP, U_ORD, 128)
+            copy(A("pc", w, w + 1), bank(1 + w, 0, 1), "S")
+        mm(0, UP, U_ORD, XQ, x0, C)
         ts(A("ft", 0, 512, 4), bank(0, 0, 128), A("pc", 0, 1), None, AL.is_lt)
         ts(A("ft", 512, 1152, 4), bank(0, 128, 288), A("pc", 0, 1), None, AL.is_le)
         ts(A("ft", 1, 1024, 4), bank(0, 0, 256), A("pc", 1, 2), None, AL.is_lt)
         ts(A("ft", 1025, 1152, 4), bank(0, 256, 288), A("pc", 1, 2), None, AL.is_le)
+        part("ties")
+        act(A("th", 0, 128), A("tri", 0, 128), AF.Identity, A("pc", 0, 1))
+        act(A("th", 128, 256), A("tri", 0, 128), AF.Identity, A("pc", 1, 2))
+        act(A("th", 256, 288, 1, 96, 128), A("tri", 96, 128, 1, 96, 128), AF.Identity, A("pc", 2, 3, 1, 96, 128))
         ts(A("ft", 2, 1152, 4, 96, 128), bank(0, 0, 288, 1, 96, 128), A("pc", 2, 3, 1, 96, 128), None, AL.is_lt)
+        part("sort")
         tt(A("ft", 3, 1152, 4), bank(0, 0, 288), A("th", 0, 288), AL.is_equal)
         quant(FQ, 0, C, A("ft", 0, 1152))
-        mm(0, CQ, 0, FQ, 0, C)
-        scan(A("w1", 0, 288), A("rw", 0, 288), bank(0, 0, 288), AL.add, AL.min)
-        ts(A("o1", 0, 18), A("w1", 15, 288, 16), pb(14), None, AL.add)
-        copy(ind(A("lst", 0, 288), A("o1", 0, 18)), A("iot", 0, 288))
-        scan(A("w2", 0, 128), A("rw", 0, 128), A("lst", 0, 128), AL.add, AL.min)
-        ts(A("sl%d" % t, 0, 8), A("w2", 15, 128, 16), pb(13), None, AL.add)
-        send(t, 1, 400.0, [A("sl%d" % t, 0, 8)])
+        for w, c0 in enumerate(blocks):
+            mm(1 + w, FQ, c0, CQ, C_ONE, 128)
+            ts(A("oh", w, 4 * H, 4), A("nrow", 0, H), bank(1 + w, 0, 1), None, AL.is_equal)
+        quant(NQ, 0, 128, A("oh", 0, 512))
+        mm(0, CQ, C_HI, NQ, 0, 128, True, False)
+        mm(0, CQ, C_LO, NQ, 0, 128, False, True)
+        scan(A("w2", 0, H), A("rw", 0, H), bank(0, 0, H), AL.add, AL.min)
+        ts(A("sl%d" % t, 0, 6), A("w2", 15, H, 16), pb(13), None, AL.add)
+        send(t, 1, 400.0, [A("sl%d" % t, 0, 6)], 300.0)
         issued = A("wire", 8 + t, 9 + t)
         land(t, 2, 100.0, [issued])
-        frames("fl", (1, 2, 3), "ff", GQ, 0)
-        counted(A("fl", 0, C), A("lown", 0, 9))
-        tt(A("baseb", 0, 9), A("sb", 0, 9), A("kb", 15, 144, 16), AL.subtract)
-        tt(A("basea", 0, 144), A("sa", 0, 144), bank(2, 0, 144), AL.subtract)
-        copy(A("oag", 0, 18), bank(2, 0, 144, 8), "VS", float(TURN))
-        tt(A("oaf", 0, 18), A("oag", 0, 18), A("idx", 0, 18), AL.add)
-        copy(A("oa", 0, 18), A("oaf", 0, 18))
-        step = min(MADE, 2)
+        part("vown")
         for r in range(MADE):
-            for b in range(4):
-                stream(EQ, 240 * b + 16 * r, X, C, C, A("vw", TURN * r + C * b, TURN * r + C * b + C), 0.5)
-            if r % step == step - 1:
-                r0 = r + 1 - step
-                for to in range(r0 + MADE, 8, MADE):
-                    c0, cut, w = TURN * r0, 16 * (to - r0), TURN * step
-                    dma(A("vw", TURN * to, TURN * to + w, 1, 0, 128 - cut), A("vw", c0, c0 + w, 1, cut, 128), "Y", DMA_T + 1500 * step, issued)
-                    dma(A("vw", TURN * to, TURN * to + w, 1, 128 - cut, 128), A("vw", c0, c0 + w, 1, 0, cut), "Y", DMA_T + 1500 * step, issued)
+            for c in range(3):
+                unpack(XQ, x0 + H * (c + 1), r, TURN * r + FAR * c)
+        part("down")
+        spread(0, TURN, MADE, issued, EARLY)
+        part("mown")
         for r in range(8):
-            stream(UP, mark_at(r), X, C, C, A("mk", r, 8 * C, 8), None)
+            k = stream()
+            mm(k, UP, mark_at(r), XQ, x0, C)
+            copy(A("mk", MT * r, MT * r + C), bank(k, 0, C), "VS")
+        part("fown")
+        frames("fl", 4, XQ, x0, "ff", GQ, 0)
+        part("kown")
+        copy(A("fa", 1, 577, 4), ind(A("fl", 0, C), A("lown", 0, 9)), "VS")
+        quant(KQ, 0, 200, A("fa", 0, 800))
+        halves(1, C_OWN, KQ)
+        tt(A("oaf", 0, 18), bank(1, 0, 72, 4), A("idx", 0, 18), AL.add)
+        copy(A("oa", 0, 18), A("oaf", 0, 18))
+        part("ah")
         for b in range(4):
-            copy(A("ah", C * b, C * b + C), ind(A("vw", C * b, OWN - C * (3 - b)), A("oa", 0, 18)), "VS")
-            copy(A("af", C * b, C * b + C), A("ah", C * b, C * b + C), "VS", 2.0)
+            copy(A("ah", C * b, C * b + C), ind(A("vw", H * b, OWN - H * (3 - b)), A("oa", 0, 18)), "VS")
+        part("af")
+        for b in (0, 2):
+            copy(A("af", C * b, C * b + 2 * C), A("ah", C * b, C * b + 2 * C), "VS", 2.0)
+        part("ffar")
         land(t, 0, WIRE_X, [A(FX[0], 0, C), A(FX[1], 0, C)])
-        for w, c0 in enumerate((0, 128, 160)):
-            mm((0, 4, 3)[w], FX, c0, UP, 128, 128)
-        frames("flx", (0, 4, 3), "fg", JQ, 192)
-        land(t, 1, WIRE_L, [A("ll%d" % t, 0, 8)])
+        frames("flx", 3, FX, 0, "fg", JQ, 192)
+        part("list")
+        land(t, 1, WIRE_L, [A("ll%d" % t, 0, 6)])
         copy(A("fl", C, E), ind(A("flx", 0, C), A("ll%d" % t, 0, 6)), "VS")
-        pick(L, 0, FX, C, A("ll%d" % t, 0, 8))
+        part("pick")
+        pick(BQ, b1 - H, FX, C, A("ll%d" % t, 0, 6))
+        part("vfar")
+        for r in range(MADEB):
+            unpack(BQ, b1, r, OWN + FAR * r)
+        part("dfar")
+        spread(OWN, FAR, MADEB, None, 8)
+        part("mfar")
         for r in range(8):
-            stream(UP, mark_at(r), L, 128, H, A("mk", 8 * C + r, 8 * E, 8), None)
-        counted(A("fl", 0, E), A("lnb", 0, 9))
-        tt(A("ab", 0, 9), A("kb", 15, 144, 16), A("baseb", 0, 9), AL.add)
-        ts(A("sb", 0, 9), A("ab", 0, 9), 7, None, AL.bitwise_and)
-        tt(A("obf", 0, 9), A("sb", 0, 9), A("nb8b", 0, 9), AL.add)
-        copy(A("ob", 0, 9), A("obf", 0, 9))
-        tt(A("aa", 0, 144), bank(2, 0, 144), A("basea", 0, 144), AL.add)
-        ts(A("sa", 0, 144), A("aa", 0, 144), 7, None, AL.bitwise_and)
-        tt(A("offs", 0, 144), A("sa", 0, 144), A("mul", 0, 144), AL.mult)
-        tt(A("offa", 1, 145), A("offs", 0, 144), A("nbm", 0, 144), AL.add)
-        tt(A("dl", 0, 144), A("offa", 0, 144), A("offa", 1, 145), AL.subtract)
-        for b in range(4):
-            for r in range(8):
-                at = OWN + FAR * r + C * b
-                stream(EQ, 240 * b + 16 * r, L, 128, H, A("vw", at, at + H), 0.5)
-        copy(A("mm", 8, 152), ind(A("mk", 0, 8 * E), A("ob", 0, 9)), "VS")
+            k = stream()
+            mm(k, UP, mark_at(r), BQ, b1 - 128, 128)
+            copy(A("mk", MT * r + C, MT * r + E), bank(k, 128 - H, 128), "VS")
+        part("knb")
+        copy(A("fa", 0, 576, 4), ind(A("fl", 0, E), A("lnb", 0, 9)), "VS")
+        quant(HQ, 0, 200, A("fa", 0, 800))
+        mm(1, CQ, C_SUM, HQ, 0, 144)
+        scan(A("kb", 0, 144), A("rw", 0, 144), bank(1, 0, 144), AL.add, AL.min)
+        tt(A("ab", 0, 9), A("kb", 15, 144, 16), A("vb", 0, 9), AL.add)
+        ts(A("vb", 0, 9), A("ab", 0, 9), 8 * MT - 1, None, AL.bitwise_and)
+        copy(A("ob", 0, 9), A("vb", 0, 9))
+        part("offs")
+        halves(2, C_CNT, HQ)
+        tt(A("aa", 0, 72), bank(2, 0, 72), A("sa", 0, 72), AL.add)
+        ts(A("sa", 0, 72), A("aa", 0, 72), 7, None, AL.bitwise_and)
+        tt(A("offs", 0, 72), A("sa", 0, 72), A("mul", 0, 72), AL.mult)
+        tt(A("offa", 1, 73), A("offs", 0, 72), A("nbm", 0, 72), AL.add)
+        tt(A("dl", 0, 72), A("offa", 0, 72), A("offa", 1, 73), AL.subtract)
+        part("choose")
+        copy(A("mm", 8, 152), ind(A("mk", 0, 7 * MT + E), A("ob", 0, 9)), "VS")
         scan(A("px", 0, 144), A("mm", 7, 151), A("rc", 0, 144), AL.max, AL.add)
         tt(A("fa", 0, 576, 4), A("mm", 8, 152), A("px", 0, 144), AL.is_le)
-        quant(HQ, 0, 150, A("fa", 0, 600))
-        mm(1, CQ, 512, HQ, 0, 144, True, False)
-        mm(1, CQ, 640, HQ, 4, 144, False, True)
-        scan(A("zz", 0, 144), A("dl", 0, 144), bank(1, 0, 144), AL.add, AL.mult)
-        tt(A("ocf", 0, 18), A("zz", 3, 144, 8), A("offa", 4, 145, 8), AL.add)
+        quant(KQ, 0, 200, A("fa", 0, 800))
+        halves(1, C_CHO, KQ)
+        scan(A("zz", 0, 72), A("dl", 0, 72), bank(1, 0, 72), AL.add, AL.mult)
+        tt(A("ocf", 0, 18), A("zz", 3, 72, 4), A("offa", 4, 73, 4), AL.add)
         copy(A("oz", 0, 18), A("ocf", 0, 18))
         runs = ((0, 160), (160, 288))
         for h, (c0, c1) in enumerate(runs):
+            part("z%d" % h)
             for b in range(4):
-                tt(A("zt", 4 * c0 + b, 4 * c1, 4), ind(A("vw", C * b, C * b + OWN + 29 * H), A("oz", c0 // 16, c1 // 16)),
+                tt(A("zt", 4 * c0 + b, 4 * c1, 4), ind(A("vw", H * b, OWN + 8 * FAR - H * (3 - b)), A("oz", c0 // 16, c1 // 16)),
                    A("ah", C * b + c0, C * b + c1), AL.add)
             quant(ZQ, c0, c1 - c0, A("zt", 4 * c0, 4 * c1))
+            part("r%d" % h)
             for b in range(4):
                 mm(4 * h + b, WQ, 128 * b, ZQ, c0, c1 - c0)
                 act(A("rr", C * b + c0, C * b + c1), bank(4 * h + b, 0, c1 - c0), AF.Relu, None, 0.03125)
         for h, (c0, c1) in enumerate(runs):
+            part("x%d" % h)
             for b in range(4):
                 tt(A("xt", 4 * c0 + b, 4 * c1, 4), A("rr", C * b + c0, C * b + c1), A("af", C * b + c0, C * b + c1), AL.add)
-            quant(XQ[t + 1], c0, c1 - c0, A("xt", 4 * c0, 4 * c1))
+            quant(XQ, x0 + C + c0, c1 - c0, A("xt", 4 * c0, 4 * c1))
+    part("oe")
+    x0 = PRE + 3 * C
+    copy(A("saf", 0, 72, 1, 0, 32), A("sa", 0, 72, 1, 0, 32))
     for c in range(4):
-        copy(A("oe1", 32 * c, 32 * c + 18, 1, 0, 32), A("sa", c, 144, 8, 0, 32))
+        copy(A("oe1", 32 * c, 32 * c + 18, 1, 0, 32), A("saf", c, 72, 4, 0, 32), "VS")
     turn(A("oe2", 0, 128, 1, 0, 32), A("oe1", 0, 128, 1, 0, 32))
-    for c in range(4):
-        dma(hbm("oe", (c, every)), A("oe2", 32 * c, 32 * c + 16, 1, 0, 18))
+    dma([(hbm("oe", (c, every)), A("oe2", 32 * c, 32 * c + 16, 1, 0, 18)) for c in range(4)])
     for h, (c0, c1) in enumerate(((0, 160), (160, 288))):
-        mm(h, VQ, 0, XQ[3], c0, c1 - c0)
+        part("out%d" % h)
+        mm(h, VQ, 0, XQ, x0 + c0, c1 - c0)
         copy(A("yo", c0, c1), bank(h, 0, c1 - c0), "VS")
-    dma(hbm("oc", every), cast(A("xq3", 0, C), 8))
-    for k in range(4):
-        dma(hbm("osc", (slice(4 * k, 4 * k + 4), every)), A("xs3", 0, C, 1, 32 * k, 32 * k + 4), "Y" if k % 2 else "S")
-    dma(hbm("y", every), A("yo", 0, C), "S")
+        dma([(hbm("y", (every, slice(c0, c1))), A("yo", c0, c1))], "S" if h else "Y")
+        dma([(hbm("oc", (every, slice(4 * c0, 4 * c1))), cast(A("xq", x0 + c0, x0 + c1), 8))], "Y")
+    dma([(hbm("osc", (slice(4 * k, 4 * k + 4), every)), A("xs", x0, x0 + C, 1, 32 * k, 32 * k + 4)) for k in range(4)], "Y")
     return ops
 
 
@@ -480,7 +580,7 @@ def _depends(ops):
             for j, m2, lo2, hi2, w2 in old:
                 if j != i and m & m2 and lo < hi2 and lo2 < hi:
                     if w or w2:
-                        deps[j] = deps.get(j, False) or not (op["acc"] and a[1] == "ps")
+                        deps[j] = deps.get(j, False) or not (a[1] == "ps" and w and w2)
                     elif a[1] == "ps":
                         deps.setdefault(j, False)
             if w:
@@ -489,22 +589,24 @@ def _depends(ops):
         op["deps"] = deps
 
 
-def _kind(op):
-    w = op["wr"][0] if op["wr"] else A("out", 0, 1)
-    name = w[1].rstrip("0123")
-    if name == "ps":
-        return "p" + op["rd"][2][1].rstrip("0123") + str(min(w[4] // 512, 5))
-    if name in ("vw", "mk"):
-        return name + str(w[4] >= (OWN if name == "vw" else 8 * C))
-    if name in ("zt", "xt", "rr"):
-        return name + str(w[4] % C > 0 if name == "rr" else w[4] >= 640)
-    return name + str(w[4]) + (op["rd"][0][1] + str(op["rd"][0][5]) if name == "fa" else "")
+def _gap(row, t, hold):
+    lo, hi = 0, len(row)
+    while lo < hi:
+        mid = (lo + hi) // 2
+        if row[mid][1] <= t:
+            lo = mid + 1
+        else:
+            hi = mid
+    while lo < len(row) and row[lo][0] < t + hold:
+        t = max(t, row[lo][1])
+        lo += 1
+    return t, lo
 
 
 def _place(ops, before, turn, spare):
     n = len(ops)
-    busy = {e: [] for e in "VSPGYN"}
-    done, eng = [0.0] * n, [None] * n
+    busy = {e: [] for e in "VSPGYND"}
+    done, eng, start = [0.0] * n, [None] * n, [0.0] * n
     for i in turn:
         op, best = ops[i], None
         for e, (cost, f) in op["how"].items():
@@ -513,35 +615,30 @@ def _place(ops, before, turn, spare):
                 d = done[j] + (HOP if hard or eng[j] != e else 0.0)
                 if d > t:
                     t = d
-            hold = 100.0 if op["tag"] == "dma" else 1.0 if e == "N" else cost
-            row = busy[e]
-            lo, hi = 0, len(row)
-            while lo < hi:
-                mid = (lo + hi) // 2
-                if row[mid][1] <= t:
-                    lo = mid + 1
-                else:
-                    hi = mid
-            while lo < len(row) and row[lo][0] < t + hold:
-                t = max(t, row[lo][1])
-                lo += 1
+            hold = 80.0 * op["calls"] if op["tag"] == "dma" else 1.0 if e == "N" else cost
+            t, lo = _gap(busy[e], t, hold)
+            t2 = t
+            if op["load"]:
+                while True:
+                    t2, ld = _gap(busy["D"], t, op["load"])
+                    if t2 == t or e != "Y":
+                        break
+                    t, lo = _gap(busy[e], t2, hold)
+                cost += t2 - t + (op["load"] if op["tag"] == "dma" else 0.0)
             worth = t + cost + (spare.get(op["kind"], 400.0) if e == "V" else 0.0)
             if best is None or worth < best[0]:
-                best = (worth, t, e, lo, hold, cost)
-        done[i], eng[i] = best[1] + best[5], best[2]
+                best = (worth, t, e, lo, hold, cost, t2)
+        done[i], eng[i], start[i] = best[1] + best[5], best[2], best[1]
         busy[best[2]].insert(best[3], (best[1], best[1] + best[4], i))
-    return max(done), done, eng, {e: [x[2] for x in busy[e]] for e in busy}
+        if op["load"]:
+            busy["D"].insert(_gap(busy["D"], best[6], op["load"])[1], (best[6], best[6] + op["load"], i))
+    return max(done), start, eng, {e: [x[2] for x in busy[e]] for e in busy}
 
 
 def _schedule():
     ops = _program()
     _depends(ops)
-    n, count = len(ops), {}
-    for op in ops:
-        op["kind"] = _kind(op)
-        if op["kind"] in ("hq0", "kb0"):
-            count[op["kind"]] = count.get(op["kind"], 0) + 1
-            op["kind"] += str(count[op["kind"]] % (3 if op["kind"] == "hq0" else 2))
+    n = len(ops)
     before = [list(op["deps"].items()) for op in ops]
     after = [[] for _ in range(n)]
     for i in range(n):
@@ -549,11 +646,10 @@ def _schedule():
             after[j].append(i)
     left = [0.0] * n
     for i in range(n - 1, -1, -1):
-        left[i] = min(c for c, f in ops[i]["how"].values()) + HOP + max([left[k] for k in after[i]] + [0.0])
+        left[i] = min(c for c, f in ops[i]["how"].values()) + ops[i]["load"] + HOP + max([left[k] for k in after[i]] + [0.0])
     kinds = sorted(set(op["kind"] for op in ops))
     free = sorted(set(op["kind"] for op in ops if len(op["how"]) > 1))
-    ahead = {"vwFalse": 2500, "ztFalse": 2000, "zq0": 4000, "rrFalse": 3000, "xtFalse": 500, "mm8": 2000, "jq0": 2500}
-    spare = {"vwTrue": 9000, "vwFalse": 3000, "mkTrue": 1500, "mm8": 9000, "af0": 9000, "af288": 9000, "af576": 9000, "af864": 9000}
+    ahead, spare = dict(AHEAD), dict(SPARE)
     seed, now, best = [12345], None, None
 
     def draw(row):
@@ -563,7 +659,7 @@ def _schedule():
     for trial in range(TRIES):
         a2, s2 = dict(ahead), dict(spare)
         for k in range(draw((1, 1, 2, 3)) if trial else 0):
-            if draw(range(5)) == 0:
+            if draw(range(4)) == 0:
                 s2[draw(free)] = draw((0, 100, 200, 400, 800, 1500, 3000, 9000))
             else:
                 name = draw(kinds)
@@ -575,12 +671,20 @@ def _schedule():
         if now is None or got[0] <= now + draw(range(150)) * (1.0 - trial / TRIES):
             now, ahead, spare = got[0], a2, s2
             if best is None or now < best[0]:
-                best = got
-    span, done, eng, order = best
+                best = got + (a2, s2)
+    span, start, eng, order = best[:4]
     for i, op in enumerate(ops):
-        op["eng"], op["at"] = eng[i], done[i] - op["how"][eng[i]][0]
+        op["eng"], op["at"] = eng[i], start[i]
+    pool = [i for i in order["G"] if ops[i]["tag"] is None]
+    for j, i in zip(pool, pool[1:]):
+        ops[i]["deps"][j] = True
+    for i in order["Y"]:
+        ended = [j for j in order["V"] if start[j] + ops[j]["how"]["V"][0] + HOP <= start[i]]
+        if ended:
+            ops[i]["deps"][ended[-1]] = True
     for op in ops:
         op["all"] = set(j for j, hard in op["deps"].items() if hard or ops[j]["eng"] != op["eng"])
+    for op in ops:
         inner = set(j for k in op["all"] if ops[k]["eng"] != "N" for j in ops[k]["all"])
         op["waits"] = [j for j in sorted(op["all"]) if j not in inner]
     wanted = set(j for op in ops for j in op["waits"])
@@ -590,17 +694,24 @@ def _schedule():
         for i in order[e]:
             op = ops[i]
             if op["tag"] == "dma":
-                op["sig"] = ("d%d" % i, 16)
+                op["sig"] = ("d%d" % i, 16 * op["calls"])
                 names.append("d%d" % i)
             elif op["tag"] is None and i in wanted:
                 k += 1
                 op["sig"] = ("on" + e, k)
             else:
                 op["sig"] = None
-    return ops, order, names, span
+    return ops, order, names, span, best[4:]
 
 
-OPS, ORDER, _DMA_SEMS, SPAN = _schedule()
+AHEAD = {"load": 2000, "sort": -500, "ties": 200, "etile": 6700, "loadv": -2000, "dfar": 500, "pb": 6500, "edges": 700, "blank0": -4500,
+         "x0": -2800, "oe": 2200, "lists": -200, "rw": 2200, "pre": 500, "offs": 500, "rf": 5800, "qu2": 2500, "z0": 1700, "qv": 2000,
+         "af": -1000, "sel": 200, "fill": -200, "x1": -3900, "pre2": 3200, "edgea": 2300, "list": -4000}
+SPARE = {"vown": 200, "mown": 3000, "ah": 3000, "vfar": 0, "mfar": 0, "rw": 9000, "sel": 800, "pb2": 1500, "edgea": 800, "qu": 3000,
+         "out0": 0, "lu": 800, "qu3": 3000, "dig": 9000, "oe": 200, "af": 100, "out1": 0, "blank": 400, "lists": 9000, "pick": 3000,
+         "knb": 1500, "edgeb": 200, "etile": 100, "fown": 0, "kown": 9000, "blank0": 1500, "choose": 9000, "edges": 3000, "qu2": 0,
+         "ffar": 100, "list": 400}
+OPS, ORDER, _DMA_SEMS, SPAN, FOUND = _schedule()
 SEMAPHORES = ["onV", "onS", "onP", "onG", "left", "issued"] + [k % t for t in range(3) for k in ("arrx%d", "arrl%d", "rela%d", "relb%d")] + _DMA_SEMS
 
 
@@ -648,7 +759,7 @@ def _hand_on(g, core, T, topo):
             if k == 0:
                 g.remote_dma(T["fxs%d" % t][:, 0:C], T["rs%d" % t][:, 0:C], T.sem["arrx%d" % t], T.sem.left, pid, rid, topo.mask(core, dst))
             else:
-                g.remote_dma(T["ll%d" % t][:, 0:8], T["rl%d" % t][:, 0:8], T.sem["arrl%d" % t], T.sem.left, pid, rid, topo.mask(core, dst))
+                g.remote_dma(T["ll%d" % t][:, 0:6], T["rl%d" % t][:, 0:6], T.sem["arrl%d" % t], T.sem.left, pid, rid, topo.mask(core, dst))
             sent += 2 * len(topo.engines(core, dst))
     if sent:
         g.wait_ge(T.sem.left, sent)
@@ -659,11 +770,11 @@ def _send(g, core, T, topo, dst, t, kind):
     first = via[kind] if via else dst
     rid, pid = topo.addr(first, core)
     eng = topo.engines(core, first)
+    x0 = PRE + C * t
     if kind:
         out, sem = (T["rl%d" % t], T.sem["relb%d" % t]) if via else (T["ll%d" % t], T.sem["arrl%d" % t])
-        g.remote_dma(out[:, 0:8], T["sl%d" % t][:, 0:8], sem, T.sem.left, pid, rid, _bits(eng))
-        if MADE < 8:
-            g.sem_inc(T.sem.issued, 1)
+        g.remote_dma(out[:, 0:6], T["sl%d" % t][:, 0:6], sem, T.sem.left, pid, rid, _bits(eng))
+        g.sem_inc(T.sem.issued, 1)
         return len(eng)
     half, parts = len(eng) // 2, []
     for k in range(2):
@@ -671,10 +782,10 @@ def _send(g, core, T, topo, dst, t, kind):
         out = _codes(T, "rq%d" % t, 0, C // 2) if via else _codes(T, "fxq%d" % t, k * C // 2, (k + 1) * C // 2)
         parts.append(RemoteDMATransfer(dst_ids=[DstId(rid=r2, pnc=p2)], dma_engine_mask=_bits(eng[k * half:(k + 1) * half]),
                                        remote_sem=T.sem[("rela%d" if via else "arrx%d") % t],
-                                       src=_codes(T, "xq%d" % t, k * C // 2, (k + 1) * C // 2), dst=out))
+                                       src=_codes(T, "xq", x0 + k * C // 2, x0 + (k + 1) * C // 2), dst=out))
     g.remote_dma_fused(parts, local_sem=T.sem.left)
     out, sem = (T["rs%d" % t], T.sem["relb%d" % t]) if via else (T["fxs%d" % t], T.sem["arrx%d" % t])
-    g.remote_dma(out[:, 0:C], T["xs%d" % t][:, 0:C], sem, T.sem.left, pid, rid, _bits(eng))
+    g.remote_dma(out[:, 0:C], T["xs"][:, x0:x0 + C], sem, T.sem.left, pid, rid, _bits(eng))
     return 2 * len(eng)
 
 
@@ -686,7 +797,7 @@ def rank_program(g, core, T, topo):
     n = len(T.cores)
     queues = {"V": g.vector, "S": g.scalar, "P": g.tensor, "G": g, "Y": g.sync}
     R = lambda a: _real(T, a)
-    top, waited, sent = {}, {}, 0
+    top, waited, sent = {"issued": len(STEP)}, {}, 0
     for e in "YSVPG":
         q, have = queues[e], {}
         for i in ORDER[e]:
@@ -713,7 +824,8 @@ def rank_program(g, core, T, topo):
             call = op["how"][e][1](q, R)
             if op["sig"] is not None:
                 name, k = op["sig"]
-                call.then_inc(T.sem[name], 16 if op["tag"] == "dma" else 1)
+                for one in (call if op["tag"] == "dma" else [call]):
+                    one.then_inc(T.sem[name], 16 if op["tag"] == "dma" else 1)
                 top[name] = k
     g.wait_ge(T.sem.left, sent)
     for name, k in top.items():

@@ -7,12 +7,16 @@ BIG = 1.0e29
 PRE = 128
 TURN, OWN, FAR = 4 * C, 32 * C, 4 * H
 MT = 512
-MADE, MADEB, EARLY = 1, 2, 2
-EW = 128 + 16 * (max(MADE, MADEB) - 1)
-CAP, HOLD = 65536.0, 16384.0
-TRIES = 1
-CYC, PEC, FIX, HOP, DMA_T, WIRE_X, WIRE_L = 1.0, 0.6, 60.0, 120.0, 1700.0, 5000.0, 3500.0
-ROW, RATE = 25.0, 25.0
+MADEB, EARLY = 2, 1
+HEAD = ("VVSVVV", "VSSVVV", "VSSVVV")
+MCOPY = 0
+EW = 128 + 16 * (MADEB - 1)
+CAP, HOLD, ROUND = 65536.0, 16384.0, 12582912.0
+TRIES, MOVES, HEAT = 1, 55000, 40
+SLACK, PULL = 120.0, 0.5
+CUT = 160
+CYC, PEC, FIX, HOP, DMA_T, ROW, RATE = 1.0, 0.6, 60.0, 120.0, 1700.0, 24.0, 26.0
+WIRE_X, WIRE_L = (5000.0, 4000.0, 2800.0), (3500.0, 3500.0, 2000.0)
 F32, BF, I32, U16, X4, U8 = "float32", "bfloat16", "int32", "uint16", "float8_e4m3fn_x4", "uint8"
 SIZE = {F32: 4, BF: 2, I32: 4, U16: 2, X4: 4, U8: 1}
 
@@ -24,24 +28,25 @@ for _n, _c, _d in [
     ("fq", 288, X4), ("fs", 288, U8), ("gq", 128, X4), ("gs", 128, U8), ("jq", 128, X4), ("js", 128, U8),
     ("nq", 128, X4), ("ns", 128, U8), ("hq", 200, X4), ("hs", 200, U8), ("kq", 200, X4), ("ks", 200, U8),
     ("zq", 288, X4), ("zs", 288, U8), ("xq", PRE + 4 * C, X4), ("xs", PRE + 4 * C, U8), ("bq", PRE + 3 * H, X4), ("bs", PRE + 3 * H, U8),
-    ("ones", 512, BF), ("ebig", 4 * EW + 8, BF), ("dig", 1024, BF), ("sel", 2176, BF), ("tri", 128, BF), ("zb", 576, BF), ("zf", 160, F32),
-    ("rw", 144, BF), ("rf", 192, BF), ("rc", 144, BF), ("qrow", 144, BF), ("grow", 128, BF), ("nrow", 96, BF), ("iot", 32, F32),
+    ("ones", 512, BF), ("ebig", 4 * EW + 8, BF), ("dig", 1024, BF), ("sel", 2176, BF), ("tri", 128, BF), ("zb", 576, BF),
+    ("rw", 144, BF), ("rf", 192, BF), ("rc", 144, BF), ("qrow", 144, BF), ("grow", 128, BF), ("nrow", 96, BF),
     ("ci", 96, I32), ("cf", 320, F32), ("pb", 32, F32),
-    ("lu", 28, U16), ("l12", 20, U16), ("l3", 6, U16), ("lown", 10, U16), ("lnb", 10, U16),
+    ("lu", 28, U16), ("lfix", 36, U16), ("lnb", 10, U16),
     ("m0", 256, I32), ("m1", 128, F32), ("vv", 160, F32), ("vg", 320, F32), ("vt", 320, F32), ("vi", 80, I32),
     ("nbm", 72, F32), ("mul", 72, F32), ("sa", 72, I32), ("aa", 72, I32), ("offs", 72, F32), ("offa", 76, F32), ("dl", 72, F32),
-    ("pc", 4, F32), ("th", 288, F32), ("ft", 1152, BF), ("oh", 512, BF), ("w2", 96, F32),
+    ("pc", 4, F32), ("th", 288, F32), ("sg", 3 * C, BF), ("ft", 1152, BF), ("oh", 512, BF), ("w2", 96, F32),
     ("pm", 384, F32), ("ff", 512, BF), ("fg", 512, BF), ("fl", 384, BF), ("flx", 288, BF), ("fa", 800, BF), ("kb", 144, F32),
     ("oa", 18, U16), ("ob", 10, U16), ("mk", 8 * MT, F32), ("vw", OWN + 8 * FAR, BF), ("mm", 152, F32), ("px", 144, F32),
     ("zz", 72, F32), ("oz", 18, U16), ("ah", 1152, BF), ("af", 1152, BF), ("rr", 1152, F32), ("yo", 288, F32),
     ("saf", 72, F32), ("oe1", 128, F32), ("oe2", 128, F32),
 ] + [(k % t, c, d) for t in range(3) for k, c, d in (
         ("fxq%d", C, X4), ("fxs%d", C, U8), ("ll%d", 8, U16), ("sl%d", 8, U16),
-        ("rq%d", C // 2, X4), ("rs%d", C, U8), ("rl%d", 8, U16))]:
+        ("rq%d", CUT, X4), ("rs%d", C, U8), ("rl%d", 8, U16))]:
     SCRATCH[_n] = ("sbuf", [128, _c], _d)
 SHARE = {"pi": ("ci", 0), "vb": ("ci", 32), "ab": ("ci", 48), "nbi": ("ci", 64),
-         "ma": ("cf", 0), "mb": ("cf", 32), "idx": ("cf", 96), "lrow": ("cf", 128), "c18": ("cf", 160),
-         "ta": ("cf", 192), "tb": ("cf", 208), "oaf": ("cf", 224), "ocf": ("cf", 256), "tc": ("cf", 288), "td": ("cf", 304)}
+         "ma": ("cf", 0), "mb": ("cf", 32), "idx": ("cf", 64), "lrow": ("cf", 88), "lsum": ("cf", 128), "c18": ("cf", 168),
+         "oaf": ("cf", 224), "ocf": ("cf", 256), "tc": ("cf", 288), "td": ("cf", 304),
+         "l12": ("lfix", 0), "l3": ("lfix", 20), "lown": ("lfix", 26)}
 
 
 def A(name, c0, c1, step=1, p0=0, p1=128):
@@ -117,7 +122,7 @@ def _load(a):
 
 
 def _program():
-    ops, label = [], ["start"]
+    ops, label = [], ["start", 0]
     AL, AF = AluOpType, ActivationFunctionType
 
     def part(name):
@@ -132,7 +137,7 @@ def _program():
         for i in ins:
             d, f = _parts(i)
             rd += d + f
-        ops.append({"how": how, "rd": rd, "wr": wr, "tag": tag, "kind": label[0], "load": load, "calls": calls})
+        ops.append({"how": how, "rd": rd, "wr": wr, "tag": tag, "kind": label[0], "round": label[1], "load": load, "calls": calls})
 
     def vcost(n, r):
         return FIX + max(64.0, n * r) * CYC
@@ -204,10 +209,10 @@ def _program():
         a, b, c, d = A(st[0], s0, s0 + 128), A(st[1], s0, s0 + 128), A(mv[0], m0, m0 + n), A(mv[1], m0, m0 + n)
         add({"P": (20 + (n + 16) * PEC, lambda q, R: q.matmul_mx(R(o), R(a), R(b), R(c), R(d), start, stop))}, [o], [a, b, c, d])
 
-    def pick(dst, d0, src, ncols, off):
+    def pick(dst, d0, src, ncols, off, eng="VS"):
         n = _count(ind(None, off))
         copy(cast(A(dst[0], d0, d0 + n), 32), ind(cast(A(src[0], 0, ncols), 32), off), "V")
-        copy(A(dst[1], d0, d0 + n), ind(A(src[1], 0, ncols), off), "VS")
+        copy(A(dst[1], d0, d0 + n), ind(A(src[1], 0, ncols), off), eng)
 
     def dma(pairs, eng="Y", behind=None):
         load = sum(_load(o if o[0] != "hbm" else i) for o, i in pairs)
@@ -227,14 +232,17 @@ def _program():
             f = lambda q, R: q.iota(R(out), pat, base, cm)
         add({"G": (150 + 2 * _count(out) * CYC, f)}, [out], [])
 
+    def nought(out):
+        iota(out, [[0, _count(out)]], 0, 0)
+
     def where(out, in_, pat, op, fillv, base, cm):
         add({"G": (190 + 2 * _count(out) * CYC, lambda q, R: q.affine_select(R(out), R(in_), pat, op, fillv, base, cm))}, [out], [in_])
 
     def send(t, kind, cost, ins, load):
-        add({"G": (cost, None)}, [A("wire", 2 * t + kind, 2 * t + kind + 1)], ins, tag=("send", t, kind), load=load)
+        add({"G": (cost, None)}, [A("wire", 3 * t + kind, 3 * t + kind + 1)], ins, tag=("send", t, kind), load=load)
 
     def land(t, kind, cost, outs):
-        add({"N": (cost, None)}, outs, [A("wire", 2 * t + min(kind, 1), 2 * t + min(kind, 1) + 1)], tag=("land", t, kind))
+        add({"N": (cost, None)}, outs, [A("wire", 3 * t + 2, 3 * t + 3) if kind else A("wire", 3 * t, 3 * t + 2)], tag=("land", t, kind))
 
     UQ, VQ, WQ, UP, EQ, CQ = ("uq", "us"), ("vq", "vs"), ("wq", "wsc"), ("upq", "ups"), ("eq", "es"), ("cq", "cs")
     FQ, GQ, JQ, NQ, HQ, KQ, ZQ, XQ, BQ = [(k + "q", k + "s") for k in "fgjnhkzxb"]
@@ -246,8 +254,8 @@ def _program():
         return A("pb", k, k + 1, 1, p0, 128)
 
     part("load")
-    dma([(A("xin", 0, 1152), hbm("x", every))], "Y")
-    dma([(A("uin", 0, 512), hbm("u", every))], "S")
+    dma([(A("uin", 0, 512), hbm("u", every))], "Y")
+    dma([(A("xin", 0, 1152), hbm("x", every))], "S")
     part("loadn")
     dma([(A("m0", 32 * c, 32 * c + 32, 1, 0, 9), hbm("nb", (c, every))) for c in range(4)]
         + [(A("m0", 128 + 32 * c, 160 + 32 * c, 1, 0, 9), hbm("e", (c, every))) for c in range(4)])
@@ -260,7 +268,7 @@ def _program():
         iota(A("pi", k, k + 1), [[1, 1]], 0, 1 << k, False)
     ts(A("pi", 3, 6), A("pi", 0, 3), 15, None, AL.bitwise_and)
     copy(A("pb", 0, 6), A("pi", 0, 6))
-    P, Q16, Q8X2, Q4X4, G16, G, B3X8, B2X8, B3 = pb(0), pb(3), pb(4), pb(5), pb(6), pb(7), pb(23), pb(24), pb(25)
+    P, Q16, Q8X2, Q4X4, G16, G, B3X8, B2X8 = pb(0), pb(3), pb(4), pb(5), pb(6), pb(7), pb(23), pb(24)
     part("pb2")
     lin(G16, Q16, -1.0, P)
     lin(G, G16, 0.0625, 0.0)
@@ -271,10 +279,10 @@ def _program():
     fill(A("ones", 0, 512), 1.0)
     fill(A("lu", 0, 10), 2)
     part("blank0")
-    zero(A("ft", 2, 1152, 4, 0, 96))
-    zero(A("oh", 0, 512))
-    zero(A("dig", 3, 1024, 4))
-    zero(A("dig", 2, 1024, 4, 0, 96))
+    zero(A("ft", 1, 1152, 4, 0, 96))
+    blank([("dig", 0, 512), ("dig", 512, 1024)])
+    part("blank1")
+    blank([("oh", 0, 512)])
     part("lu")
     lin(pb(22), Q8X2, 8.0, 1.0)
     ts(A("lu", 10, 18), A("ones", 0, 8), pb(22), None, AL.mult)
@@ -282,20 +290,18 @@ def _program():
     part("qu")
     quant(UQ, 0, 128, A("uin", 0, 512))
     quant(XQ, PRE, C, A("xin", 0, 1152))
-    pick(UP, U_ORD, UQ, 128, A("lu", 0, 9))
+    pick(UP, U_ORD, UQ, 128, A("lu", 0, 8))
     part("qu2")
     pick(UP, U_FRM, UQ, 128, A("lu", 10, 18))
     again(UP, U_FRM + 128, UP, U_FRM, 128)
     part("qu3")
     pick(UP, U_MRK, UQ, 128, A("lu", 18, 27))
     again(UP, U_MRK + 144, UP, U_MRK + 1, 136)
-    part("pre")
-    again(XQ, 0, XQ, PRE, PRE)
     part("pre2")
     again(BQ, 0, XQ, PRE, PRE)
     part("tri")
     where(A("tri", 0, 128), A("zb", 0, 128), [[1, 128]], AL.is_ge, BIG, 0, -1)
-    fill(A("th", 256, 288, 1, 0, 96), BIG)
+    fill(A("th", 128, CUT, 1, 0, 96), BIG)
     quant(CQ, C_ONE, 128, A("ones", 0, 512))
     part("etile")
     where(A("ebig", 0, 512), A("ones", 0, 512), [[-1, 512]], AL.is_equal, 0.0, 3, 4)
@@ -312,20 +318,21 @@ def _program():
         copy(A("dig", at, at - at % 4 + 512, 4, q0, 128), A("ones", 0, 128, 1, q0, 128), "VS", pb(col, q0))
     quant(CQ, C_HI, 256, A("dig", 0, 1024))
     part("rw")
-    iota(A("qrow", 0, 144), [[0, 9], [1, 16]], 0, 0)
-    lin(pb(21), Q16, 1.0, 1.0)
-    ts(A("ma", 0, 32), A("qrow", 0, 32), Q16, CAP, AL.is_equal, AL.mult)
-    ts(A("mb", 0, 32), A("qrow", 0, 32), pb(21), -HOLD, AL.is_equal, AL.mult)
-    tt(A("rw", 0, 32), A("ma", 0, 32), A("mb", 0, 32), AL.add)
-    copy(A("rw", 32, 64), A("rw", 0, 32), "VS")
-    copy(A("rw", 64, 96), A("rw", 0, 32), "VS")
-    copy(A("rw", 96, 144), A("rw", 0, 48), "VS")
+    head = A("rw", 0, 144, 1, 0, 16)
+    where(head, A("zb", 0, 144, 1, 0, 16), [[0, 9], [1, 16]], AL.not_equal, CAP, 0, -1)
+    where(head, head, [[0, 9], [1, 16]], AL.not_equal, -HOLD, -1, -1)
+    dma([(A("rw", 0, 144, 1, k, k + 16), head) for k in range(16, 128, 16)])
+    part("qrow")
     ts(pb(13), Q16, 15.0, HOLD, AL.not_equal, AL.mult)
     part("rf")
-    blank([("rf", 0, 192), ("ff", 0, 256), ("fg", 0, 256), ("rc", 0, 144)])
-    fill(A("rf", 0, 192, 8), -BIG)
+    where(A("rf", 0, 192), A("zb", 0, 192), [[0, 24], [1, 8]], AL.not_equal, -BIG, 0, 0)
+    nought(A("ff", 3, 256, 4))
+    nought(A("fg", 3, 256, 4))
+    part("sel0")
+    blank([("sel", 0, 512), ("sel", 512, 1056)])
+    blank([("sel", 1056, 1600), ("sel", 1600, 2176)])
     part("sel")
-    blank([("sel", 0, 512), ("sel", 512, 1056), ("sel", 1056, 1600), ("sel", 1600, 2176)])
+    iota(A("qrow", 0, 144), [[0, 9], [1, 16]], 0, 0)
     iota(A("grow", 0, 128), [[1, 8], [0, 16]], 0, 0)
     ts(A("sel", 0, 512, 4), A("grow", 0, 128), G, MT / 2.0, AL.is_equal, AL.mult)
     copy(A("sel", 1, 512, 4), A("sel", 0, 512, 4), "VS", -1.0)
@@ -336,35 +343,33 @@ def _program():
     quant(CQ, C_SUM, 264, A("sel", 0, 1056))
     quant(CQ, C_OWN, 280, A("sel", 1056, 2176))
     part("blank")
-    fill(A("rc", 0, 144, 4), -BIG)
-    zero(A("zf", 0, 160))
-    blank([("fa", 0, 400), ("fa", 400, 800)])
-    dma([(A("vv", 0, 160), A("zf", 0, 160))])
-    dma([(A("mm", 0, 8), A("zf", 0, 8)), (A("offa", 0, 4), A("zf", 0, 4)), (A("oe1", 0, 128, 1, 0, 32), A("zf", 0, 128, 1, 0, 32))])
+    nought(A("vv", 0, 160))
+    for c0 in range(0, 800, 200):
+        nought(A("fa", c0, c0 + 200))
     part("gaps")
-    for r in range(7):
-        iota(A("mk", MT * r + E, MT * r + MT), [[0, MT - E]], 0, 0)
+    where(A("rc", 0, 144), A("zb", 0, 144), [[0, 36], [1, 4]], AL.not_equal, -BIG, 0, 0)
+    for a in [A("mm", 0, 8), A("offa", 0, 1), A("oe1", 0, 128, 1, 0, 32)] + [A("mk", MT * r + E, MT * r + MT) for r in range(7)]:
+        nought(a)
     part("lists")
-    iota(A("iot", 0, 32), [[1, 32]], 0, 0)
     iota(A("lrow", 0, 4), [[8, 2], [1, 2]], 0, 0)
     iota(A("lrow", 4, 20), [[16, 2], [32, 4], [0, 2]], 0, 0)
+    iota(A("lrow", 20, 26), [[2, 6]], 64, 0)
+    iota(A("lrow", 26, 31), [[64, 5]], 0, 0)
+    iota(A("lrow", 31, 36), [[64, 5]], 5 * 64 + 8 - C, 0)
     iota(A("idx", 0, 18), [[FAR, 3], [16, 6]], 0, 0)
+    iota(pb(25), [[0, 1]], -2, 0)
     lin(A("idx", 0, 18), A("idx", 0, 18), 1.0, Q16)
     lin(pb(8), B2X8, 2.0, G)
     lin(pb(9), Q4X4, 8.0, pb(8))
-    lin(pb(10), B2X8, 16.0, 64.0)
+    lin(pb(10), B3X8, 0.125, 0.0)
     lin(pb(11), Q4X4, 8.0, pb(10))
-    lin(pb(12), B3X8, 0.125, pb(11))
+    lin(pb(12), B2X8, 16.0, pb(11))
     lin(pb(14), B3X8, -0.125, 1.0)
-    lin(B3, B3X8, 0.125, 0.0)
-    lin(pb(15), B3X8, 4.0, 0.0)
-    ts(A("l12", 0, 4), A("lrow", 0, 4), pb(9), None, AL.add)
-    ts(A("l12", 4, 20), A("lrow", 4, 20), Q16, None, AL.add)
-    ts(A("l3", 0, 5), A("iot", 0, 5), 2.0, pb(12), AL.mult, AL.add)
-    lin(A("ta", 0, 9), A("iot", 0, 9), 64.0, pb(15))
-    ts(A("tb", 0, 9), A("ta", 0, 9), float(C), 8.0 - C, AL.is_ge, AL.mult)
-    tt(A("tb", 0, 9), A("ta", 0, 9), A("tb", 0, 9), AL.add)
-    ts(A("lown", 0, 9), A("tb", 0, 9), pb(8), None, AL.add)
+    lin(pb(15), B3X8, 4.0, pb(8))
+    lin(pb(16), B3X8, (32.0 + 8 - C) / 8, pb(8))
+    for c0, c1, col in ((0, 4, pb(9)), (4, 20, Q16), (20, 26, pb(12)), (26, 30, pb(15)), (30, 31, pb(16)), (31, 36, pb(15))):
+        lin(A("lsum", c0, c1), A("lrow", c0, c1), 1.0, col)
+    copy(A("lfix", 0, 36), A("lsum", 0, 36))
     part("edges")
     ts(A("m1", 0, 128, 1, 0, 9), A("m0", 128, 256, 1, 0, 9), float(MT), None, AL.mult)
     tt(A("vv", 0, 128, 1, 0, 9), A("m1", 0, 128, 1, 0, 9), A("m0", 0, 128, 1, 0, 9), AL.add)
@@ -375,7 +380,7 @@ def _program():
     copy(A("c18", 0, 9), A("vt", 0, 9), "VS")
     copy(A("c18", 9, 18), A("vt", 32, 41), "VS")
     copy(A("tc", 0, 9), A("c18", 0, 18, 2), "VS", pb(14))
-    copy(A("td", 0, 9), A("c18", 1, 18, 2), "VS", B3)
+    copy(A("td", 0, 9), A("c18", 1, 18, 2), "VS", pb(10))
     tt(A("vb", 0, 9), A("tc", 0, 9), A("td", 0, 9), AL.add)
     ts(A("nbi", 0, 9), A("vb", 0, 9), MT - 1, None, AL.bitwise_and)
     copy(A("lnb", 0, 9), A("nbi", 0, 9))
@@ -383,36 +388,44 @@ def _program():
     copy(A("vi", 0, 80), ind(A("vt", 0, 320), A("l3", 0, 5)))
     ts(A("sa", 0, 72), A("vi", 0, 72), 9, None, AL.logical_shift_right)
     ts(A("aa", 0, 72), A("vi", 0, 72), MT - 1, None, AL.bitwise_and)
-    ts(A("dl", 0, 72), A("aa", 0, 72), float(C), None, AL.is_ge)
+    copy(A("saf", 0, 72), A("aa", 0, 72))
+    lin(A("zz", 0, 72), A("saf", 0, 72), 1.0 / H, 0.5 / H - 0.5)
+    lin(A("dl", 0, 72), A("zz", 0, 72), 1.0, ROUND)
+    lin(A("zz", 0, 72), A("dl", 0, 72), 1.0, -ROUND)
+    act(A("dl", 0, 72), A("zz", 0, 72), AF.Relu, pb(25))
+    copy(A("offs", 0, 72), A("zz", 0, 72), "VS", float(C))
     lin(A("mul", 0, 72), A("dl", 0, 72), float(FAR - TURN), float(TURN))
-    ts(A("zz", 0, 72), A("aa", 0, 72), float(H), float(C), AL.is_ge, AL.mult)
-    ts(A("saf", 0, 72), A("aa", 0, 72), float(2 * H), float(C), AL.is_ge, AL.mult)
-    copy(A("offs", 0, 72), A("dl", 0, 72), "VS", float(OWN - 3 * C))
-    tt(A("nbm", 0, 72), A("zz", 0, 72), A("aa", 0, 72), AL.add)
-    tt(A("offs", 0, 72), A("offs", 0, 72), A("saf", 0, 72), AL.add)
-    tt(A("nbm", 0, 72), A("nbm", 0, 72), A("offs", 0, 72), AL.add)
+    copy(A("zz", 0, 72), A("dl", 0, 72), "VS", float(OWN - 4 * C))
+    tt(A("nbm", 0, 72), A("offs", 0, 72), A("saf", 0, 72), AL.add)
+    tt(A("nbm", 0, 72), A("nbm", 0, 72), A("zz", 0, 72), AL.add)
     part("qv")
     quant(VQ, 0, 128, A("vin", 0, 512))
 
-    turns = [0]
+    turns, banks = [0], [(5, 6, 7)]
 
     def stream():
         turns[0] += 1
-        return 5 + turns[0] % 3
+        return banks[0][turns[0] % len(banks[0])]
 
     def unpack(mv, end, r, at):
+        if mv == XQ and end - 128 - H < PRE:
+            for b in range(4):
+                k = stream()
+                mm(k, EQ, EW * b + 16 * r, mv, end - H, 128)
+                copy(A("vw", at + H * b, at + H * b + H), bank(k, 0, H), "VS", 0.5)
+            return
         for m in range(2):
             k = stream()
             mm(k, EQ, EW * (2 * m + 1) + 16 * r, mv, end - 128 - H, 128 + H)
             mm(k, EQ, EW * 2 * m + 16 * r, mv, end - 128, 128)
             copy(A("vw", at + 2 * H * m, at + 2 * H * m + 2 * H), bank(k, 128 - H, 128 + H), "VS", 0.5)
 
-    def spread(at, width, made, issued, early):
-        for n, to in enumerate(range(made, 8, made)):
+    def spread(at, width, made, turns_to, behind):
+        for to in turns_to:
             cut, w = 16 * to, width * made
             dma([(A("vw", at + width * to, at + width * to + w, 1, 0, 128 - cut), A("vw", at, at + w, 1, cut, 128)),
                  (A("vw", at + width * to, at + width * to + w, 1, 128 - cut, 128), A("vw", at, at + w, 1, 0, cut))],
-                "Y", None if n < early else issued)
+                "Y", behind)
 
     def frames(to, k, src, x0, ff, gq, at):
         for w, c0 in ((2, 160), (1, 128), (0, 0)):
@@ -423,9 +436,12 @@ def _program():
             ts(A(ff, w, 256, 4), A("pm", a, a + 64), A("pm", a + 7, a + 8), None, AL.is_lt)
         copy(A(ff, 256, 512), A(ff, 0, 256), "VS")
         quant(gq, 0, 128, A(ff, 0, 512))
-        for w, n in ((2, C), (1, 256), (0, 128)):
+        for w, n in ((1, 256), (0, 128)):
             mm(k, gq, 0, EQ, EW * w + 128 - n, n)
-        copy(A(to, 0, C), bank(k, 0, C), "VS")
+        copy(A(to, 0, 256), bank(k, 0, 256), "VS")
+        k = stream()
+        mm(k, gq, 0, EQ, EW * 2, 128)
+        copy(A(to, 256, C), bank(k, 96, 128), "VS")
 
     def halves(k, tile, mv):
         mm(k, CQ, tile + 8, mv, 0, 128, True, False)
@@ -434,27 +450,61 @@ def _program():
     def mark_at(r):
         return U_MRK + r if r % 2 == 0 else U_MRK + 144 + r - 1
 
-    blocks = (0, 128, 160)
+    blocks, runs = (0, 128, 160), ((0, CUT), (CUT, C))
     for t in range(3):
         x0, b1, FX = PRE + C * t, PRE + H * (t + 1), ("fxq%d" % t, "fxs%d" % t)
+        label[1] = t
         part("sendx")
-        send(t, 0, 800.0, [A("xq", x0, x0 + C), A("xs", x0, x0 + C)], 1200.0)
+        send(t, 0, 400.0, [A("xq", x0, x0 + CUT)], 500.0)
+        send(t, 1, 800.0, [A("xq", x0 + CUT, x0 + C), A("xs", x0, x0 + C)], 700.0)
         part("sort")
-        for w, c0 in enumerate(blocks):
-            mm(1 + w, XQ, x0 + c0, UP, U_ORD, 128)
+        def flags(on, k, w, c0, c1, strict):
+            q0 = 96 if w == 1 else 0
+            out, row, pc = A("ft", 4 * c0 + w, 4 * c1, 4, q0), bank(k, c0, c1, 1, q0), A("pc", w, w + 1, 1, q0)
+            if on == "V":
+                ts(out, row, pc, None, AL.is_lt if strict else AL.is_le)
+            else:
+                sign = A("sg", C * w + c0, C * w + c1, 1, q0)
+                act(sign, row, AF.Sign, pc, -1.0)
+                act(out, sign, AF.Relu if strict else AF.Sign, None if strict else A("ones", 0, 1, 1, q0))
+
+        part("head")
+        for w in range(2):
+            mm(1 + w, XQ, x0 + 32 * w, UP, U_ORD, 128)
             copy(A("pc", w, w + 1), bank(1 + w, 0, 1), "S")
-        mm(0, UP, U_ORD, XQ, x0, C)
-        ts(A("ft", 0, 512, 4), bank(0, 0, 128), A("pc", 0, 1), None, AL.is_lt)
-        ts(A("ft", 512, 1152, 4), bank(0, 128, 288), A("pc", 0, 1), None, AL.is_le)
-        ts(A("ft", 1, 1024, 4), bank(0, 0, 256), A("pc", 1, 2), None, AL.is_lt)
-        ts(A("ft", 1025, 1152, 4), bank(0, 256, 288), A("pc", 1, 2), None, AL.is_le)
-        part("ties")
+        jobs = HEAD[t]
+        early = {"S": 4, "V": stream()}
+        for on in sorted(set(jobs[:3] + ("V" if t else ""))):
+            if t or on == "S":
+                mm(early[on], UP, U_ORD, XQ, x0, CUT)
         act(A("th", 0, 128), A("tri", 0, 128), AF.Identity, A("pc", 0, 1))
-        act(A("th", 128, 256), A("tri", 0, 128), AF.Identity, A("pc", 1, 2))
-        act(A("th", 256, 288, 1, 96, 128), A("tri", 96, 128, 1, 96, 128), AF.Identity, A("pc", 2, 3, 1, 96, 128))
-        ts(A("ft", 2, 1152, 4, 96, 128), bank(0, 0, 288, 1, 96, 128), A("pc", 2, 3, 1, 96, 128), None, AL.is_lt)
+        act(A("th", 128, CUT, 1, 96, 128), A("tri", 96, 128, 1, 96, 128), AF.Identity, A("pc", 1, 2, 1, 96, 128))
+        first = ((0, 0, 128, True), (0, 128, CUT, False), (1, 0, CUT, True))
+        for on, job in zip(jobs, first):
+            if t or on == "S":
+                flags(on, early[on], *job)
+        if t:
+            tt(A("ft", 3, 4 * CUT, 4), bank(early["V"], 0, CUT), A("th", 0, CUT), AL.is_equal)
         part("sort")
-        tt(A("ft", 3, 1152, 4), bank(0, 0, 288), A("th", 0, 288), AL.is_equal)
+        late = {"V": 0, "S": stream()}
+        mm(3, XQ, x0 + CUT, UP, U_ORD, 128)
+        copy(A("pc", 2, 3), bank(3, 0, 1), "S")
+        for on in sorted(set(jobs[3:] + "V"), reverse=True):
+            mm(late[on], UP, U_ORD, XQ, x0, C)
+        act(A("th", CUT, C), A("tri", 0, 128), AF.Identity, A("pc", 2, 3))
+        for on, job in zip(jobs, first):
+            if on == "V" and not t:
+                flags(on, 0, *job)
+        for on, job in zip(jobs[3:], ((0, CUT, C, False), (1, CUT, C, False), (2, 0, C, True))):
+            flags(on, late[on], *job)
+        c0 = CUT if t else 0
+        tt(A("ft", 4 * c0 + 3, 4 * C, 4), bank(0, c0, C), A("th", c0, C), AL.is_equal)
+        part("vown")
+        for c in range(3):
+            unpack(XQ, x0 + H * (c + 1), 0, FAR * c)
+        part("early")
+        spread(0, TURN, 1, range(1, 1 + EARLY), None)
+        part("sort")
         quant(FQ, 0, C, A("ft", 0, 1152))
         for w, c0 in enumerate(blocks):
             mm(1 + w, FQ, c0, CQ, C_ONE, 128)
@@ -464,20 +514,20 @@ def _program():
         mm(0, CQ, C_LO, NQ, 0, 128, False, True)
         scan(A("w2", 0, H), A("rw", 0, H), bank(0, 0, H), AL.add, AL.min)
         ts(A("sl%d" % t, 0, 6), A("w2", 15, H, 16), pb(13), None, AL.add)
-        send(t, 1, 400.0, [A("sl%d" % t, 0, 6)], 300.0)
-        issued = A("wire", 8 + t, 9 + t)
+        send(t, 2, 400.0, [A("sl%d" % t, 0, 6)], 300.0)
+        issued = A("wire", 16 + t, 17 + t)
         land(t, 2, 100.0, [issued])
-        part("vown")
-        for r in range(MADE):
-            for c in range(3):
-                unpack(XQ, x0 + H * (c + 1), r, TURN * r + FAR * c)
         part("down")
-        spread(0, TURN, MADE, issued, EARLY)
+        spread(0, TURN, 1, range(1 + EARLY, 8), issued)
         part("mown")
-        for r in range(8):
+        for r in range(8 - MCOPY):
             k = stream()
             mm(k, UP, mark_at(r), XQ, x0, C)
             copy(A("mk", MT * r, MT * r + C), bank(k, 0, C), "VS")
+        part("dmark")
+        for r in range(8 - MCOPY, 8):
+            dma([(A("mk", MT * r, MT * r + C, 1, 0, 128 - r), A("mk", 0, C, 1, r, 128)),
+                 (A("mk", MT * r, MT * r + C, 1, 128 - r, 128), A("mk", 0, C, 1, 0, r))], "Y", issued)
         part("fown")
         frames("fl", 4, XQ, x0, "ff", GQ, 0)
         part("kown")
@@ -486,32 +536,36 @@ def _program():
         halves(1, C_OWN, KQ)
         tt(A("oaf", 0, 18), bank(1, 0, 72, 4), A("idx", 0, 18), AL.add)
         copy(A("oa", 0, 18), A("oaf", 0, 18))
-        part("ah")
-        for b in range(4):
-            copy(A("ah", C * b, C * b + C), ind(A("vw", H * b, OWN - H * (3 - b)), A("oa", 0, 18)), "VS")
+        for h, (c0, c1) in enumerate(runs):
+            part("ah%d" % h)
+            for b in range(4):
+                copy(A("ah", C * b + c0, C * b + c1), ind(A("vw", H * b, OWN - H * (3 - b)), A("oa", c0 // 16, c1 // 16)), "VS")
         part("af")
         for b in (0, 2):
             copy(A("af", C * b, C * b + 2 * C), A("ah", C * b, C * b + 2 * C), "VS", 2.0)
         part("ffar")
-        land(t, 0, WIRE_X, [A(FX[0], 0, C), A(FX[1], 0, C)])
+        land(t, 0, WIRE_X[t], [A(FX[0], 0, C), A(FX[1], 0, C)])
         frames("flx", 3, FX, 0, "fg", JQ, 192)
         part("list")
-        land(t, 1, WIRE_L, [A("ll%d" % t, 0, 6)])
-        copy(A("fl", C, E), ind(A("flx", 0, C), A("ll%d" % t, 0, 6)), "VS")
+        land(t, 1, WIRE_L[t], [A("ll%d" % t, 0, 6)])
+        copy(A("fl", C, E), ind(A("flx", 0, C), A("ll%d" % t, 0, 6)), "S")
         part("pick")
-        pick(BQ, b1 - H, FX, C, A("ll%d" % t, 0, 6))
+        pick(BQ, b1 - H, FX, C, A("ll%d" % t, 0, 6), "S")
+        turns[0], banks[0] = -1, (0, 5, 6, 7, 4, 3)
         part("vfar")
         for r in range(MADEB):
             unpack(BQ, b1, r, OWN + FAR * r)
         part("dfar")
-        spread(OWN, FAR, MADEB, None, 8)
+        spread(OWN, FAR, MADEB, range(MADEB, 8, MADEB), None)
         part("mfar")
         for r in range(8):
             k = stream()
             mm(k, UP, mark_at(r), BQ, b1 - 128, 128)
             copy(A("mk", MT * r + C, MT * r + E), bank(k, 128 - H, 128), "VS")
+        banks[0] = (5, 6, 7)
+        part("knbg")
+        copy(A("fa", 0, 576, 4), ind(A("fl", 0, E), A("lnb", 0, 9)), "V")
         part("knb")
-        copy(A("fa", 0, 576, 4), ind(A("fl", 0, E), A("lnb", 0, 9)), "VS")
         quant(HQ, 0, 200, A("fa", 0, 800))
         mm(1, CQ, C_SUM, HQ, 0, 144)
         scan(A("kb", 0, 144), A("rw", 0, 144), bank(1, 0, 144), AL.add, AL.min)
@@ -534,7 +588,6 @@ def _program():
         scan(A("zz", 0, 72), A("dl", 0, 72), bank(1, 0, 72), AL.add, AL.mult)
         tt(A("ocf", 0, 18), A("zz", 3, 72, 4), A("offa", 4, 73, 4), AL.add)
         copy(A("oz", 0, 18), A("ocf", 0, 18))
-        runs = ((0, 160), (160, 288))
         for h, (c0, c1) in enumerate(runs):
             part("z%d" % h)
             for b in range(4):
@@ -557,7 +610,7 @@ def _program():
         copy(A("oe1", 32 * c, 32 * c + 18, 1, 0, 32), A("saf", c, 72, 4, 0, 32), "VS")
     turn(A("oe2", 0, 128, 1, 0, 32), A("oe1", 0, 128, 1, 0, 32))
     dma([(hbm("oe", (c, every)), A("oe2", 32 * c, 32 * c + 16, 1, 0, 18)) for c in range(4)])
-    for h, (c0, c1) in enumerate(((0, 160), (160, 288))):
+    for h, (c0, c1) in enumerate(runs):
         part("out%d" % h)
         mm(h, VQ, 0, XQ, x0 + c0, c1 - c0)
         copy(A("yo", c0, c1), bank(h, 0, c1 - c0), "VS")
@@ -612,7 +665,7 @@ def _place(ops, before, turn, spare):
         for e, (cost, f) in op["how"].items():
             t = 0.0
             for j, hard in before[i]:
-                d = done[j] + (HOP if hard or eng[j] != e else 0.0)
+                d = done[j] + (hard or (HOP if eng[j] != e else 0.0))
                 if d > t:
                     t = d
             hold = 80.0 * op["calls"] if op["tag"] == "dma" else 1.0 if e == "N" else cost
@@ -632,14 +685,134 @@ def _place(ops, before, turn, spare):
         busy[best[2]].insert(best[3], (best[1], best[1] + best[4], i))
         if op["load"]:
             busy["D"].insert(_gap(busy["D"], best[6], op["load"])[1], (best[6], best[6] + op["load"], i))
-    return max(done), start, eng, {e: [x[2] for x in busy[e]] for e in busy}
+    return max(done), start, eng, {e: [x[2] for x in busy[e]] for e in busy}, done
+
+
+def _run(times, before, turn, eng, old=None, first=0, behind=None, tail=None, limit=0.0):
+    n = len(turn)
+    if old is None:
+        done, held, marks = [0.0] * n, [None] * n, []
+        free, last = {e: 0.0 for e in "VSPGYN"}, {e: None for e in "VSPGYN"}
+    else:
+        done, held, marks = old[1][:], old[2][:], old[3][:first // 32]
+        free, last = dict(old[3][first // 32][0]), dict(old[3][first // 32][1])
+    for at in range(first // 32 * 32, n, 32):
+        marks.append((dict(free), dict(last)))
+        for i in turn[at:at + 32]:
+            e = eng[i]
+            cost, hold, load = times[i][e]
+            t, by, queue = free[e], last[e], True
+            if load and free["Y"] > t:
+                t, by = free["Y"], last["Y"]
+            for j, hard in before[i]:
+                d = done[j] + (hard or (HOP if eng[j] != e else 0.0))
+                if d > t:
+                    t, by, queue = d, j, False
+            if tail is not None and t + tail[i] > limit and i in behind:
+                return None
+            done[i], held[i] = t + cost, (by, queue)
+            free[e], last[e] = t + hold, i
+            if load:
+                free["Y"], last["Y"] = t + load, i
+    return max(done), done, held, marks
+
+
+def _improve(ops, before, turn, eng, draw):
+    for op in ops:
+        op["time"] = {}
+        for e, (cost, f) in op["how"].items():
+            if op["tag"] == "dma":
+                load = max(op["load"], 80.0 * op["calls"])
+                op["time"][e] = (cost + op["load"], load if e == "Y" else 80.0 * op["calls"], load)
+            else:
+                op["time"][e] = (cost, 0.0 if e == "N" else cost, op["load"])
+    times = [op["time"] for op in ops]
+    now = _run(times, before, turn, eng)
+    best, moves = (now, turn, eng), None
+    for step in range(MOVES):
+        if moves is None:
+            tail, nxt = [0.0] * len(turn), {e: 0.0 for e in "VSPGYN"}
+            for i in reversed(turn):
+                e = eng[i]
+                cost, hold, load = times[i][e]
+                q = hold + nxt[e]
+                if load and load + nxt["Y"] > q:
+                    q = load + nxt["Y"]
+                if tail[i] + cost > q:
+                    q = tail[i] + cost
+                tail[i] = nxt[e] = q
+                if load:
+                    nxt["Y"] = q
+                for j, hard in before[i]:
+                    d = q + (hard or (HOP if eng[j] != e else 0.0))
+                    if d > tail[j]:
+                        tail[j] = d
+            moves, near = [], []
+            for i in turn:
+                if now[1][i] - times[i][eng[i]][0] + tail[i] > now[0] - SLACK:
+                    near.append(i)
+                    j, queue = now[2][i]
+                    if queue and j is not None:
+                        moves.append((j, i))
+                    if len(times[i]) > 1:
+                        moves.append((None, i))
+            mean = sum(now[1][i] for i in near) / len(near)
+        j, i = draw(moves)
+        turn2, eng2 = turn, eng
+        if j is None:
+            eng2, a = list(eng), turn.index(i)
+            eng2[i], b = "V" if eng[i] == "S" else "S", a
+        elif draw((0, 0, 1)):
+            a = turn.index(j)
+            b = min(len(turn), turn.index(i) + draw((1, 4, 10, 30)))
+            back, rest, late = [j], [], {j}
+            for k in turn[a + 1:b]:
+                if any(m in late for m, hard in before[k]):
+                    back.append(k)
+                    late.add(k)
+                else:
+                    rest.append(k)
+            if i in late:
+                continue
+            turn2 = turn[:a] + rest + back + turn[b:]
+        else:
+            a, b = turn.index(j), turn.index(i)
+            if draw((0, 0, 1)):
+                a = max(0, a - draw((3, 10, 30)))
+            need, front, rest = set(k for k, hard in before[i]), [i], []
+            for k in reversed(turn[a:b]):
+                if k in need:
+                    front.append(k)
+                    need.update(m for m, hard in before[k])
+                else:
+                    rest.append(k)
+            if j in need:
+                continue
+            turn2 = turn[:a] + front[::-1] + rest[::-1] + turn[b + 1:]
+        limit = now[0] + draw(range(HEAT)) * (1.0 - step / MOVES) + 0.001
+        got = _run(times, before, turn2, eng2, now, a, set(turn2[b + 1:b + 80]), tail, limit)
+        if got is not None and got[0] + PULL * (sum(got[1][i] for i in near) / len(near) - mean) <= limit:
+            now, turn, eng, moves = got, turn2, eng2, None
+            if now[0] < best[0][0]:
+                best = (now, turn, eng)
+    now, turn, eng = best
+    return now[0], [d - times[i][eng[i]][0] for i, d in enumerate(now[1])], eng, {e: [i for i in turn if eng[i] == e] for e in "VSPGYN"}
+
+
+def _before(ops):
+    before = [[(j, HOP if hard else 0.0) for j, hard in op["deps"].items()] for op in ops]
+    for i, op in enumerate(ops):
+        if op["tag"] == "dma" and op["kind"] == "early" and op["round"] > 0:
+            k = min(j for j in range(i, len(ops)) if ops[j]["tag"] == ("send", op["round"], 2))
+            before[k].append((i, -DMA_T))
+    return before
 
 
 def _schedule():
     ops = _program()
     _depends(ops)
     n = len(ops)
-    before = [list(op["deps"].items()) for op in ops]
+    before = _before(ops)
     after = [[] for _ in range(n)]
     for i in range(n):
         for j, hard in before[i]:
@@ -672,22 +845,31 @@ def _schedule():
             now, ahead, spare = got[0], a2, s2
             if best is None or now < best[0]:
                 best = got + (a2, s2)
-    span, start, eng, order = best[:4]
+    span, start, eng, order = _improve(ops, before, sorted(range(n), key=lambda k: best[1][k]), best[2], draw)
     for i, op in enumerate(ops):
         op["eng"], op["at"] = eng[i], start[i]
-    pool = [i for i in order["G"] if ops[i]["tag"] is None]
-    for j, i in zip(pool, pool[1:]):
-        ops[i]["deps"][j] = True
     for i in order["Y"]:
         ended = [j for j in order["V"] if start[j] + ops[j]["how"]["V"][0] + HOP <= start[i]]
-        if ended:
+        if ended and ops[i]["kind"] != "load":
             ops[i]["deps"][ended[-1]] = True
     for op in ops:
         op["all"] = set(j for j, hard in op["deps"].items() if hard or ops[j]["eng"] != op["eng"])
-    for op in ops:
-        inner = set(j for k in op["all"] if ops[k]["eng"] != "N" for j in ops[k]["all"])
-        op["waits"] = [j for j in sorted(op["all"]) if j not in inner]
-    wanted = set(j for op in ops for j in op["waits"])
+    wanted = set(j for op in ops for j in op["all"])
+    known, raised, covers = {e: 0 for e in order}, {e: 0 for e in order}, [0] * n
+    for i in sorted(range(n), key=lambda k: start[k]):
+        op, e = ops[i], eng[i]
+        op["waits"] = []
+        for j in sorted(op["all"], key=lambda k: -start[k]):
+            if not known[e] >> j & 1:
+                op["waits"].append(j)
+                known[e] |= covers[j]
+        if e == "N":
+            covers[i] = 1 << i
+        elif op["tag"] is None and i in wanted and e != "G":
+            raised[e] |= 1 << i
+            covers[i] = known[e] | raised[e]
+        else:
+            covers[i] = known[e] | 1 << i
     names = []
     for e in "VSPGY":
         k = 0
@@ -696,23 +878,26 @@ def _schedule():
             if op["tag"] == "dma":
                 op["sig"] = ("d%d" % i, 16 * op["calls"])
                 names.append("d%d" % i)
+            elif op["tag"] is None and i in wanted and e == "G":
+                op["sig"] = ("g%d" % i, 1)
+                names.append("g%d" % i)
             elif op["tag"] is None and i in wanted:
                 k += 1
                 op["sig"] = ("on" + e, k)
             else:
                 op["sig"] = None
-    return ops, order, names, span, best[4:]
+    return ops, order, names, span, best[5:]
 
 
-AHEAD = {"load": 2000, "sort": -500, "ties": 200, "etile": 6700, "loadv": -2000, "dfar": 500, "pb": 6500, "edges": 700, "blank0": -4500,
-         "x0": -2800, "oe": 2200, "lists": -200, "rw": 2200, "pre": 500, "offs": 500, "rf": 5800, "qu2": 2500, "z0": 1700, "qv": 2000,
-         "af": -1000, "sel": 200, "fill": -200, "x1": -3900, "pre2": 3200, "edgea": 2300, "list": -4000}
-SPARE = {"vown": 200, "mown": 3000, "ah": 3000, "vfar": 0, "mfar": 0, "rw": 9000, "sel": 800, "pb2": 1500, "edgea": 800, "qu": 3000,
-         "out0": 0, "lu": 800, "qu3": 3000, "dig": 9000, "oe": 200, "af": 100, "out1": 0, "blank": 400, "lists": 9000, "pick": 3000,
-         "knb": 1500, "edgeb": 200, "etile": 100, "fown": 0, "kown": 9000, "blank0": 1500, "choose": 9000, "edges": 3000, "qu2": 0,
-         "ffar": 100, "list": 400}
+AHEAD = {"etile": 9400, "qu": 11500, "pick": 10300, "vown": 100, "qu2": 7800, "down": 300, "oe": -4000, "blank0": 2000, "ffar": -500,
+         "pb2": 1300, "vfar": -1800, "z1": -1900, "loadv": -4000, "qu3": 8300, "fill": 4900, "choose": 1000, "dfar": -2000,
+         "dig": 3300, "sel0": -2200, "loadn": 300, "z0": 4900, "pb": 100, "x0": 2200, "out0": -700, "early": 100, "sel": 500,
+         "sendx": 1300, "qrow": 200, "sort": 300, "r1": 3300, "lu": -300, "af": -3900}
+SPARE = {"vown": 100, "mown": 800, "ah0": 800, "ah1": 200, "vfar": 200, "mfar": 200, "af": 0, "choose": 200, "kown": 0, "sel": 0,
+         "qu": 1500, "qu2": 800, "dig": 9000, "qu3": 9000, "lists": 800, "edges": 400, "blank0": 100, "out0": 400, "lu": 400,
+         "ffar": 800, "pb2": 200, "etile": 1500, "edgea": 100, "out1": 100, "oe": 400, "edgeb": 1500, "fown": 800}
 OPS, ORDER, _DMA_SEMS, SPAN, FOUND = _schedule()
-SEMAPHORES = ["onV", "onS", "onP", "onG", "left", "issued"] + [k % t for t in range(3) for k in ("arrx%d", "arrl%d", "rela%d", "relb%d")] + _DMA_SEMS
+SEMAPHORES = ["onV", "onS", "onP", "left", "issued"] + [k % t for t in range(3) for k in ("arrx%d", "arrl%d", "rela%d", "relb%d")] + _DMA_SEMS
 
 
 def _bits(engines):
@@ -723,23 +908,41 @@ def _bits(engines):
 
 
 def _helpers(T, topo, src, dst):
+    able = [c for c in topo.cores_of(src) if T.rank_of(c) is None and topo.may_write(c, dst)]
+    return [c for c in able if topo.die(c) == topo.die(src)], [c for c in able if topo.die(c) != topo.die(src)]
+
+
+def _pieces(T, topo, rank, t):
+    n = len(T.cores)
+    src, dst = T.cores[rank], T.cores[(rank - STEP[t]) % n]
     if topo.may_write(src, dst):
-        return []
-    near = [c for c in topo.cores_of(src) if topo.die(c) == topo.die(src) and T.rank_of(c) is None and topo.may_write(c, dst)]
-    return near[:2]
+        return [(0, "q", 0, CUT, None), (1, "q", CUT, C, None), (1, "s", 0, C, None), (2, "l", 0, 6, None)]
+    near, far = _helpers(T, topo, src, dst)
+    others = [r for r in range(n) if r != rank and T.cores[r] in topo.cores_of(src)]
+    if all(topo.may_write(T.cores[r], T.cores[(r - STEP[t]) % n]) for r in others):
+        plane = [(1, "s", 0, C // 2, far[0]), (1, "s", C // 2, C, far[1])]
+    else:
+        plane = [(1, "s", 0, C, near[0])]
+    return [(0, "q", 0, CUT, near[0]), (1, "q", CUT, C, near[1])] + plane + [(2, "l", 0, 6, near[1])]
 
 
-def _arrivals(T, topo, src, dst, kind):
-    via = _helpers(T, topo, src, dst)
-    if not via:
-        return len(topo.engines(src, dst)) * (1 if kind else 2)
-    if kind:
-        return len(topo.engines(via[1], dst))
-    return 2 * len(topo.engines(via[0], dst)) + len(topo.engines(via[1], dst))
+def _view(T, names, what, c0, c1):
+    a = T[names["qsl".index(what)]][:, c0:c1]
+    return a.bitcast(dt.uint8) if what == "q" else a
 
 
-def _codes(T, name, c0, c1):
-    return T[name][:, c0:c1].bitcast(dt.uint8)
+def _landing(T, t, what, c0, c1):
+    return _view(T, ("fxq%d" % t, "fxs%d" % t, "ll%d" % t), what, c0, c1), T.sem[("arrl%d" if what == "l" else "arrx%d") % t]
+
+
+def _halt(T, t, what, c0, c1):
+    return _view(T, ("rq%d" % t, "rs%d" % t, "rl%d" % t), what, 0, c1 - c0), T.sem[("rela%d" if what == "q" else "relb%d") % t]
+
+
+def _arrivals(T, topo, giver, t, kind):
+    src, dst = T.cores[giver], T.cores[(giver - STEP[t]) % len(T.cores)]
+    return sum(len(topo.engines(src if via is None else via, dst)) for call, what, c0, c1, via in _pieces(T, topo, giver, t)
+               if (what == "l") == bool(kind))
 
 
 def _hand_on(g, core, T, topo):
@@ -747,46 +950,42 @@ def _hand_on(g, core, T, topo):
     for t, d in enumerate(STEP):
         for r in range(n):
             src, dst = T.cores[r], T.cores[(r - d) % n]
-            via = _helpers(T, topo, src, dst)
-            if core not in via:
-                continue
-            k, width = via.index(core), len(topo.engines(src, core))
-            rid, pid = topo.addr(dst, core)
-            g.wait_ge(T.sem["rela%d" % t], width // 2)
-            g.remote_dma(_codes(T, "fxq%d" % t, k * C // 2, (k + 1) * C // 2), _codes(T, "rq%d" % t, 0, C // 2),
-                         T.sem["arrx%d" % t], T.sem.left, pid, rid, topo.mask(core, dst))
-            g.wait_ge(T.sem["relb%d" % t], width)
-            if k == 0:
-                g.remote_dma(T["fxs%d" % t][:, 0:C], T["rs%d" % t][:, 0:C], T.sem["arrx%d" % t], T.sem.left, pid, rid, topo.mask(core, dst))
-            else:
-                g.remote_dma(T["ll%d" % t][:, 0:6], T["rl%d" % t][:, 0:6], T.sem["arrl%d" % t], T.sem.left, pid, rid, topo.mask(core, dst))
-            sent += 2 * len(topo.engines(core, dst))
+            for call, what, c0, c1, via in _pieces(T, topo, r, t):
+                if via != core:
+                    continue
+                rid, pid = topo.addr(dst, core)
+                here, sem = _halt(T, t, what, c0, c1)
+                out, landed = _landing(T, t, what, c0, c1)
+                g.wait_ge(sem, len(topo.engines(src, core)) // (2 if what == "s" and c1 - c0 < C else 1))
+                g.remote_dma(out, here, landed, T.sem.left, pid, rid, topo.mask(core, dst))
+                sent += len(topo.engines(core, dst))
     if sent:
         g.wait_ge(T.sem.left, sent)
 
 
-def _send(g, core, T, topo, dst, t, kind):
-    via = _helpers(T, topo, core, dst)
-    first = via[kind] if via else dst
-    rid, pid = topo.addr(first, core)
-    eng = topo.engines(core, first)
-    x0 = PRE + C * t
-    if kind:
-        out, sem = (T["rl%d" % t], T.sem["relb%d" % t]) if via else (T["ll%d" % t], T.sem["arrl%d" % t])
-        g.remote_dma(out[:, 0:6], T["sl%d" % t][:, 0:6], sem, T.sem.left, pid, rid, _bits(eng))
+def _send(g, core, T, topo, rank, t, kind):
+    dst, x0, sent, parts = T.cores[(rank - STEP[t]) % len(T.cores)], PRE + C * t, 0, []
+    for call, what, c0, c1, via in _pieces(T, topo, rank, t):
+        if call != kind:
+            continue
+        to = dst if via is None else via
+        rid, pid = topo.addr(to, core)
+        eng = topo.engines(core, to)
+        out, sem = _landing(T, t, what, c0, c1) if via is None else _halt(T, t, what, c0, c1)
+        src = T["sl%d" % t][:, c0:c1] if what == "l" else _view(T, ("xq", "xs"), what, x0 + c0, x0 + c1)
+        if what == "s" and c1 - c0 < C:
+            half = len(eng) // 2
+            parts.append(RemoteDMATransfer(dst_ids=[DstId(rid=rid, pnc=pid)], dma_engine_mask=_bits(eng[len(parts) * half:][:half]),
+                                           remote_sem=sem, src=src, dst=out))
+            sent += half
+        else:
+            g.remote_dma(out, src, sem, T.sem.left, pid, rid, _bits(eng))
+            sent += len(eng)
+    if parts:
+        g.remote_dma_fused(parts, local_sem=T.sem.left)
+    if kind == 2:
         g.sem_inc(T.sem.issued, 1)
-        return len(eng)
-    half, parts = len(eng) // 2, []
-    for k in range(2):
-        r2, p2 = topo.addr(via[k] if via else dst, core)
-        out = _codes(T, "rq%d" % t, 0, C // 2) if via else _codes(T, "fxq%d" % t, k * C // 2, (k + 1) * C // 2)
-        parts.append(RemoteDMATransfer(dst_ids=[DstId(rid=r2, pnc=p2)], dma_engine_mask=_bits(eng[k * half:(k + 1) * half]),
-                                       remote_sem=T.sem[("rela%d" if via else "arrx%d") % t],
-                                       src=_codes(T, "xq", x0 + k * C // 2, x0 + (k + 1) * C // 2), dst=out))
-    g.remote_dma_fused(parts, local_sem=T.sem.left)
-    out, sem = (T["rs%d" % t], T.sem["relb%d" % t]) if via else (T["fxs%d" % t], T.sem["arrx%d" % t])
-    g.remote_dma(out[:, 0:C], T["xs"][:, x0:x0 + C], sem, T.sem.left, pid, rid, _bits(eng))
-    return 2 * len(eng)
+    return sent
 
 
 def rank_program(g, core, T, topo):
@@ -810,7 +1009,7 @@ def rank_program(g, core, T, topo):
                     name, k = "issued", tag[1] + 1
                 else:
                     name = ("arrl%d" if tag[2] else "arrx%d") % tag[1]
-                    k = _arrivals(T, topo, T.cores[(rank + STEP[tag[1]]) % n], core, tag[2])
+                    k = _arrivals(T, topo, (rank + STEP[tag[1]]) % n, tag[1], tag[2])
                 wants[name] = max(wants.get(name, 0), k)
             for name, k in wants.items():
                 if have.get(name, 0) < k:
@@ -818,8 +1017,7 @@ def rank_program(g, core, T, topo):
                     have[name] = k
                     waited[name] = max(waited.get(name, 0), k)
             if op["how"][e][1] is None:
-                t = op["tag"][1]
-                sent += _send(g, core, T, topo, T.cores[(rank - STEP[t]) % n], t, op["tag"][2])
+                sent += _send(g, core, T, topo, rank, op["tag"][1], op["tag"][2])
                 continue
             call = op["how"][e][1](q, R)
             if op["sig"] is not None:

from concourse.bass import DstId, RemoteDMATransfer
from concourse.mybir import dt, AluOpType, ActivationFunctionType

C, H, E = 288, 96, 384
STEP = [1, 2, 4]
BIG = 1.0e29
PRE = 128
TURN, OWN, FAR = 4 * C, 32 * C, 4 * H
MT = 512
MADEB, EARLY = 2, 1
HEAD = ("VVSVVV", "VSSVVV", "VSSVVV")
MCOPY = 0
EW = 128 + 16 * (MADEB - 1)
CAP, HOLD, ROUND = 65536.0, 16384.0, 12582912.0
TRIES, MOVES, HEAT = 1, 55000, 40
SLACK, PULL = 120.0, 0.5
CUT = 160
CYC, PEC, FIX, HOP, DMA_T, ROW, RATE = 1.0, 0.6, 60.0, 120.0, 1700.0, 24.0, 26.0
WIRE_X, WIRE_L = (5000.0, 4000.0, 2800.0), (3500.0, 3500.0, 2000.0)
F32, BF, I32, U16, X4, U8 = "float32", "bfloat16", "int32", "uint16", "float8_e4m3fn_x4", "uint8"
SIZE = {F32: 4, BF: 2, I32: 4, U16: 2, X4: 4, U8: 1}

SCRATCH = {"ps": ("psum", [128, 4096], F32)}
for _n, _c, _d in [
    ("xin", 1152, BF), ("uin", 512, BF), ("vin", 512, BF), ("xt", 1152, BF), ("zt", 1152, BF),
    ("wq", 512, X4), ("wsc", 512, U8), ("uq", 128, X4), ("us", 128, U8), ("vq", 128, X4), ("vs", 128, U8),
    ("upq", 688, X4), ("ups", 688, U8), ("eq", 4 * EW, X4), ("es", 4 * EW, U8), ("cq", 928, X4), ("cs", 928, U8),
    ("fq", 288, X4), ("fs", 288, U8), ("gq", 128, X4), ("gs", 128, U8), ("jq", 128, X4), ("js", 128, U8),
    ("nq", 128, X4), ("ns", 128, U8), ("hq", 200, X4), ("hs", 200, U8), ("kq", 200, X4), ("ks", 200, U8),
    ("zq", 288, X4), ("zs", 288, U8), ("xq", PRE + 4 * C, X4), ("xs", PRE + 4 * C, U8), ("bq", PRE + 3 * H, X4), ("bs", PRE + 3 * H, U8),
    ("ones", 512, BF), ("ebig", 4 * EW + 8, BF), ("dig", 1024, BF), ("sel", 2176, BF), ("tri", 128, BF), ("zb", 576, BF),
    ("rw", 144, BF), ("rf", 192, BF), ("rc", 144, BF), ("qrow", 144, BF), ("grow", 128, BF), ("nrow", 96, BF),
    ("ci", 96, I32), ("cf", 320, F32), ("pb", 32, F32),
    ("lu", 28, U16), ("lfix", 36, U16), ("lnb", 10, U16),
    ("m0", 256, I32), ("m1", 128, F32), ("vv", 160, F32), ("vg", 320, F32), ("vt", 320, F32), ("vi", 80, I32),
    ("nbm", 72, F32), ("mul", 72, F32), ("sa", 72, I32), ("aa", 72, I32), ("offs", 72, F32), ("offa", 76, F32), ("dl", 72, F32),
    ("pc", 4, F32), ("th", 288, F32), ("sg", 3 * C, BF), ("ft", 1152, BF), ("oh", 512, BF), ("w2", 96, F32),
    ("pm", 384, F32), ("ff", 512, BF), ("fg", 512, BF), ("fl", 384, BF), ("flx", 288, BF), ("fa", 800, BF), ("kb", 144, F32),
    ("oa", 18, U16), ("ob", 10, U16), ("mk", 8 * MT, F32), ("vw", OWN + 8 * FAR, BF), ("mm", 152, F32), ("px", 144, F32),
    ("zz", 72, F32), ("oz", 18, U16), ("ah", 1152, BF), ("af", 1152, BF), ("rr", 1152, F32), ("yo", 288, F32),
    ("saf", 72, F32), ("oe1", 128, F32), ("oe2", 128, F32),
] + [(k % t, c, d) for t in range(3) for k, c, d in (
        ("fxq%d", C, X4), ("fxs%d", C, U8), ("ll%d", 8, U16), ("sl%d", 8, U16),
        ("rq%d", CUT, X4), ("rs%d", C, U8), ("rl%d", 8, U16))]:
    SCRATCH[_n] = ("sbuf", [128, _c], _d)
SHARE = {"pi": ("ci", 0), "vb": ("ci", 32), "ab": ("ci", 48), "nbi": ("ci", 64),
         "ma": ("cf", 0), "mb": ("cf", 32), "idx": ("cf", 64), "lrow": ("cf", 88), "lsum": ("cf", 128), "c18": ("cf", 168),
         "oaf": ("cf", 224), "ocf": ("cf", 256), "tc": ("cf", 288), "td": ("cf", 304),
         "l12": ("lfix", 0), "l3": ("lfix", 20), "lown": ("lfix", 26)}


def A(name, c0, c1, step=1, p0=0, p1=128):
    name, at = SHARE.get(name, (name, 0))
    return ("ap", name, p0, p1, at + c0, at + c1, step)


def bank(k, c0, c1, step=1, p0=0, p1=128):
    return A("ps", 512 * k + c0, 512 * k + c1, step, p0, p1)


def cast(a, d):
    return ("cast", a, d)


def ind(a, off):
    return ("ind", a, off)


def hbm(name, idx):
    return ("hbm", name, idx)


def _real(T, a):
    if not isinstance(a, tuple):
        return a
    if a[0] == "ap":
        if a[6] == 1:
            return T[a[1]][a[2]:a[3], a[4]:a[5]]
        return T[a[1]][a[2]:a[3], a[4]:a[5]:a[6]]
    if a[0] == "cast":
        return _real(T, a[1]).bitcast(dt.uint8 if a[2] == 8 else dt.uint32)
    if a[0] == "ind":
        return _real(T, a[1]).indirect(_real(T, a[2]))
    return T[a[1]][a[2]]


def _parts(a):
    if not isinstance(a, tuple) or a[0] == "hbm":
        return [], []
    if a[0] == "ap":
        return [a], []
    if a[0] == "cast":
        return _parts(a[1])
    return _parts(a[1])[0], [a[2]]


def _count(a):
    if a[0] == "ind":
        return 16 * (a[2][5] - a[2][4])
    if a[0] == "cast":
        return _count(a[1])
    return len(range(a[4], a[5], a[6]))


def _two(a):
    return a[0] == "ap" and SCRATCH[a[1]][2] == BF


def _mask(a):
    if a[6] == 1:
        return ((1 << (a[5] - a[4])) - 1) << a[4]
    m = 0
    for c in range(a[4], a[5], a[6]):
        m |= 1 << c
    return m


def _load(a):
    a = _parts(a)[0][0]
    rows, width = a[3] - a[2], _count(a) * SIZE[SCRATCH[a[1]][2]]
    return max(rows, 16) / 16.0 * ROW + rows * width / (16.0 * RATE)


def _program():
    ops, label = [], ["start", 0]
    AL, AF = AluOpType, ActivationFunctionType

    def part(name):
        label[0] = name

    def add(how, outs, ins, tag=None, load=0.0, calls=1):
        rd, wr = [], []
        for o in outs:
            d, f = _parts(o)
            wr += d
            rd += f
        for i in ins:
            d, f = _parts(i)
            rd += d + f
        ops.append({"how": how, "rd": rd, "wr": wr, "tag": tag, "kind": label[0], "round": label[1], "load": load, "calls": calls})

    def vcost(n, r):
        return FIX + max(64.0, n * r) * CYC

    def rate(out, in_):
        if in_[0] == "ind":
            return 1.56
        return 0.5 if _two(out) and _two(in_) else 1.0

    def copy(out, in_, eng="V", scale=None):
        n, how = _count(out), {}
        if "V" in eng:
            if scale is None:
                how["V"] = (vcost(n, rate(out, in_)), lambda q, R: q.tensor_copy(R(out), R(in_)))
            else:
                how["V"] = (vcost(n, rate(out, in_)), lambda q, R: q.tensor_scalar(R(out), R(in_), R(scale), None, AL.mult))
        if "S" in eng:
            r = 1.56 if in_[0] == "ind" else 1.0
            if scale is None:
                how["S"] = (vcost(n, r), lambda q, R: q.activation(R(out), R(in_), AF.Copy))
            else:
                how["S"] = (vcost(n, r), lambda q, R: q.activation(R(out), R(in_), AF.Copy if isinstance(scale, float) else AF.Identity, scale=R(scale)))
        add(how, [out], [in_, scale])

    def lin(out, in_, m, plus):
        c = vcost(_count(out), 1.0)
        add({"V": (c, lambda q, R: q.tensor_scalar(R(out), R(in_), m, R(plus), AL.mult, AL.add)),
             "S": (c, lambda q, R: q.activation(R(out), R(in_), AF.Copy if isinstance(plus, float) else AF.Identity, bias=R(plus), scale=m))},
            [out], [in_, plus])

    def ts(out, in0, s1, s2, op0, op1=None):
        if op1 is None:
            f = lambda q, R: q.tensor_scalar(R(out), R(in0), R(s1), None, op0)
        else:
            f = lambda q, R: q.tensor_scalar(R(out), R(in0), R(s1), R(s2), op0, op1)
        add({"V": (vcost(_count(out), rate(out, in0)), f)}, [out], [in0, s1, s2])

    def tt(out, in0, in1, op):
        r = 1.0 if "ps" in (in0[1], in1[1]) else 2.0
        add({"V": (vcost(_count(out), r), lambda q, R: q.tensor_tensor(R(out), R(in0), R(in1), op))}, [out], [in0, in1])

    def scan(out, d0, d1, op0, op1):
        add({"V": (vcost(_count(out), 1.0), lambda q, R: q.tensor_tensor_scan(R(out), R(d0), R(d1), 0.0, op0, op1))}, [out], [d0, d1])

    def fill(out, v):
        add({"V": (vcost(_count(out), 0.5 if _two(out) else 1.0), lambda q, R: q.memset(R(out), v))}, [out], [])

    def zero(out):
        src = A("ones", 0, _count(out), 1, out[2], out[3])
        add({"V": (vcost(_count(out), 0.5 if _two(out) else 1.0), lambda q, R: q.memset(R(out), 0.0)),
             "S": (vcost(_count(out), 1.0), lambda q, R: q.activation(R(out), R(src), AF.Copy, scale=0.0))}, [out], [src])

    def turn(out, in_):
        add({"V": (vcost(_count(out), 1.0), lambda q, R: q.transpose(R(out), R(in_)))}, [out], [in_])

    def act(out, in_, func, bias=None, scale=1.0):
        if bias is None:
            f = lambda q, R: q.activation(R(out), R(in_), func, scale=scale)
        else:
            f = lambda q, R: q.activation(R(out), R(in_), func, bias=R(bias), scale=scale)
        add({"S": (vcost(_count(out), 1.0), f)}, [out], [in_, bias])

    def quant(pair, c0, n, in_):
        o, s = A(pair[0], c0, c0 + n), A(pair[1], c0, c0 + n)
        add({"V": (FIX + n, lambda q, R: q.quantize_mx(R(o), R(s), R(in_)))}, [o, s], [in_])

    def mm(k, st, s0, mv, m0, n, start=True, stop=True):
        o = bank(k, 0, n)
        a, b, c, d = A(st[0], s0, s0 + 128), A(st[1], s0, s0 + 128), A(mv[0], m0, m0 + n), A(mv[1], m0, m0 + n)
        add({"P": (20 + (n + 16) * PEC, lambda q, R: q.matmul_mx(R(o), R(a), R(b), R(c), R(d), start, stop))}, [o], [a, b, c, d])

    def pick(dst, d0, src, ncols, off, eng="VS"):
        n = _count(ind(None, off))
        copy(cast(A(dst[0], d0, d0 + n), 32), ind(cast(A(src[0], 0, ncols), 32), off), "V")
        copy(A(dst[1], d0, d0 + n), ind(A(src[1], 0, ncols), off), eng)

    def dma(pairs, eng="Y", behind=None):
        load = sum(_load(o if o[0] != "hbm" else i) for o, i in pairs)
        add({e: (DMA_T, lambda q, R: [q.dma_start(R(o), R(i)) for o, i in pairs]) for e in eng},
            [o for o, i in pairs], [i for o, i in pairs] + [behind], tag="dma", load=load, calls=len(pairs))

    def blank(runs):
        dma([(A(name, c0, c1), A("zb", 0, c1 - c0)) for name, c0, c1 in runs])

    def again(dst, d0, src, s0, n):
        dma([(cast(A(dst[0], d0, d0 + n), 8), cast(A(src[0], s0, s0 + n), 8)), (A(dst[1], d0, d0 + n), A(src[1], s0, s0 + n))])

    def iota(out, pat, base, cm, flag=True):
        if flag:
            f = lambda q, R: q.iota(R(out), pat, base, cm, allow_small_or_imprecise_dtypes=True)
        else:
            f = lambda q, R: q.iota(R(out), pat, base, cm)
        add({"G": (150 + 2 * _count(out) * CYC, f)}, [out], [])

    def nought(out):
        iota(out, [[0, _count(out)]], 0, 0)

    def where(out, in_, pat, op, fillv, base, cm):
        add({"G": (190 + 2 * _count(out) * CYC, lambda q, R: q.affine_select(R(out), R(in_), pat, op, fillv, base, cm))}, [out], [in_])

    def send(t, kind, cost, ins, load):
        add({"G": (cost, None)}, [A("wire", 3 * t + kind, 3 * t + kind + 1)], ins, tag=("send", t, kind), load=load)

    def land(t, kind, cost, outs):
        add({"N": (cost, None)}, outs, [A("wire", 3 * t + 2, 3 * t + 3) if kind else A("wire", 3 * t, 3 * t + 2)], tag=("land", t, kind))

    UQ, VQ, WQ, UP, EQ, CQ = ("uq", "us"), ("vq", "vs"), ("wq", "wsc"), ("upq", "ups"), ("eq", "es"), ("cq", "cs")
    FQ, GQ, JQ, NQ, HQ, KQ, ZQ, XQ, BQ = [(k + "q", k + "s") for k in "fgjnhkzxb"]
    U_ORD, U_FRM, U_MRK = 0, 144, 400
    C_ONE, C_HI, C_LO, C_SUM, C_CNT, C_OWN, C_CHO = 0, 128, 256, 384, 512, 648, 792
    every = slice(None)

    def pb(k, p0=0):
        return A("pb", k, k + 1, 1, p0, 128)

    part("load")
    dma([(A("uin", 0, 512), hbm("u", every))], "Y")
    dma([(A("xin", 0, 1152), hbm("x", every))], "S")
    part("loadn")
    dma([(A("m0", 32 * c, 32 * c + 32, 1, 0, 9), hbm("nb", (c, every))) for c in range(4)]
        + [(A("m0", 128 + 32 * c, 160 + 32 * c, 1, 0, 9), hbm("e", (c, every))) for c in range(4)])
    part("loadw")
    dma([(cast(A("wq", 0, 512), 8), hbm("wc", every)), (A("wsc", 0, 512), hbm("ws", every))])
    part("loadv")
    dma([(A("vin", 0, 512), hbm("v", every))])
    part("pb")
    for k in range(3):
        iota(A("pi", k, k + 1), [[1, 1]], 0, 1 << k, False)
    ts(A("pi", 3, 6), A("pi", 0, 3), 15, None, AL.bitwise_and)
    copy(A("pb", 0, 6), A("pi", 0, 6))
    P, Q16, Q8X2, Q4X4, G16, G, B3X8, B2X8 = pb(0), pb(3), pb(4), pb(5), pb(6), pb(7), pb(23), pb(24)
    part("pb2")
    lin(G16, Q16, -1.0, P)
    lin(G, G16, 0.0625, 0.0)
    lin(B3X8, Q8X2, -0.5, Q16)
    lin(B2X8, Q4X4, -0.5, Q8X2)
    part("fill")
    fill(A("zb", 0, 576), 0.0)
    fill(A("ones", 0, 512), 1.0)
    fill(A("lu", 0, 10), 2)
    part("blank0")
    zero(A("ft", 1, 1152, 4, 0, 96))
    blank([("dig", 0, 512), ("dig", 512, 1024)])
    part("blank1")
    blank([("oh", 0, 512)])
    part("lu")
    lin(pb(22), Q8X2, 8.0, 1.0)
    ts(A("lu", 10, 18), A("ones", 0, 8), pb(22), None, AL.mult)
    ts(A("lu", 18, 27), A("ones", 0, 9), Q8X2, 8.0, AL.mult, AL.mult)
    part("qu")
    quant(UQ, 0, 128, A("uin", 0, 512))
    quant(XQ, PRE, C, A("xin", 0, 1152))
    pick(UP, U_ORD, UQ, 128, A("lu", 0, 8))
    part("qu2")
    pick(UP, U_FRM, UQ, 128, A("lu", 10, 18))
    again(UP, U_FRM + 128, UP, U_FRM, 128)
    part("qu3")
    pick(UP, U_MRK, UQ, 128, A("lu", 18, 27))
    again(UP, U_MRK + 144, UP, U_MRK + 1, 136)
    part("pre2")
    again(BQ, 0, XQ, PRE, PRE)
    part("tri")
    where(A("tri", 0, 128), A("zb", 0, 128), [[1, 128]], AL.is_ge, BIG, 0, -1)
    fill(A("th", 128, CUT, 1, 0, 96), BIG)
    quant(CQ, C_ONE, 128, A("ones", 0, 512))
    part("etile")
    where(A("ebig", 0, 512), A("ones", 0, 512), [[-1, 512]], AL.is_equal, 0.0, 3, 4)
    copy(A("ebig", 512, 4 * EW + 8), A("ebig", 0, 4 * EW + 8 - 512), "VS")
    for b in range(4):
        quant(EQ, EW * b, EW, A("ebig", 3 - b, 4 * EW + 3 - b))
    part("dig")
    iota(A("nrow", 0, H), [[1, H]], 1, 0)
    lin(pb(17), G16, 1.0, 128.0)
    lin(pb(18), G16, 2.0, 64.0)
    lin(pb(19), G16, -1.0, 96.0)
    lin(pb(20), pb(19), 1.0, Q16)
    for at, col, q0 in ((0, 6, 0), (1, 17, 0), (2, 18, 96), (512, 3, 0), (513, 3, 0), (514, 20, 96)):
        copy(A("dig", at, at - at % 4 + 512, 4, q0, 128), A("ones", 0, 128, 1, q0, 128), "VS", pb(col, q0))
    quant(CQ, C_HI, 256, A("dig", 0, 1024))
    part("rw")
    head = A("rw", 0, 144, 1, 0, 16)
    where(head, A("zb", 0, 144, 1, 0, 16), [[0, 9], [1, 16]], AL.not_equal, CAP, 0, -1)
    where(head, head, [[0, 9], [1, 16]], AL.not_equal, -HOLD, -1, -1)
    dma([(A("rw", 0, 144, 1, k, k + 16), head) for k in range(16, 128, 16)])
    part("qrow")
    ts(pb(13), Q16, 15.0, HOLD, AL.not_equal, AL.mult)
    part("rf")
    where(A("rf", 0, 192), A("zb", 0, 192), [[0, 24], [1, 8]], AL.not_equal, -BIG, 0, 0)
    nought(A("ff", 3, 256, 4))
    nought(A("fg", 3, 256, 4))
    part("sel0")
    blank([("sel", 0, 512), ("sel", 512, 1056)])
    blank([("sel", 1056, 1600), ("sel", 1600, 2176)])
    part("sel")
    iota(A("qrow", 0, 144), [[0, 9], [1, 16]], 0, 0)
    iota(A("grow", 0, 128), [[1, 8], [0, 16]], 0, 0)
    ts(A("sel", 0, 512, 4), A("grow", 0, 128), G, MT / 2.0, AL.is_equal, AL.mult)
    copy(A("sel", 1, 512, 4), A("sel", 0, 512, 4), "VS", -1.0)
    ts(A("sel", 512, 1056, 4), A("qrow", 8, 144), G, 0.5, AL.is_equal, AL.mult)
    copy(A("sel", 513, 1056, 4), A("sel", 512, 1056, 4), "VS", -1.0)
    copy(A("sel", 1057, 1600, 4), A("sel", 512, 1056, 4), "VS", float(TURN))
    where(A("sel", 1600, 2176, 4), A("ones", 0, 144), [[-1, 9], [-16, 16]], AL.is_equal, 0.0, -7, 1)
    quant(CQ, C_SUM, 264, A("sel", 0, 1056))
    quant(CQ, C_OWN, 280, A("sel", 1056, 2176))
    part("blank")
    nought(A("vv", 0, 160))
    for c0 in range(0, 800, 200):
        nought(A("fa", c0, c0 + 200))
    part("gaps")
    where(A("rc", 0, 144), A("zb", 0, 144), [[0, 36], [1, 4]], AL.not_equal, -BIG, 0, 0)
    for a in [A("mm", 0, 8), A("offa", 0, 1), A("oe1", 0, 128, 1, 0, 32)] + [A("mk", MT * r + E, MT * r + MT) for r in range(7)]:
        nought(a)
    part("lists")
    iota(A("lrow", 0, 4), [[8, 2], [1, 2]], 0, 0)
    iota(A("lrow", 4, 20), [[16, 2], [32, 4], [0, 2]], 0, 0)
    iota(A("lrow", 20, 26), [[2, 6]], 64, 0)
    iota(A("lrow", 26, 31), [[64, 5]], 0, 0)
    iota(A("lrow", 31, 36), [[64, 5]], 5 * 64 + 8 - C, 0)
    iota(A("idx", 0, 18), [[FAR, 3], [16, 6]], 0, 0)
    iota(pb(25), [[0, 1]], -2, 0)
    lin(A("idx", 0, 18), A("idx", 0, 18), 1.0, Q16)
    lin(pb(8), B2X8, 2.0, G)
    lin(pb(9), Q4X4, 8.0, pb(8))
    lin(pb(10), B3X8, 0.125, 0.0)
    lin(pb(11), Q4X4, 8.0, pb(10))
    lin(pb(12), B2X8, 16.0, pb(11))
    lin(pb(14), B3X8, -0.125, 1.0)
    lin(pb(15), B3X8, 4.0, pb(8))
    lin(pb(16), B3X8, (32.0 + 8 - C) / 8, pb(8))
    for c0, c1, col in ((0, 4, pb(9)), (4, 20, Q16), (20, 26, pb(12)), (26, 30, pb(15)), (30, 31, pb(16)), (31, 36, pb(15))):
        lin(A("lsum", c0, c1), A("lrow", c0, c1), 1.0, col)
    copy(A("lfix", 0, 36), A("lsum", 0, 36))
    part("edges")
    ts(A("m1", 0, 128, 1, 0, 9), A("m0", 128, 256, 1, 0, 9), float(MT), None, AL.mult)
    tt(A("vv", 0, 128, 1, 0, 9), A("m1", 0, 128, 1, 0, 9), A("m0", 0, 128, 1, 0, 9), AL.add)
    dma([(A("vv", 0, 128, 1, k, k + 9), A("vv", 0, 128, 1, 0, 9)) for k in (32, 64, 96)])
    copy(A("vg", 0, 320), ind(A("vv", 0, 160), A("l12", 0, 20)), "VS")
    turn(A("vt", 0, 320), A("vg", 0, 320))
    part("edgeb")
    copy(A("c18", 0, 9), A("vt", 0, 9), "VS")
    copy(A("c18", 9, 18), A("vt", 32, 41), "VS")
    copy(A("tc", 0, 9), A("c18", 0, 18, 2), "VS", pb(14))
    copy(A("td", 0, 9), A("c18", 1, 18, 2), "VS", pb(10))
    tt(A("vb", 0, 9), A("tc", 0, 9), A("td", 0, 9), AL.add)
    ts(A("nbi", 0, 9), A("vb", 0, 9), MT - 1, None, AL.bitwise_and)
    copy(A("lnb", 0, 9), A("nbi", 0, 9))
    part("edgea")
    copy(A("vi", 0, 80), ind(A("vt", 0, 320), A("l3", 0, 5)))
    ts(A("sa", 0, 72), A("vi", 0, 72), 9, None, AL.logical_shift_right)
    ts(A("aa", 0, 72), A("vi", 0, 72), MT - 1, None, AL.bitwise_and)
    copy(A("saf", 0, 72), A("aa", 0, 72))
    lin(A("zz", 0, 72), A("saf", 0, 72), 1.0 / H, 0.5 / H - 0.5)
    lin(A("dl", 0, 72), A("zz", 0, 72), 1.0, ROUND)
    lin(A("zz", 0, 72), A("dl", 0, 72), 1.0, -ROUND)
    act(A("dl", 0, 72), A("zz", 0, 72), AF.Relu, pb(25))
    copy(A("offs", 0, 72), A("zz", 0, 72), "VS", float(C))
    lin(A("mul", 0, 72), A("dl", 0, 72), float(FAR - TURN), float(TURN))
    copy(A("zz", 0, 72), A("dl", 0, 72), "VS", float(OWN - 4 * C))
    tt(A("nbm", 0, 72), A("offs", 0, 72), A("saf", 0, 72), AL.add)
    tt(A("nbm", 0, 72), A("nbm", 0, 72), A("zz", 0, 72), AL.add)
    part("qv")
    quant(VQ, 0, 128, A("vin", 0, 512))

    turns, banks = [0], [(5, 6, 7)]

    def stream():
        turns[0] += 1
        return banks[0][turns[0] % len(banks[0])]

    def unpack(mv, end, r, at):
        if mv == XQ and end - 128 - H < PRE:
            for b in range(4):
                k = stream()
                mm(k, EQ, EW * b + 16 * r, mv, end - H, 128)
                copy(A("vw", at + H * b, at + H * b + H), bank(k, 0, H), "VS", 0.5)
            return
        for m in range(2):
            k = stream()
            mm(k, EQ, EW * (2 * m + 1) + 16 * r, mv, end - 128 - H, 128 + H)
            mm(k, EQ, EW * 2 * m + 16 * r, mv, end - 128, 128)
            copy(A("vw", at + 2 * H * m, at + 2 * H * m + 2 * H), bank(k, 128 - H, 128 + H), "VS", 0.5)

    def spread(at, width, made, turns_to, behind):
        for to in turns_to:
            cut, w = 16 * to, width * made
            dma([(A("vw", at + width * to, at + width * to + w, 1, 0, 128 - cut), A("vw", at, at + w, 1, cut, 128)),
                 (A("vw", at + width * to, at + width * to + w, 1, 128 - cut, 128), A("vw", at, at + w, 1, 0, cut))],
                "Y", behind)

    def frames(to, k, src, x0, ff, gq, at):
        for w, c0 in ((2, 160), (1, 128), (0, 0)):
            mm(k, src, x0 + c0, UP, U_FRM, 128 + 64 * w)
        scan(A("pm", at, at + 192), A("rf", 0, 192), bank(k, 64, 256), AL.add, AL.max)
        for w in range(3):
            a = at + 64 * w
            ts(A(ff, w, 256, 4), A("pm", a, a + 64), A("pm", a + 7, a + 8), None, AL.is_lt)
        copy(A(ff, 256, 512), A(ff, 0, 256), "VS")
        quant(gq, 0, 128, A(ff, 0, 512))
        for w, n in ((1, 256), (0, 128)):
            mm(k, gq, 0, EQ, EW * w + 128 - n, n)
        copy(A(to, 0, 256), bank(k, 0, 256), "VS")
        k = stream()
        mm(k, gq, 0, EQ, EW * 2, 128)
        copy(A(to, 256, C), bank(k, 96, 128), "VS")

    def halves(k, tile, mv):
        mm(k, CQ, tile + 8, mv, 0, 128, True, False)
        mm(k, CQ, tile, mv, 72, 128, False, True)

    def mark_at(r):
        return U_MRK + r if r % 2 == 0 else U_MRK + 144 + r - 1

    blocks, runs = (0, 128, 160), ((0, CUT), (CUT, C))
    for t in range(3):
        x0, b1, FX = PRE + C * t, PRE + H * (t + 1), ("fxq%d" % t, "fxs%d" % t)
        label[1] = t
        part("sendx")
        send(t, 0, 400.0, [A("xq", x0, x0 + CUT)], 500.0)
        send(t, 1, 800.0, [A("xq", x0 + CUT, x0 + C), A("xs", x0, x0 + C)], 700.0)
        part("sort")
        def flags(on, k, w, c0, c1, strict):
            q0 = 96 if w == 1 else 0
            out, row, pc = A("ft", 4 * c0 + w, 4 * c1, 4, q0), bank(k, c0, c1, 1, q0), A("pc", w, w + 1, 1, q0)
            if on == "V":
                ts(out, row, pc, None, AL.is_lt if strict else AL.is_le)
            else:
                sign = A("sg", C * w + c0, C * w + c1, 1, q0)
                act(sign, row, AF.Sign, pc, -1.0)
                act(out, sign, AF.Relu if strict else AF.Sign, None if strict else A("ones", 0, 1, 1, q0))

        part("head")
        for w in range(2):
            mm(1 + w, XQ, x0 + 32 * w, UP, U_ORD, 128)
            copy(A("pc", w, w + 1), bank(1 + w, 0, 1), "S")
        jobs = HEAD[t]
        early = {"S": 4, "V": stream()}
        for on in sorted(set(jobs[:3] + ("V" if t else ""))):
            if t or on == "S":
                mm(early[on], UP, U_ORD, XQ, x0, CUT)
        act(A("th", 0, 128), A("tri", 0, 128), AF.Identity, A("pc", 0, 1))
        act(A("th", 128, CUT, 1, 96, 128), A("tri", 96, 128, 1, 96, 128), AF.Identity, A("pc", 1, 2, 1, 96, 128))
        first = ((0, 0, 128, True), (0, 128, CUT, False), (1, 0, CUT, True))
        for on, job in zip(jobs, first):
            if t or on == "S":
                flags(on, early[on], *job)
        if t:
            tt(A("ft", 3, 4 * CUT, 4), bank(early["V"], 0, CUT), A("th", 0, CUT), AL.is_equal)
        part("sort")
        late = {"V": 0, "S": stream()}
        mm(3, XQ, x0 + CUT, UP, U_ORD, 128)
        copy(A("pc", 2, 3), bank(3, 0, 1), "S")
        for on in sorted(set(jobs[3:] + "V"), reverse=True):
            mm(late[on], UP, U_ORD, XQ, x0, C)
        act(A("th", CUT, C), A("tri", 0, 128), AF.Identity, A("pc", 2, 3))
        for on, job in zip(jobs, first):
            if on == "V" and not t:
                flags(on, 0, *job)
        for on, job in zip(jobs[3:], ((0, CUT, C, False), (1, CUT, C, False), (2, 0, C, True))):
            flags(on, late[on], *job)
        c0 = CUT if t else 0
        tt(A("ft", 4 * c0 + 3, 4 * C, 4), bank(0, c0, C), A("th", c0, C), AL.is_equal)
        part("vown")
        for c in range(3):
            unpack(XQ, x0 + H * (c + 1), 0, FAR * c)
        part("early")
        spread(0, TURN, 1, range(1, 1 + EARLY), None)
        part("sort")
        quant(FQ, 0, C, A("ft", 0, 1152))
        for w, c0 in enumerate(blocks):
            mm(1 + w, FQ, c0, CQ, C_ONE, 128)
            ts(A("oh", w, 4 * H, 4), A("nrow", 0, H), bank(1 + w, 0, 1), None, AL.is_equal)
        quant(NQ, 0, 128, A("oh", 0, 512))
        mm(0, CQ, C_HI, NQ, 0, 128, True, False)
        mm(0, CQ, C_LO, NQ, 0, 128, False, True)
        scan(A("w2", 0, H), A("rw", 0, H), bank(0, 0, H), AL.add, AL.min)
        ts(A("sl%d" % t, 0, 6), A("w2", 15, H, 16), pb(13), None, AL.add)
        send(t, 2, 400.0, [A("sl%d" % t, 0, 6)], 300.0)
        issued = A("wire", 16 + t, 17 + t)
        land(t, 2, 100.0, [issued])
        part("down")
        spread(0, TURN, 1, range(1 + EARLY, 8), issued)
        part("mown")
        for r in range(8 - MCOPY):
            k = stream()
            mm(k, UP, mark_at(r), XQ, x0, C)
            copy(A("mk", MT * r, MT * r + C), bank(k, 0, C), "VS")
        part("dmark")
        for r in range(8 - MCOPY, 8):
            dma([(A("mk", MT * r, MT * r + C, 1, 0, 128 - r), A("mk", 0, C, 1, r, 128)),
                 (A("mk", MT * r, MT * r + C, 1, 128 - r, 128), A("mk", 0, C, 1, 0, r))], "Y", issued)
        part("fown")
        frames("fl", 4, XQ, x0, "ff", GQ, 0)
        part("kown")
        copy(A("fa", 1, 577, 4), ind(A("fl", 0, C), A("lown", 0, 9)), "VS")
        quant(KQ, 0, 200, A("fa", 0, 800))
        halves(1, C_OWN, KQ)
        tt(A("oaf", 0, 18), bank(1, 0, 72, 4), A("idx", 0, 18), AL.add)
        copy(A("oa", 0, 18), A("oaf", 0, 18))
        for h, (c0, c1) in enumerate(runs):
            part("ah%d" % h)
            for b in range(4):
                copy(A("ah", C * b + c0, C * b + c1), ind(A("vw", H * b, OWN - H * (3 - b)), A("oa", c0 // 16, c1 // 16)), "VS")
        part("af")
        for b in (0, 2):
            copy(A("af", C * b, C * b + 2 * C), A("ah", C * b, C * b + 2 * C), "VS", 2.0)
        part("ffar")
        land(t, 0, WIRE_X[t], [A(FX[0], 0, C), A(FX[1], 0, C)])
        frames("flx", 3, FX, 0, "fg", JQ, 192)
        part("list")
        land(t, 1, WIRE_L[t], [A("ll%d" % t, 0, 6)])
        copy(A("fl", C, E), ind(A("flx", 0, C), A("ll%d" % t, 0, 6)), "S")
        part("pick")
        pick(BQ, b1 - H, FX, C, A("ll%d" % t, 0, 6), "S")
        turns[0], banks[0] = -1, (0, 5, 6, 7, 4, 3)
        part("vfar")
        for r in range(MADEB):
            unpack(BQ, b1, r, OWN + FAR * r)
        part("dfar")
        spread(OWN, FAR, MADEB, range(MADEB, 8, MADEB), None)
        part("mfar")
        for r in range(8):
            k = stream()
            mm(k, UP, mark_at(r), BQ, b1 - 128, 128)
            copy(A("mk", MT * r + C, MT * r + E), bank(k, 128 - H, 128), "VS")
        banks[0] = (5, 6, 7)
        part("knbg")
        copy(A("fa", 0, 576, 4), ind(A("fl", 0, E), A("lnb", 0, 9)), "V")
        part("knb")
        quant(HQ, 0, 200, A("fa", 0, 800))
        mm(1, CQ, C_SUM, HQ, 0, 144)
        scan(A("kb", 0, 144), A("rw", 0, 144), bank(1, 0, 144), AL.add, AL.min)
        tt(A("ab", 0, 9), A("kb", 15, 144, 16), A("vb", 0, 9), AL.add)
        ts(A("vb", 0, 9), A("ab", 0, 9), 8 * MT - 1, None, AL.bitwise_and)
        copy(A("ob", 0, 9), A("vb", 0, 9))
        part("offs")
        halves(2, C_CNT, HQ)
        tt(A("aa", 0, 72), bank(2, 0, 72), A("sa", 0, 72), AL.add)
        ts(A("sa", 0, 72), A("aa", 0, 72), 7, None, AL.bitwise_and)
        tt(A("offs", 0, 72), A("sa", 0, 72), A("mul", 0, 72), AL.mult)
        tt(A("offa", 1, 73), A("offs", 0, 72), A("nbm", 0, 72), AL.add)
        tt(A("dl", 0, 72), A("offa", 0, 72), A("offa", 1, 73), AL.subtract)
        part("choose")
        copy(A("mm", 8, 152), ind(A("mk", 0, 7 * MT + E), A("ob", 0, 9)), "VS")
        scan(A("px", 0, 144), A("mm", 7, 151), A("rc", 0, 144), AL.max, AL.add)
        tt(A("fa", 0, 576, 4), A("mm", 8, 152), A("px", 0, 144), AL.is_le)
        quant(KQ, 0, 200, A("fa", 0, 800))
        halves(1, C_CHO, KQ)
        scan(A("zz", 0, 72), A("dl", 0, 72), bank(1, 0, 72), AL.add, AL.mult)
        tt(A("ocf", 0, 18), A("zz", 3, 72, 4), A("offa", 4, 73, 4), AL.add)
        copy(A("oz", 0, 18), A("ocf", 0, 18))
        for h, (c0, c1) in enumerate(runs):
            part("z%d" % h)
            for b in range(4):
                tt(A("zt", 4 * c0 + b, 4 * c1, 4), ind(A("vw", H * b, OWN + 8 * FAR - H * (3 - b)), A("oz", c0 // 16, c1 // 16)),
                   A("ah", C * b + c0, C * b + c1), AL.add)
            quant(ZQ, c0, c1 - c0, A("zt", 4 * c0, 4 * c1))
            part("r%d" % h)
            for b in range(4):
                mm(4 * h + b, WQ, 128 * b, ZQ, c0, c1 - c0)
                act(A("rr", C * b + c0, C * b + c1), bank(4 * h + b, 0, c1 - c0), AF.Relu, None, 0.03125)
        for h, (c0, c1) in enumerate(runs):
            part("x%d" % h)
            for b in range(4):
                tt(A("xt", 4 * c0 + b, 4 * c1, 4), A("rr", C * b + c0, C * b + c1), A("af", C * b + c0, C * b + c1), AL.add)
            quant(XQ, x0 + C + c0, c1 - c0, A("xt", 4 * c0, 4 * c1))
    part("oe")
    x0 = PRE + 3 * C
    copy(A("saf", 0, 72, 1, 0, 32), A("sa", 0, 72, 1, 0, 32))
    for c in range(4):
        copy(A("oe1", 32 * c, 32 * c + 18, 1, 0, 32), A("saf", c, 72, 4, 0, 32), "VS")
    turn(A("oe2", 0, 128, 1, 0, 32), A("oe1", 0, 128, 1, 0, 32))
    dma([(hbm("oe", (c, every)), A("oe2", 32 * c, 32 * c + 16, 1, 0, 18)) for c in range(4)])
    for h, (c0, c1) in enumerate(runs):
        part("out%d" % h)
        mm(h, VQ, 0, XQ, x0 + c0, c1 - c0)
        copy(A("yo", c0, c1), bank(h, 0, c1 - c0), "VS")
        dma([(hbm("y", (every, slice(c0, c1))), A("yo", c0, c1))], "S" if h else "Y")
        dma([(hbm("oc", (every, slice(4 * c0, 4 * c1))), cast(A("xq", x0 + c0, x0 + c1), 8))], "Y")
    dma([(hbm("osc", (slice(4 * k, 4 * k + 4), every)), A("xs", x0, x0 + C, 1, 32 * k, 32 * k + 4)) for k in range(4)], "Y")
    return ops


def _depends(ops):
    seen = {}
    for i, op in enumerate(ops):
        deps = {}
        for a, w in [(a, False) for a in op["rd"]] + [(a, True) for a in op["wr"]]:
            if a[1] == "ps":
                key, m, lo, hi = ("ps", a[4] // 512), 1, 0, 128
            else:
                key, m, lo, hi = a[1], _mask(a), a[2], a[3]
            old = seen.setdefault(key, [])
            for j, m2, lo2, hi2, w2 in old:
                if j != i and m & m2 and lo < hi2 and lo2 < hi:
                    if w or w2:
                        deps[j] = deps.get(j, False) or not (a[1] == "ps" and w and w2)
                    elif a[1] == "ps":
                        deps.setdefault(j, False)
            if w:
                old[:] = [o for o in old if o[0] == i or not (o[1] & ~m == 0 and lo <= o[2] and o[3] <= hi)]
            old.append((i, m, lo, hi, w))
        op["deps"] = deps


def _gap(row, t, hold):
    lo, hi = 0, len(row)
    while lo < hi:
        mid = (lo + hi) // 2
        if row[mid][1] <= t:
            lo = mid + 1
        else:
            hi = mid
    while lo < len(row) and row[lo][0] < t + hold:
        t = max(t, row[lo][1])
        lo += 1
    return t, lo


def _place(ops, before, turn, spare):
    n = len(ops)
    busy = {e: [] for e in "VSPGYND"}
    done, eng, start = [0.0] * n, [None] * n, [0.0] * n
    for i in turn:
        op, best = ops[i], None
        for e, (cost, f) in op["how"].items():
            t = 0.0
            for j, hard in before[i]:
                d = done[j] + (hard or (HOP if eng[j] != e else 0.0))
                if d > t:
                    t = d
            hold = 80.0 * op["calls"] if op["tag"] == "dma" else 1.0 if e == "N" else cost
            t, lo = _gap(busy[e], t, hold)
            t2 = t
            if op["load"]:
                while True:
                    t2, ld = _gap(busy["D"], t, op["load"])
                    if t2 == t or e != "Y":
                        break
                    t, lo = _gap(busy[e], t2, hold)
                cost += t2 - t + (op["load"] if op["tag"] == "dma" else 0.0)
            worth = t + cost + (spare.get(op["kind"], 400.0) if e == "V" else 0.0)
            if best is None or worth < best[0]:
                best = (worth, t, e, lo, hold, cost, t2)
        done[i], eng[i], start[i] = best[1] + best[5], best[2], best[1]
        busy[best[2]].insert(best[3], (best[1], best[1] + best[4], i))
        if op["load"]:
            busy["D"].insert(_gap(busy["D"], best[6], op["load"])[1], (best[6], best[6] + op["load"], i))
    return max(done), start, eng, {e: [x[2] for x in busy[e]] for e in busy}, done


def _run(times, before, turn, eng, old=None, first=0, behind=None, tail=None, limit=0.0):
    n = len(turn)
    if old is None:
        done, held, marks = [0.0] * n, [None] * n, []
        free, last = {e: 0.0 for e in "VSPGYN"}, {e: None for e in "VSPGYN"}
    else:
        done, held, marks = old[1][:], old[2][:], old[3][:first // 32]
        free, last = dict(old[3][first // 32][0]), dict(old[3][first // 32][1])
    for at in range(first // 32 * 32, n, 32):
        marks.append((dict(free), dict(last)))
        for i in turn[at:at + 32]:
            e = eng[i]
            cost, hold, load = times[i][e]
            t, by, queue = free[e], last[e], True
            if load and free["Y"] > t:
                t, by = free["Y"], last["Y"]
            for j, hard in before[i]:
                d = done[j] + (hard or (HOP if eng[j] != e else 0.0))
                if d > t:
                    t, by, queue = d, j, False
            if tail is not None and t + tail[i] > limit and i in behind:
                return None
            done[i], held[i] = t + cost, (by, queue)
            free[e], last[e] = t + hold, i
            if load:
                free["Y"], last["Y"] = t + load, i
    return max(done), done, held, marks


def _improve(ops, before, turn, eng, draw):
    for op in ops:
        op["time"] = {}
        for e, (cost, f) in op["how"].items():
            if op["tag"] == "dma":
                load = max(op["load"], 80.0 * op["calls"])
                op["time"][e] = (cost + op["load"], load if e == "Y" else 80.0 * op["calls"], load)
            else:
                op["time"][e] = (cost, 0.0 if e == "N" else cost, op["load"])
    times = [op["time"] for op in ops]
    now = _run(times, before, turn, eng)
    best, moves = (now, turn, eng), None
    for step in range(MOVES):
        if moves is None:
            tail, nxt = [0.0] * len(turn), {e: 0.0 for e in "VSPGYN"}
            for i in reversed(turn):
                e = eng[i]
                cost, hold, load = times[i][e]
                q = hold + nxt[e]
                if load and load + nxt["Y"] > q:
                    q = load + nxt["Y"]
                if tail[i] + cost > q:
                    q = tail[i] + cost
                tail[i] = nxt[e] = q
                if load:
                    nxt["Y"] = q
                for j, hard in before[i]:
                    d = q + (hard or (HOP if eng[j] != e else 0.0))
                    if d > tail[j]:
                        tail[j] = d
            moves, near = [], []
            for i in turn:
                if now[1][i] - times[i][eng[i]][0] + tail[i] > now[0] - SLACK:
                    near.append(i)
                    j, queue = now[2][i]
                    if queue and j is not None:
                        moves.append((j, i))
                    if len(times[i]) > 1:
                        moves.append((None, i))
            mean = sum(now[1][i] for i in near) / len(near)
        j, i = draw(moves)
        turn2, eng2 = turn, eng
        if j is None:
            eng2, a = list(eng), turn.index(i)
            eng2[i], b = "V" if eng[i] == "S" else "S", a
        elif draw((0, 0, 1)):
            a = turn.index(j)
            b = min(len(turn), turn.index(i) + draw((1, 4, 10, 30)))
            back, rest, late = [j], [], {j}
            for k in turn[a + 1:b]:
                if any(m in late for m, hard in before[k]):
                    back.append(k)
                    late.add(k)
                else:
                    rest.append(k)
            if i in late:
                continue
            turn2 = turn[:a] + rest + back + turn[b:]
        else:
            a, b = turn.index(j), turn.index(i)
            if draw((0, 0, 1)):
                a = max(0, a - draw((3, 10, 30)))
            need, front, rest = set(k for k, hard in before[i]), [i], []
            for k in reversed(turn[a:b]):
                if k in need:
                    front.append(k)
                    need.update(m for m, hard in before[k])
                else:
                    rest.append(k)
            if j in need:
                continue
            turn2 = turn[:a] + front[::-1] + rest[::-1] + turn[b + 1:]
        limit = now[0] + draw(range(HEAT)) * (1.0 - step / MOVES) + 0.001
        got = _run(times, before, turn2, eng2, now, a, set(turn2[b + 1:b + 80]), tail, limit)
        if got is not None and got[0] + PULL * (sum(got[1][i] for i in near) / len(near) - mean) <= limit:
            now, turn, eng, moves = got, turn2, eng2, None
            if now[0] < best[0][0]:
                best = (now, turn, eng)
    now, turn, eng = best
    return now[0], [d - times[i][eng[i]][0] for i, d in enumerate(now[1])], eng, {e: [i for i in turn if eng[i] == e] for e in "VSPGYN"}


def _before(ops):
    before = [[(j, HOP if hard else 0.0) for j, hard in op["deps"].items()] for op in ops]
    for i, op in enumerate(ops):
        if op["tag"] == "dma" and op["kind"] == "early" and op["round"] > 0:
            k = min(j for j in range(i, len(ops)) if ops[j]["tag"] == ("send", op["round"], 2))
            before[k].append((i, -DMA_T))
    return before


def _schedule():
    ops = _program()
    _depends(ops)
    n = len(ops)
    before = _before(ops)
    after = [[] for _ in range(n)]
    for i in range(n):
        for j, hard in before[i]:
            after[j].append(i)
    left = [0.0] * n
    for i in range(n - 1, -1, -1):
        left[i] = min(c for c, f in ops[i]["how"].values()) + ops[i]["load"] + HOP + max([left[k] for k in after[i]] + [0.0])
    kinds = sorted(set(op["kind"] for op in ops))
    free = sorted(set(op["kind"] for op in ops if len(op["how"]) > 1))
    ahead, spare = dict(AHEAD), dict(SPARE)
    seed, now, best = [12345], None, None

    def draw(row):
        seed[0] = (seed[0] * 1103515245 + 12345) % 2147483648
        return row[(seed[0] >> 8) % len(row)]

    for trial in range(TRIES):
        a2, s2 = dict(ahead), dict(spare)
        for k in range(draw((1, 1, 2, 3)) if trial else 0):
            if draw(range(4)) == 0:
                s2[draw(free)] = draw((0, 100, 200, 400, 800, 1500, 3000, 9000))
            else:
                name = draw(kinds)
                a2[name] = draw((0, a2.get(name, 0) + draw((-1, 1)) * draw((200, 500, 1000, 2000, 4000))))
        key = [0.0] * n
        for i in range(n - 1, -1, -1):
            key[i] = max([left[i] + a2.get(ops[i]["kind"], 0)] + [key[k] + 1.0 for k in after[i]])
        got = _place(ops, before, sorted(range(n), key=lambda k: -key[k]), s2)
        if now is None or got[0] <= now + draw(range(150)) * (1.0 - trial / TRIES):
            now, ahead, spare = got[0], a2, s2
            if best is None or now < best[0]:
                best = got + (a2, s2)
    span, start, eng, order = _improve(ops, before, sorted(range(n), key=lambda k: best[1][k]), best[2], draw)
    for i, op in enumerate(ops):
        op["eng"], op["at"] = eng[i], start[i]
    for i in order["Y"]:
        ended = [j for j in order["V"] if start[j] + ops[j]["how"]["V"][0] + HOP <= start[i]]
        if ended and ops[i]["kind"] != "load":
            ops[i]["deps"][ended[-1]] = True
    for op in ops:
        op["all"] = set(j for j, hard in op["deps"].items() if hard or ops[j]["eng"] != op["eng"])
    wanted = set(j for op in ops for j in op["all"])
    known, raised, covers = {e: 0 for e in order}, {e: 0 for e in order}, [0] * n
    for i in sorted(range(n), key=lambda k: start[k]):
        op, e = ops[i], eng[i]
        op["waits"] = []
        for j in sorted(op["all"], key=lambda k: -start[k]):
            if not known[e] >> j & 1:
                op["waits"].append(j)
                known[e] |= covers[j]
        if e == "N":
            covers[i] = 1 << i
        elif op["tag"] is None and i in wanted and e != "G":
            raised[e] |= 1 << i
            covers[i] = known[e] | raised[e]
        else:
            covers[i] = known[e] | 1 << i
    names = []
    for e in "VSPGY":
        k = 0
        for i in order[e]:
            op = ops[i]
            if op["tag"] == "dma":
                op["sig"] = ("d%d" % i, 16 * op["calls"])
                names.append("d%d" % i)
            elif op["tag"] is None and i in wanted and e == "G":
                op["sig"] = ("g%d" % i, 1)
                names.append("g%d" % i)
            elif op["tag"] is None and i in wanted:
                k += 1
                op["sig"] = ("on" + e, k)
            else:
                op["sig"] = None
    return ops, order, names, span, best[5:]


AHEAD = {"etile": 9400, "qu": 11500, "pick": 10300, "vown": 100, "qu2": 7800, "down": 300, "oe": -4000, "blank0": 2000, "ffar": -500,
         "pb2": 1300, "vfar": -1800, "z1": -1900, "loadv": -4000, "qu3": 8300, "fill": 4900, "choose": 1000, "dfar": -2000,
         "dig": 3300, "sel0": -2200, "loadn": 300, "z0": 4900, "pb": 100, "x0": 2200, "out0": -700, "early": 100, "sel": 500,
         "sendx": 1300, "qrow": 200, "sort": 300, "r1": 3300, "lu": -300, "af": -3900}
SPARE = {"vown": 100, "mown": 800, "ah0": 800, "ah1": 200, "vfar": 200, "mfar": 200, "af": 0, "choose": 200, "kown": 0, "sel": 0,
         "qu": 1500, "qu2": 800, "dig": 9000, "qu3": 9000, "lists": 800, "edges": 400, "blank0": 100, "out0": 400, "lu": 400,
         "ffar": 800, "pb2": 200, "etile": 1500, "edgea": 100, "out1": 100, "oe": 400, "edgeb": 1500, "fown": 800}
OPS, ORDER, _DMA_SEMS, SPAN, FOUND = _schedule()
SEMAPHORES = ["onV", "onS", "onP", "left", "issued"] + [k % t for t in range(3) for k in ("arrx%d", "arrl%d", "rela%d", "relb%d")] + _DMA_SEMS


def _bits(engines):
    m = 0
    for k in engines:
        m |= 1 << k
    return m


def _helpers(T, topo, src, dst):
    able = [c for c in topo.cores_of(src) if T.rank_of(c) is None and topo.may_write(c, dst)]
    return [c for c in able if topo.die(c) == topo.die(src)], [c for c in able if topo.die(c) != topo.die(src)]


def _pieces(T, topo, rank, t):
    n = len(T.cores)
    src, dst = T.cores[rank], T.cores[(rank - STEP[t]) % n]
    if topo.may_write(src, dst):
        return [(0, "q", 0, CUT, None), (1, "q", CUT, C, None), (1, "s", 0, C, None), (2, "l", 0, 6, None)]
    near, far = _helpers(T, topo, src, dst)
    others = [r for r in range(n) if r != rank and T.cores[r] in topo.cores_of(src)]
    if all(topo.may_write(T.cores[r], T.cores[(r - STEP[t]) % n]) for r in others):
        plane = [(1, "s", 0, C // 2, far[0]), (1, "s", C // 2, C, far[1])]
    else:
        plane = [(1, "s", 0, C, near[0])]
    return [(0, "q", 0, CUT, near[0]), (1, "q", CUT, C, near[1])] + plane + [(2, "l", 0, 6, near[1])]


def _view(T, names, what, c0, c1):
    a = T[names["qsl".index(what)]][:, c0:c1]
    return a.bitcast(dt.uint8) if what == "q" else a


def _landing(T, t, what, c0, c1):
    return _view(T, ("fxq%d" % t, "fxs%d" % t, "ll%d" % t), what, c0, c1), T.sem[("arrl%d" if what == "l" else "arrx%d") % t]


def _halt(T, t, what, c0, c1):
    return _view(T, ("rq%d" % t, "rs%d" % t, "rl%d" % t), what, 0, c1 - c0), T.sem[("rela%d" if what == "q" else "relb%d") % t]


def _arrivals(T, topo, giver, t, kind):
    src, dst = T.cores[giver], T.cores[(giver - STEP[t]) % len(T.cores)]
    return sum(len(topo.engines(src if via is None else via, dst)) for call, what, c0, c1, via in _pieces(T, topo, giver, t)
               if (what == "l") == bool(kind))


def _hand_on(g, core, T, topo):
    n, sent = len(T.cores), 0
    for t, d in enumerate(STEP):
        for r in range(n):
            src, dst = T.cores[r], T.cores[(r - d) % n]
            for call, what, c0, c1, via in _pieces(T, topo, r, t):
                if via != core:
                    continue
                rid, pid = topo.addr(dst, core)
                here, sem = _halt(T, t, what, c0, c1)
                out, landed = _landing(T, t, what, c0, c1)
                g.wait_ge(sem, len(topo.engines(src, core)) // (2 if what == "s" and c1 - c0 < C else 1))
                g.remote_dma(out, here, landed, T.sem.left, pid, rid, topo.mask(core, dst))
                sent += len(topo.engines(core, dst))
    if sent:
        g.wait_ge(T.sem.left, sent)


def _send(g, core, T, topo, rank, t, kind):
    dst, x0, sent, parts = T.cores[(rank - STEP[t]) % len(T.cores)], PRE + C * t, 0, []
    for call, what, c0, c1, via in _pieces(T, topo, rank, t):
        if call != kind:
            continue
        to = dst if via is None else via
        rid, pid = topo.addr(to, core)
        eng = topo.engines(core, to)
        out, sem = _landing(T, t, what, c0, c1) if via is None else _halt(T, t, what, c0, c1)
        src = T["sl%d" % t][:, c0:c1] if what == "l" else _view(T, ("xq", "xs"), what, x0 + c0, x0 + c1)
        if what == "s" and c1 - c0 < C:
            half = len(eng) // 2
            parts.append(RemoteDMATransfer(dst_ids=[DstId(rid=rid, pnc=pid)], dma_engine_mask=_bits(eng[len(parts) * half:][:half]),
                                           remote_sem=sem, src=src, dst=out))
            sent += half
        else:
            g.remote_dma(out, src, sem, T.sem.left, pid, rid, _bits(eng))
            sent += len(eng)
    if parts:
        g.remote_dma_fused(parts, local_sem=T.sem.left)
    if kind == 2:
        g.sem_inc(T.sem.issued, 1)
    return sent


def rank_program(g, core, T, topo):
    rank = T.rank_of(core)
    if rank is None:
        _hand_on(g, core, T, topo)
        return
    n = len(T.cores)
    queues = {"V": g.vector, "S": g.scalar, "P": g.tensor, "G": g, "Y": g.sync}
    R = lambda a: _real(T, a)
    top, waited, sent = {"issued": len(STEP)}, {}, 0
    for e in "YSVPG":
        q, have = queues[e], {}
        for i in ORDER[e]:
            op, wants = OPS[i], {}
            for j in op["waits"]:
                tag = OPS[j]["tag"]
                if OPS[j]["eng"] != "N":
                    name, k = OPS[j]["sig"]
                elif tag[2] == 2:
                    name, k = "issued", tag[1] + 1
                else:
                    name = ("arrl%d" if tag[2] else "arrx%d") % tag[1]
                    k = _arrivals(T, topo, (rank + STEP[tag[1]]) % n, tag[1], tag[2])
                wants[name] = max(wants.get(name, 0), k)
            for name, k in wants.items():
                if have.get(name, 0) < k:
                    q.wait_ge(T.sem[name], k)
                    have[name] = k
                    waited[name] = max(waited.get(name, 0), k)
            if op["how"][e][1] is None:
                sent += _send(g, core, T, topo, rank, op["tag"][1], op["tag"][2])
                continue
            call = op["how"][e][1](q, R)
            if op["sig"] is not None:
                name, k = op["sig"]
                for one in (call if op["tag"] == "dma" else [call]):
                    one.then_inc(T.sem[name], 16 if op["tag"] == "dma" else 1)
                top[name] = k
    g.wait_ge(T.sem.left, sent)
    for name, k in top.items():
        if waited.get(name, 0) < k:
            g.wait_ge(T.sem[name], k)
